import numpy as np
import ml_dtypes


def mxq(x, axis, fmt="e4m3"):
    dtype, down = {"e4m3": (ml_dtypes.float8_e4m3fn, 7), "e5m2": (ml_dtypes.float8_e5m2, 14)}[fmt]
    v = np.moveaxis(np.asarray(x, np.float32).astype(ml_dtypes.bfloat16).astype(np.float64), axis, -1)
    blocks = v.reshape(v.shape[:-1] + (-1, 32))
    amax = np.abs(blocks).max(-1, keepdims=True)
    byte = np.maximum(np.where(amax > 0, np.frexp(amax)[1] - 1 + 127, 0) - down, 1)
    scale = np.exp2(byte - 127.0)
    codes = (blocks / scale).astype(np.float32).astype(dtype).astype(np.float64)
    return np.moveaxis((codes * scale).reshape(v.shape), -1, axis)


WIDE = False


def mx_kscale(k):
    if not WIDE:
        return np.ones(k)
    levels = np.array([10, -10, 5, -5, 0])
    if k % 512:
        return np.exp2(np.random.permutation(np.resize(levels, k // 32))).repeat(32)
    a = np.empty((k // 512, 16))
    for p in range(k // 512):
        a[p, :8] = np.random.permutation(np.resize(levels, 8))
        for g in range(8):
            far = levels[np.abs(levels - a[p, g]) >= 10]
            a[p, g + 8] = far[np.random.randint(len(far))]
    return np.exp2(a.ravel()).repeat(32)


def f64(x):
    return np.asarray(x).astype(np.float64)


def striped(idx):
    return np.tile(idx.reshape(-1, 16).T, (8, 1)).astype(np.uint16)


def unstriped(offs):
    return offs[:16].T.reshape(-1).astype(np.int64)


E2M1 = np.array([0.0, 0.5, 1.0, 1.5, 2.0, 3.0, 4.0, 6.0, -0.0, -0.5, -1.0, -1.5, -2.0, -3.0, -4.0, -6.0])


def pack_weight(w, fmt):
    k, n = w.shape
    w = f64(np.asarray(w, np.float32).astype(ml_dtypes.bfloat16)).reshape(k // 32, 32, n)
    amax = np.abs(w).max(1)
    if fmt == "e4m3":
        byte = np.frexp(amax)[1] - 1 + 127 - 7
    else:
        mant, ex = np.frexp(amax / 6.0)
        byte = np.where(mant > 0.5, ex, ex - 1) + 127
    byte = np.clip(np.where(amax > 0, byte, 1), 1, 254)
    scaled = (w * np.exp2(127.0 - byte)[:, None, :]).reshape(k, n).astype(np.float32)
    by_word = np.ascontiguousarray(scaled.reshape(k // 512, 128, 4, n).transpose(0, 1, 3, 2))
    if fmt == "e4m3":
        words = by_word.astype(ml_dtypes.float8_e4m3fn).view(np.uint8)
    else:
        c = by_word.astype(ml_dtypes.float4_e2m1fn).view(np.uint8) & 0xF
        words = (c[..., 0::2] | (c[..., 1::2] << 4)).reshape(k // 512, 128, 2 * n)
    return np.ascontiguousarray(words), np.ascontiguousarray(byte.astype(np.uint8).reshape(k // 512, 16, n))


def unpack_weight(words, scales, fmt):
    g, _, n = scales.shape
    words = np.ascontiguousarray(words).reshape(g, 128, n, -1)
    if fmt == "e4m3":
        vals = words.view(ml_dtypes.float8_e4m3fn).astype(np.float64)
    else:
        nib = np.empty((g, 128, n, 4), np.uint8)
        nib[..., 0::2] = words & 0xF
        nib[..., 1::2] = words >> 4
        vals = E2M1[nib]
    vals = vals * np.repeat(np.exp2(scales.astype(np.float64) - 127.0), 8, axis=1)[..., None]
    return vals.transpose(0, 1, 3, 2).reshape(g * 512, n)


def gelu(v):
    return 0.5 * v * (1.0 + np.tanh(np.sqrt(2.0 / np.pi) * (v + 0.044715 * v**3)))


def bf(x):
    return np.asarray(x, np.float32).astype(ml_dtypes.bfloat16)

def planes(Y):
    n, m = Y.shape
    b = f64(bf(Y)).reshape(n // 32, 32, m)
    amax = np.abs(b).max(1)
    byte = np.clip(np.where(amax > 0, np.frexp(amax)[1] - 1 + 127 - 7, 1), 1, 254)
    codes = (b * np.exp2(127.0 - byte)[:, None, :]).reshape(n, m).astype(np.float32).astype(ml_dtypes.float8_e4m3fn).view(np.uint8)
    words = codes.reshape(n // 512, 128, 4, m).transpose(0, 1, 3, 2)
    return np.ascontiguousarray(words), np.ascontiguousarray(byte.astype(np.uint8).reshape(n // 512, 16, m))


K, H, T, S, T2, S2 = 1024, 512, 2048, 1024, 4096, 1536

def setup_inputs():
    n = np.random.standard_normal
    s = mx_kscale(K)[:, None]
    u = mx_kscale(H)[:, None]
    tab_words, tab_scales = pack_weight(n((K, T)) * s, "e4m3")
    tab2_words, tab2_scales = pack_weight(1.5 * n((H, T2)) / np.sqrt(H) / u, "e4m3")
    wp_words, wp_scales = pack_weight(n((K, H)) / np.sqrt(K) / s * u.T, "e2m1")
    wg = (n((K, H)) / np.sqrt(K) / s).astype(np.float32)
    strength = np.exp(0.8 * n(S2)).astype(np.float32)
    offs = striped(np.random.permutation(T)[:S])
    offs2 = striped(np.random.permutation(T2)[:S2])
    return {"tab_words": tab_words, "tab_scales": tab_scales,
            "tab2_words": tab2_words, "tab2_scales": tab2_scales,
            "wp_words": wp_words, "wp_scales": wp_scales,
            "wg": wg, "strength": strength, "offs": offs, "offs2": offs2}

def reference(tab_words, tab_scales, tab2_words, tab2_scales, wp_words, wp_scales,
              wg, strength, offs, offs2):
    v = unpack_weight(tab_words, tab_scales, "e4m3")[:, unstriped(offs)]
    v2 = unpack_weight(tab2_words, tab2_scales, "e4m3")[:, unstriped(offs2)]
    wp = unpack_weight(wp_words, wp_scales, "e2m1")
    p = wp.T @ v
    a = mxq(f64(wg), 0, "e4m3").T @ v
    h = p * (1.0 / (1.0 + np.exp(-a)))
    m = v2.T @ mxq(h, 0, "e4m3")
    y = f64(strength)[:, None] * (m * m * m)
    words, scales = planes(y)
    return y, words, scales

@@ -1,0 +1,290 @@
+from contextlib import ExitStack
+
+import concourse.mybir as mybir
+
+K, H, T, S, T2, S2 = 1024, 512, 2048, 1024, 4096, 1536
+FLOPS = 2 * 2 * K * H * S + 2 * H * S2 * S
+
+F32 = mybir.dt.float32
+BF16 = mybir.dt.bfloat16
+I32 = mybir.dt.int32
+U32 = mybir.dt.uint32
+U16 = mybir.dt.uint16
+U8 = mybir.dt.uint8
+FP8X4 = mybir.dt.float8_e4m3fn_x4
+FP4X4 = mybir.dt.float4_e2m1fn_x4
+ACT = mybir.ActivationFunctionType
+MULT = mybir.AluOpType.mult
+
+P = 128
+PACK = 4
+KP = P * PACK
+PASSES = K // KP
+HALF = 512
+HALVES = S // HALF
+JT = 128
+TILES = HALF // JT
+GROUPS = S2 // KP
+QUADS = 4
+PER_COL = 16
+
+
+def tile_list_cubic_recall_weights_kernel(
+    tc, tab_words, tab_scales, tab2_words, tab2_scales, wp_words, wp_scales, wg, strength, offs, offs2,
+    out_0, out_1, out_2,
+):
+    nc = tc.nc
+    with ExitStack() as ctx:
+        keep = ctx.enter_context(tc.tile_pool(name="keep", bufs=1))
+        ring = ctx.enter_context(tc.tile_pool(name="ring", bufs=3))
+        psum = ctx.enter_context(tc.psum_pool(name="psum", bufs=8))
+
+        def held(name, shape, dtype, tag=""):
+            return keep.tile(shape, dtype, name=name, tag=tag or name, align_bytes=64)
+
+        offs_t = keep.tile([P, S // PER_COL], U16, name="offs_t")
+        offs2_t = keep.tile([P, S2 // PER_COL], U16, name="offs2_t")
+        tab_w = [held("tab_w%d" % a, [P, T], U32) for a in range(PASSES)]
+        tab_s = held("tab_s", [P, T], U8)
+        tab2_w = held("tab2_w", [P, T2], U32)
+        tab2_s = held("tab2_s", [P, T2], U8)
+        wp_raw = held("wp_raw", [P, PASSES, 2 * H], U8)
+        wp_raw_s = held("wp_raw_s", [P, PASSES, H], U8)
+        wp_w = held("wp_w", [P, PASSES, 2 * H], U8)
+        wp_s = held("wp_s", [P, PASSES, H], U8)
+        wg_raw = [held("wg_raw%d" % a, [P, PACK, H], F32) for a in range(PASSES)]
+        wg_bf = [held("wg_bf%d" % a, [P, H * PACK], BF16) for a in range(PASSES)]
+        wg_w = [held("wg_w%d" % a, [P, H], U32) for a in range(PASSES)]
+        wg_s = [held("wg_s%d" % a, [P, H], U8) for a in range(PASSES)]
+        strength_t = held("strength_t", [P, GROUPS, PACK], F32)
+        v_w = {}
+        v_s0 = held("v_s0", [P, S], U8)
+        v_s = [v_s0]
+        v2_gw = {}
+        v2_gs = {}
+        v2_w = [held("v2_w%d" % g, [P, KP], U32) for g in range(GROUPS)]
+        v2_s = [held("v2_s%d" % g, [P, KP], U8) for g in range(GROUPS)]
+        h_bf = [held("h_bf%d" % x, [P, HALF * PACK], BF16) for x in range(HALVES)]
+        h_w = [held("h_w%d" % x, [P, HALF], U32) for x in range(HALVES)]
+        h_s = [held("h_s%d" % x, [P, HALF], U8) for x in range(HALVES)]
+        y_s = [held("y_s%d" % g, [P, S], U8) for g in range(GROUPS)]
+
+        for tile in (tab_s, wp_raw_s, tab2_s):
+            flat = tile[:] if len(tile.shape) == 2 else tile[:].rearrange("p a c -> p (a c)")
+            (nc.gpsimd if tile is tab_s else nc.vector).memset(flat.bitcast(I32), 0)
+
+        def load_words(tile, words):
+            nc.sync.dma_start(tile[:].bitcast(I32), words.rearrange("p t i -> p (t i)").bitcast(I32))
+
+        def load_wg(a):
+            nc.sync.dma_start(wg_raw[a][:], wg[a * KP:(a + 1) * KP, :].rearrange("(p j) c -> p j c", j=PACK))
+
+        nc.sync.dma_start(offs_t[:], offs)
+        nc.sync.dma_start(offs2_t[:], offs2)
+        nc.sync.dma_start(wp_raw[:].bitcast(I32), wp_words.rearrange("a p c -> p a c").bitcast(I32))
+        for q in range(QUADS):
+            nc.sync.dma_start(tab_s[32 * q:32 * q + 8, :].bitcast(I32), tab_scales[:, 4 * q:4 * q + 4, :].bitcast(I32))
+        load_wg(0)
+        load_words(tab_w[0], tab_words[0])
+        for q in range(QUADS):
+            nc.sync.dma_start(wp_raw_s[32 * q:32 * q + 4, :, :].bitcast(I32),
+                              wp_scales[:, 4 * q:4 * q + 4, :].rearrange("a r c -> r a c").bitcast(I32))
+        for q in range(QUADS):
+            nc.gpsimd.dma_start(tab2_s[32 * q:32 * q + 4, :].bitcast(I32), tab2_scales[0, 4 * q:4 * q + 4, :].bitcast(I32))
+        nc.gpsimd.dma_start(strength_t[:], strength.rearrange("(g p t) -> p g t", p=P, t=PACK))
+        load_wg(1)
+        load_words(tab_w[1], tab_words[1])
+        load_words(tab2_w, tab2_words[0])
+
+        def deal_wp():
+            for a in range(PASSES):
+                nc.vector.tensor_copy(wp_w[:, a, :].rearrange("p (t m b) -> p t m b", t=PACK, b=2),
+                                      wp_raw[:, a, :].rearrange("p (m t b) -> p t m b", t=PACK, b=2))
+            nc.vector.tensor_copy(wp_s[:].rearrange("p a (t m) -> p a t m", t=PACK),
+                                  wp_raw_s[:].rearrange("p a (m t) -> p a t m", t=PACK))
+
+        def gather_v_scales():
+            nc.vector.tensor_copy(v_s0[:], tab_s[:].indirect(offs_t[:]))
+
+        def move_v_scales():
+            v_s1 = held("v_s1", [P, S], U8, "wg_raw0")
+            v_s.append(v_s1)
+            nc.gpsimd.memset(v_s1[:].bitcast(I32), 0)
+            for q in range(QUADS):
+                nc.scalar.dma_start(v_s1[32 * q:32 * q + 4, :].bitcast(I32), v_s0[32 * q + 4:32 * q + 8, :].bitcast(I32))
+
+        def gather_v(a, x, tag=""):
+            cols = HALF // PER_COL
+            v_w[a, x] = held("v_w%d_%d" % (a, x), [P, HALF], U32, tag)
+            nc.vector.tensor_copy(v_w[a, x][:], tab_w[a][:].indirect(offs_t[:, x * cols:(x + 1) * cols]))
+
+        def round_wg(a):
+            nc.scalar.copy(wg_bf[a][:].rearrange("p (t m j) -> p m j t", t=PACK, j=PACK),
+                           wg_raw[a][:].rearrange("p j (m t) -> p m j t", t=PACK))
+
+        def quantize_wg(a):
+            nc.vector.quantize_mx(out=wg_w[a][:].bitcast(FP8X4), scales=wg_s[a][:], in_=wg_bf[a][:])
+
+        def gather_v2_scales(g, tag=""):
+            cols = KP // PER_COL
+            v2_gs[g] = held("v2_gs%d" % g, [P, KP], U8, tag)
+            nc.vector.tensor_copy(v2_gs[g][:], tab2_s[:].indirect(offs2_t[:, g * cols:(g + 1) * cols]))
+
+        def gather_v2_words(g, tag=""):
+            cols = KP // PER_COL
+            v2_gw[g] = held("v2_gw%d" % g, [P, KP], U32, tag)
+            nc.vector.tensor_copy(v2_gw[g][:], tab2_w[:].indirect(offs2_t[:, g * cols:(g + 1) * cols]))
+
+        def deal_v2_scales(g):
+            nc.vector.tensor_copy(v2_s[g][:].rearrange("p (t m) -> p t m", t=PACK),
+                                  v2_gs[g][:].rearrange("p (m t) -> p t m", t=PACK))
+
+        def deal_v2_words(g):
+            nc.vector.tensor_copy(v2_w[g][:].rearrange("p (t m) -> p m t", t=PACK),
+                                  v2_gw[g][:].rearrange("p (m t) -> p m t", t=PACK))
+
+        def p_pass(bank, a, x, u):
+            js = slice(u * JT, (u + 1) * JT)
+            sj = slice(x * HALF + u * JT, x * HALF + (u + 1) * JT)
+            for t in range(PACK):
+                nc.tensor.matmul_mx(
+                    out=bank[:, t, :],
+                    lhsT=wp_w[:, a, 2 * P * t:2 * P * (t + 1)].bitcast(FP4X4), lhsT_scale=wp_s[:, a, P * t:P * (t + 1)],
+                    rhs=v_w[a, x][:, js].bitcast(FP8X4), rhs_scale=v_s[a][:, sj],
+                    start=(a == 0 and t == 0), stop=(a == PASSES - 1 and t == PACK - 1))
+
+        def a_pass(bank, a, x, u):
+            js = slice(u * JT, (u + 1) * JT)
+            sj = slice(x * HALF + u * JT, x * HALF + (u + 1) * JT)
+            for t in range(PACK):
+                nc.tensor.matmul_mx(
+                    out=bank[:, t, :],
+                    lhsT=wg_w[a][:, P * t:P * (t + 1)].bitcast(FP8X4), lhsT_scale=wg_s[a][:, P * t:P * (t + 1)],
+                    rhs=v_w[a, x][:, js].bitcast(FP8X4), rhs_scale=v_s0[4 * a:P, sj],
+                    start=(a == 0 and t == 0), stop=(a == PASSES - 1 and t == PACK - 1))
+
+        def gate(p_bank, a_bank, x, u):
+            if (x, u) == (0, 2):
+                sig = held("sig_hold", [P, JT, PACK], F32)
+            else:
+                sig = ring.tile([P, JT, PACK], F32, name="sig")
+            nc.scalar.activation(sig[:], a_bank[:].rearrange("p t j -> p j t"), ACT.Sigmoid)
+            h_out = h_bf[x][:, u * JT * PACK:(u + 1) * JT * PACK].rearrange("p (j t) -> p j t", t=PACK)
+            nc.vector.tensor_tensor(h_out, p_bank[:].rearrange("p t j -> p j t"), sig[:], MULT)
+
+        def quantize_h(x):
+            nc.vector.quantize_mx(out=h_w[x][:].bitcast(FP8X4), scales=h_s[x][:], in_=h_bf[x][:])
+
+        def new_bank():
+            return psum.tile([P, PACK, JT], F32, name="bank")
+
+        def h_tile(x, u):
+            p_bank, a_bank = new_bank(), new_bank()
+            for a in range(PASSES):
+                a_pass(a_bank, a, x, u)
+            for a in range(PASSES):
+                p_pass(p_bank, a, x, u)
+            gate(p_bank, a_bank, x, u)
+
+        y_rows = out_0.rearrange("(g p t) j -> g p t j", p=P, t=PACK)
+
+        def cube(g, x, last):
+            y = ring.tile([P, PACK, HALF], F32, name="y", bufs=4)
+            for t in range(PACK):
+                bank = new_bank()
+                m = bank[:].rearrange("p t j -> p (t j)")
+                nc.tensor.matmul_mx(
+                    out=m, lhsT=v2_w[g][:, P * t:P * (t + 1)].bitcast(FP8X4), lhsT_scale=v2_s[g][:, P * t:P * (t + 1)],
+                    rhs=h_w[x][:].bitcast(FP8X4), rhs_scale=h_s[x][:], start=True, stop=True)
+                if (g, x, t) == (0, 0, 3):
+                    sq = held("sq_hold", [P, HALF], F32)
+                else:
+                    sq = ring.tile([P, HALF], F32, name="sq")
+                nc.scalar.activation(sq[:], m, ACT.Square)
+                nc.vector.scalar_tensor_tensor(y[:, t, :], m, strength_t[:, g, t:t + 1], sq[:], MULT, MULT)
+                if last:
+                    nc.sync.dma_start(y_rows[g, :, t, x * HALF:(x + 1) * HALF], y[:, t, :])
+            if not last:
+                nc.sync.dma_start(y_rows[g, :, :, x * HALF:(x + 1) * HALF], y[:])
+            return y
+
+        def round_y(y, on_vector):
+            y_bf = ring.tile([P, HALF * PACK], BF16, name="y_bf", align_bytes=64)
+            dst = y_bf[:].rearrange("p (c i t) -> p c t i", i=4, t=PACK)
+            src = y[:].rearrange("p t (c i) -> p c t i", i=4)
+            split = HALF // 4 - on_vector // 4
+            if split > 0:
+                nc.scalar.copy(dst[:, :split], src[:, :split])
+            if on_vector > 0:
+                nc.vector.tensor_copy(dst[:, split:], src[:, split:])
+            return y_bf
+
+        def quantize_y(y_bf, g, x):
+            y_w = ring.tile([P, HALF], U32, name="y_w", align_bytes=64)
+            nc.vector.quantize_mx(out=y_w[:].bitcast(FP8X4), scales=y_s[g][:, x * HALF:(x + 1) * HALF], in_=y_bf[:])
+            words = out_1[g].rearrange("p m t -> p (m t)").bitcast(I32)
+            nc.sync.dma_start(words[:, x * HALF:(x + 1) * HALF], y_w[:].bitcast(I32))
+
+        def store_y_scales(g):
+            for q in range(QUADS):
+                nc.sync.dma_start(out_2[g, 4 * q:4 * q + 4, :].bitcast(I32), y_s[g][32 * q:32 * q + 4, :].bitcast(I32))
+
+        deal_wp()
+        gather_v_scales()
+        round_wg(0)
+        move_v_scales()
+        gather_v(0, 0)
+        quantize_wg(0)
+        p_banks = [new_bank() for u in range(TILES)]
+        a_banks = [new_bank() for u in range(TILES)]
+        for u in range(TILES):
+            a_pass(a_banks[u], 0, 0, u)
+        for u in range(TILES):
+            p_pass(p_banks[u], 0, 0, u)
+        round_wg(1)
+        gather_v(0, 1, "wg_bf0")
+        gather_v(1, 0)
+        quantize_wg(1)
+        gather_v2_scales(0, "wg_bf1")
+        deal_v2_scales(0)
+        for u in range(TILES):
+            a_pass(a_banks[u], 1, 0, u)
+            p_pass(p_banks[u], 1, 0, u)
+            gate(p_banks[u], a_banks[u], 0, u)
+        gather_v2_words(0, "sig_hold")
+        quantize_h(0)
+        deal_v2_words(0)
+        gather_v2_scales(1, "h_bf0")
+        deal_v2_scales(1)
+        gather_v2_words(1, "h_bf0")
+        deal_v2_words(1)
+
+        y00 = cube(0, 0, False)
+        gather_v(1, 1, "sq_hold")
+        b00 = round_y(y00, 0)
+        y10 = cube(1, 0, False)
+        quantize_y(b00, 0, 0)
+        for u in range(TILES):
+            h_tile(1, u)
+        b10 = round_y(y10, 0)
+        quantize_h(1)
+        gather_v2_scales(2, "h_bf1")
+        quantize_y(b10, 1, 0)
+        deal_v2_scales(2)
+        y01 = cube(0, 1, False)
+        gather_v2_words(2, "h_bf1")
+        deal_v2_words(2)
+        y11 = cube(1, 1, False)
+        b01 = round_y(y01, 0)
+        y20 = cube(2, 0, False)
+        quantize_y(b01, 0, 1)
+        store_y_scales(0)
+        b11 = round_y(y11, 0)
+        y21 = cube(2, 1, True)
+        quantize_y(b11, 1, 1)
+        store_y_scales(1)
+        b20 = round_y(y20, 128)
+        quantize_y(b20, 2, 0)
+        b21 = round_y(y21, 384)
+        quantize_y(b21, 2, 1)
+        store_y_scales(2)

@@ -37,7 +37,7 @@ def tile_list_cubic_recall_weights_kernel(
     with ExitStack() as ctx:
         keep = ctx.enter_context(tc.tile_pool(name="keep", bufs=1))
         ring = ctx.enter_context(tc.tile_pool(name="ring", bufs=3))
-        psum = ctx.enter_context(tc.psum_pool(name="psum", bufs=8))
+        psum = ctx.enter_context(tc.psum_pool(name="psum", bufs=1))
 
         def held(name, shape, dtype, tag=""):
             return keep.tile(shape, dtype, name=name, tag=tag or name, align_bytes=64)
@@ -46,7 +46,6 @@ def tile_list_cubic_recall_weights_kernel(
         offs2_t = keep.tile([P, S2 // PER_COL], U16, name="offs2_t")
         tab_w = [held("tab_w%d" % a, [P, T], U32) for a in range(PASSES)]
         tab_s = held("tab_s", [P, T], U8)
-        tab2_w = held("tab2_w", [P, T2], U32)
         tab2_s = held("tab2_s", [P, T2], U8)
         wp_raw = held("wp_raw", [P, PASSES, 2 * H], U8)
         wp_raw_s = held("wp_raw_s", [P, PASSES, H], U8)
@@ -57,9 +56,10 @@ def tile_list_cubic_recall_weights_kernel(
         wg_w = [held("wg_w%d" % a, [P, H], U32) for a in range(PASSES)]
         wg_s = [held("wg_s%d" % a, [P, H], U8) for a in range(PASSES)]
         strength_t = held("strength_t", [P, GROUPS, PACK], F32)
-        v_w = {}
+        v_w = [held("v_w%d" % a, [P, S], U32) for a in range(PASSES)]
         v_s0 = held("v_s0", [P, S], U8)
-        v_s = [v_s0]
+        v_s1 = held("v_s1", [P, S], U8)
+        v_s = [v_s0, v_s1]
         v2_gw = {}
         v2_gs = {}
         v2_w = [held("v2_w%d" % g, [P, KP], U32) for g in range(GROUPS)]
@@ -67,9 +67,11 @@ def tile_list_cubic_recall_weights_kernel(
         h_bf = [held("h_bf%d" % x, [P, HALF * PACK], BF16) for x in range(HALVES)]
         h_w = [held("h_w%d" % x, [P, HALF], U32) for x in range(HALVES)]
         h_s = [held("h_s%d" % x, [P, HALF], U8) for x in range(HALVES)]
-        y_s = [held("y_s%d" % g, [P, S], U8) for g in range(GROUPS)]
+        y_s0 = held("y_s0", [P, S], U8)
+        y_s12 = held("y_s12", [P, S], U8)
+        y_s = [y_s0[:], y_s12[:], y_s12[4:P, :]]
 
-        for tile in (tab_s, wp_raw_s, tab2_s):
+        for tile in (tab_s, wp_raw_s, tab2_s, v_s1):
             flat = tile[:] if len(tile.shape) == 2 else tile[:].rearrange("p a c -> p (a c)")
             (nc.gpsimd if tile is tab_s else nc.vector).memset(flat.bitcast(I32), 0)
 
@@ -80,43 +82,34 @@ def tile_list_cubic_recall_weights_kernel(
             nc.sync.dma_start(wg_raw[a][:], wg[a * KP:(a + 1) * KP, :].rearrange("(p j) c -> p j c", j=PACK))
 
         nc.sync.dma_start(offs_t[:], offs)
-        nc.sync.dma_start(offs2_t[:], offs2)
         nc.sync.dma_start(wp_raw[:].bitcast(I32), wp_words.rearrange("a p c -> p a c").bitcast(I32))
         for q in range(QUADS):
             nc.sync.dma_start(tab_s[32 * q:32 * q + 8, :].bitcast(I32), tab_scales[:, 4 * q:4 * q + 4, :].bitcast(I32))
-        load_wg(0)
         load_words(tab_w[0], tab_words[0])
+        nc.sync.dma_start(offs2_t[:], offs2)
         for q in range(QUADS):
             nc.sync.dma_start(wp_raw_s[32 * q:32 * q + 4, :, :].bitcast(I32),
                               wp_scales[:, 4 * q:4 * q + 4, :].rearrange("a r c -> r a c").bitcast(I32))
-        for q in range(QUADS):
-            nc.gpsimd.dma_start(tab2_s[32 * q:32 * q + 4, :].bitcast(I32), tab2_scales[0, 4 * q:4 * q + 4, :].bitcast(I32))
-        nc.gpsimd.dma_start(strength_t[:], strength.rearrange("(g p t) -> p g t", p=P, t=PACK))
-        load_wg(1)
         load_words(tab_w[1], tab_words[1])
-        load_words(tab2_w, tab2_words[0])
+        for q in range(QUADS):
+            nc.sync.dma_start(tab2_s[32 * q:32 * q + 4, :].bitcast(I32), tab2_scales[0, 4 * q:4 * q + 4, :].bitcast(I32))
+        nc.sync.dma_start(strength_t[:], strength.rearrange("(g p t) -> p g t", p=P, t=PACK))
+        load_wg(0)
+        load_wg(1)
 
         def deal_wp():
-            for a in range(PASSES):
-                nc.vector.tensor_copy(wp_w[:, a, :].rearrange("p (t m b) -> p t m b", t=PACK, b=2),
-                                      wp_raw[:, a, :].rearrange("p (m t b) -> p t m b", t=PACK, b=2))
+            nc.vector.tensor_copy(wp_w[:].bitcast(U16).rearrange("p a (t m) -> p a t m", t=PACK),
+                                  wp_raw[:].bitcast(U16).rearrange("p a (m t) -> p a t m", t=PACK))
             nc.vector.tensor_copy(wp_s[:].rearrange("p a (t m) -> p a t m", t=PACK),
                                   wp_raw_s[:].rearrange("p a (m t) -> p a t m", t=PACK))
 
         def gather_v_scales():
             nc.vector.tensor_copy(v_s0[:], tab_s[:].indirect(offs_t[:]))
-
-        def move_v_scales():
-            v_s1 = held("v_s1", [P, S], U8, "wg_raw0")
-            v_s.append(v_s1)
-            nc.gpsimd.memset(v_s1[:].bitcast(I32), 0)
             for q in range(QUADS):
-                nc.scalar.dma_start(v_s1[32 * q:32 * q + 4, :].bitcast(I32), v_s0[32 * q + 4:32 * q + 8, :].bitcast(I32))
+                nc.sync.dma_start(v_s1[32 * q:32 * q + 4, :].bitcast(I32), v_s0[32 * q + 4:32 * q + 8, :].bitcast(I32))
 
-        def gather_v(a, x, tag=""):
-            cols = HALF // PER_COL
-            v_w[a, x] = held("v_w%d_%d" % (a, x), [P, HALF], U32, tag)
-            nc.vector.tensor_copy(v_w[a, x][:], tab_w[a][:].indirect(offs_t[:, x * cols:(x + 1) * cols]))
+        def gather_v(a):
+            nc.vector.tensor_copy(v_w[a][:], tab_w[a][:].indirect(offs_t[:]))
 
         def round_wg(a):
             nc.scalar.copy(wg_bf[a][:].rearrange("p (t m j) -> p m j t", t=PACK, j=PACK),
@@ -144,23 +137,21 @@ def tile_list_cubic_recall_weights_kernel(
                                   v2_gw[g][:].rearrange("p (m t) -> p m t", t=PACK))
 
         def p_pass(bank, a, x, u):
-            js = slice(u * JT, (u + 1) * JT)
             sj = slice(x * HALF + u * JT, x * HALF + (u + 1) * JT)
             for t in range(PACK):
                 nc.tensor.matmul_mx(
                     out=bank[:, t, :],
                     lhsT=wp_w[:, a, 2 * P * t:2 * P * (t + 1)].bitcast(FP4X4), lhsT_scale=wp_s[:, a, P * t:P * (t + 1)],
-                    rhs=v_w[a, x][:, js].bitcast(FP8X4), rhs_scale=v_s[a][:, sj],
+                    rhs=v_w[a][:, sj].bitcast(FP8X4), rhs_scale=v_s[a][:, sj],
                     start=(a == 0 and t == 0), stop=(a == PASSES - 1 and t == PACK - 1))
 
         def a_pass(bank, a, x, u):
-            js = slice(u * JT, (u + 1) * JT)
             sj = slice(x * HALF + u * JT, x * HALF + (u + 1) * JT)
             for t in range(PACK):
                 nc.tensor.matmul_mx(
                     out=bank[:, t, :],
                     lhsT=wg_w[a][:, P * t:P * (t + 1)].bitcast(FP8X4), lhsT_scale=wg_s[a][:, P * t:P * (t + 1)],
-                    rhs=v_w[a, x][:, js].bitcast(FP8X4), rhs_scale=v_s0[4 * a:P, sj],
+                    rhs=v_w[a][:, sj].bitcast(FP8X4), rhs_scale=v_s0[4 * a:P, sj],
                     start=(a == 0 and t == 0), stop=(a == PASSES - 1 and t == PACK - 1))
 
         def gate(p_bank, a_bank, x, u):
@@ -175,11 +166,11 @@ def tile_list_cubic_recall_weights_kernel(
         def quantize_h(x):
             nc.vector.quantize_mx(out=h_w[x][:].bitcast(FP8X4), scales=h_s[x][:], in_=h_bf[x][:])
 
-        def new_bank():
-            return psum.tile([P, PACK, JT], F32, name="bank")
+        def new_bank(b):
+            return psum.tile([P, PACK, JT], F32, name="bank%d" % b)
 
-        def h_tile(x, u):
-            p_bank, a_bank = new_bank(), new_bank()
+        def h_tile(x, u, pair):
+            a_bank, p_bank = new_bank(pair), new_bank(pair + TILES)
             for a in range(PASSES):
                 a_pass(a_bank, a, x, u)
             for a in range(PASSES):
@@ -188,18 +179,18 @@ def tile_list_cubic_recall_weights_kernel(
 
         y_rows = out_0.rearrange("(g p t) j -> g p t j", p=P, t=PACK)
 
-        def cube(g, x, last):
+        def cube(g, x, banks, last):
             y = ring.tile([P, PACK, HALF], F32, name="y", bufs=4)
             for t in range(PACK):
-                bank = new_bank()
+                bank = new_bank(banks[t])
                 m = bank[:].rearrange("p t j -> p (t j)")
                 nc.tensor.matmul_mx(
                     out=m, lhsT=v2_w[g][:, P * t:P * (t + 1)].bitcast(FP8X4), lhsT_scale=v2_s[g][:, P * t:P * (t + 1)],
                     rhs=h_w[x][:].bitcast(FP8X4), rhs_scale=h_s[x][:], start=True, stop=True)
-                if (g, x, t) == (0, 0, 3):
-                    sq = held("sq_hold", [P, HALF], F32)
+                if t == PACK - 1 and (g, x) in ((0, 0), (0, 1)):
+                    sq = held("sq_hold%d" % x, [P, HALF], F32)
                 else:
-                    sq = ring.tile([P, HALF], F32, name="sq")
+                    sq = ring.tile([P, HALF], F32, name="sq", bufs=8)
                 nc.scalar.activation(sq[:], m, ACT.Square)
                 nc.vector.scalar_tensor_tensor(y[:, t, :], m, strength_t[:, g, t:t + 1], sq[:], MULT, MULT)
                 if last:
@@ -208,8 +199,11 @@ def tile_list_cubic_recall_weights_kernel(
                 nc.sync.dma_start(y_rows[g, :, :, x * HALF:(x + 1) * HALF], y[:])
             return y
 
-        def round_y(y, on_vector):
-            y_bf = ring.tile([P, HALF * PACK], BF16, name="y_bf", align_bytes=64)
+        def round_y(y, on_vector, tag=""):
+            if tag:
+                y_bf = held(tag, [P, HALF * PACK], BF16)
+            else:
+                y_bf = ring.tile([P, HALF * PACK], BF16, name="y_bf", align_bytes=64)
             dst = y_bf[:].rearrange("p (c i t) -> p c t i", i=4, t=PACK)
             src = y[:].rearrange("p t (c i) -> p c t i", i=4)
             split = HALF // 4 - on_vector // 4
@@ -225,66 +219,73 @@ def tile_list_cubic_recall_weights_kernel(
             words = out_1[g].rearrange("p m t -> p (m t)").bitcast(I32)
             nc.sync.dma_start(words[:, x * HALF:(x + 1) * HALF], y_w[:].bitcast(I32))
 
-        def store_y_scales(g):
+        def store_first_scales():
             for q in range(QUADS):
-                nc.sync.dma_start(out_2[g, 4 * q:4 * q + 4, :].bitcast(I32), y_s[g][32 * q:32 * q + 4, :].bitcast(I32))
+                nc.sync.dma_start(out_2[0, 4 * q:4 * q + 4, :].bitcast(I32), y_s0[32 * q:32 * q + 4, :].bitcast(I32))
 
-        deal_wp()
+        def store_last_scales():
+            for q in range(QUADS):
+                (nc.scalar if q % 2 else nc.sync).dma_start(
+                    out_2[1:GROUPS, 4 * q:4 * q + 4, :].bitcast(I32), y_s12[32 * q:32 * q + 8, :].bitcast(I32))
+
         gather_v_scales()
-        round_wg(0)
-        move_v_scales()
-        gather_v(0, 0)
-        quantize_wg(0)
-        p_banks = [new_bank() for u in range(TILES)]
-        a_banks = [new_bank() for u in range(TILES)]
-        for u in range(TILES):
-            a_pass(a_banks[u], 0, 0, u)
+        tab2_w = held("tab2_w", [P, T2], U32, "tab_s")
+        load_words(tab2_w, tab2_words[0])
+        gather_v(0)
+        deal_wp()
+        gather_v(1)
+        p_banks = [new_bank(TILES + u) for u in range(TILES)]
+        a_banks = [new_bank(u) for u in range(TILES)]
         for u in range(TILES):
             p_pass(p_banks[u], 0, 0, u)
-        round_wg(1)
-        gather_v(0, 1, "wg_bf0")
-        gather_v(1, 0)
-        quantize_wg(1)
-        gather_v2_scales(0, "wg_bf1")
+        round_wg(0)
+        quantize_wg(0)
+        for u in range(TILES):
+            a_pass(a_banks[u], 0, 0, u)
+        gather_v2_scales(0, "wg_bf0")
         deal_v2_scales(0)
         for u in range(TILES):
-            a_pass(a_banks[u], 1, 0, u)
             p_pass(p_banks[u], 1, 0, u)
+        round_wg(1)
+        quantize_wg(1)
+        gather_v2_scales(1, "wg_bf1")
+        deal_v2_scales(1)
+        for u in range(TILES):
+            a_pass(a_banks[u], 1, 0, u)
             gate(p_banks[u], a_banks[u], 0, u)
+        gather_v2_scales(2, "sig_hold")
+        deal_v2_scales(2)
         gather_v2_words(0, "sig_hold")
         quantize_h(0)
         deal_v2_words(0)
-        gather_v2_scales(1, "h_bf0")
-        deal_v2_scales(1)
-        gather_v2_words(1, "h_bf0")
-        deal_v2_words(1)
 
-        y00 = cube(0, 0, False)
-        gather_v(1, 1, "sq_hold")
-        b00 = round_y(y00, 0)
-        y10 = cube(1, 0, False)
-        quantize_y(b00, 0, 0)
-        for u in range(TILES):
-            h_tile(1, u)
-        b10 = round_y(y10, 0)
+        inner, outer = (1, 5, 2, 6), (0, 4, 3, 7)
+        h_tile(1, 0, 0)
+        h_tile(1, 1, 3)
+        y00 = cube(0, 0, inner, False)
+        h_tile(1, 2, 1)
+        gather_v2_words(1, "sq_hold0")
+        deal_v2_words(1)
+        h_tile(1, 3, 2)
         quantize_h(1)
-        gather_v2_scales(2, "h_bf1")
-        quantize_y(b10, 1, 0)
-        deal_v2_scales(2)
-        y01 = cube(0, 1, False)
-        gather_v2_words(2, "h_bf1")
+        b00 = round_y(y00, 0)
+        quantize_y(b00, 0, 0)
+        y10 = cube(1, 0, outer, False)
+        y01 = cube(0, 1, inner, False)
+        b10 = round_y(y10, 0)
+        gather_v2_words(2, "sq_hold1")
         deal_v2_words(2)
-        y11 = cube(1, 1, False)
+        quantize_y(b10, 1, 0)
+        y11 = cube(1, 1, outer, False)
         b01 = round_y(y01, 0)
-        y20 = cube(2, 0, False)
         quantize_y(b01, 0, 1)
-        store_y_scales(0)
+        store_first_scales()
+        y20 = cube(2, 0, inner, False)
+        y21 = cube(2, 1, outer, True)
         b11 = round_y(y11, 0)
-        y21 = cube(2, 1, True)
-        quantize_y(b11, 1, 1)
-        store_y_scales(1)
-        b20 = round_y(y20, 128)
+        b20 = round_y(y20, 512)
         quantize_y(b20, 2, 0)
-        b21 = round_y(y21, 384)
+        quantize_y(b11, 1, 1)
+        b21 = round_y(y21, 256)
         quantize_y(b21, 2, 1)
-        store_y_scales(2)
+        store_last_scales()

@@ -73,7 +73,7 @@ def tile_list_cubic_recall_weights_kernel(
 
         for tile in (tab_s, wp_raw_s, tab2_s, v_s1):
             flat = tile[:] if len(tile.shape) == 2 else tile[:].rearrange("p a c -> p (a c)")
-            (nc.gpsimd if tile is tab_s else nc.vector).memset(flat.bitcast(I32), 0)
+            (nc.gpsimd if tile is tab2_s else nc.vector).memset(flat.bitcast(I32), 0)
 
         def load_words(tile, words):
             nc.sync.dma_start(tile[:].bitcast(I32), words.rearrange("p t i -> p (t i)").bitcast(I32))
@@ -82,18 +82,19 @@ def tile_list_cubic_recall_weights_kernel(
             nc.sync.dma_start(wg_raw[a][:], wg[a * KP:(a + 1) * KP, :].rearrange("(p j) c -> p j c", j=PACK))
 
         nc.sync.dma_start(offs_t[:], offs)
-        nc.sync.dma_start(wp_raw[:].bitcast(I32), wp_words.rearrange("a p c -> p a c").bitcast(I32))
-        for q in range(QUADS):
+        for q in (0, 2, 1, 3):
             nc.sync.dma_start(tab_s[32 * q:32 * q + 8, :].bitcast(I32), tab_scales[:, 4 * q:4 * q + 4, :].bitcast(I32))
-        load_words(tab_w[0], tab_words[0])
+        nc.sync.dma_start(wp_raw[:].bitcast(I32), wp_words.rearrange("a p c -> p a c").bitcast(I32))
         nc.sync.dma_start(offs2_t[:], offs2)
-        for q in range(QUADS):
-            nc.sync.dma_start(wp_raw_s[32 * q:32 * q + 4, :, :].bitcast(I32),
-                              wp_scales[:, 4 * q:4 * q + 4, :].rearrange("a r c -> r a c").bitcast(I32))
+        load_words(tab_w[0], tab_words[0])
+        for r in range(4):
+            nc.sync.dma_start(wp_raw_s[r:P:32, :, :].bitcast(I32),
+                              wp_scales.rearrange("a (q r) c -> r q a c", r=4)[r].bitcast(I32))
         load_words(tab_w[1], tab_words[1])
-        for q in range(QUADS):
-            nc.sync.dma_start(tab2_s[32 * q:32 * q + 4, :].bitcast(I32), tab2_scales[0, 4 * q:4 * q + 4, :].bitcast(I32))
-        nc.sync.dma_start(strength_t[:], strength.rearrange("(g p t) -> p g t", p=P, t=PACK))
+        for r in range(4):
+            nc.gpsimd.dma_start(tab2_s[8 + r:P:32, :].bitcast(I32),
+                                tab2_scales[0].rearrange("(q r) c -> r q c", r=4)[r].bitcast(I32))
+        nc.gpsimd.dma_start(strength_t[:], strength.rearrange("(g p t) -> p g t", p=P, t=PACK))
         load_wg(0)
         load_wg(1)
 
@@ -105,15 +106,15 @@ def tile_list_cubic_recall_weights_kernel(
 
         def gather_v_scales():
             nc.vector.tensor_copy(v_s0[:], tab_s[:].indirect(offs_t[:]))
-            for q in range(QUADS):
-                nc.sync.dma_start(v_s1[32 * q:32 * q + 4, :].bitcast(I32), v_s0[32 * q + 4:32 * q + 8, :].bitcast(I32))
+            for r in range(4):
+                nc.sync.dma_start(v_s1[r:P:32, :].bitcast(I32), v_s0[4 + r:P:32, :].bitcast(I32))
 
         def gather_v(a):
             nc.vector.tensor_copy(v_w[a][:], tab_w[a][:].indirect(offs_t[:]))
 
         def round_wg(a):
-            nc.scalar.copy(wg_bf[a][:].rearrange("p (t m j) -> p m j t", t=PACK, j=PACK),
-                           wg_raw[a][:].rearrange("p j (m t) -> p m j t", t=PACK))
+            nc.scalar.copy(wg_bf[a][:].rearrange("p (u e m j) -> p u m j e", u=2, e=2, j=PACK),
+                           wg_raw[a][:].rearrange("p j (m u e) -> p u m j e", u=2, e=2))
 
         def quantize_wg(a):
             nc.vector.quantize_mx(out=wg_w[a][:].bitcast(FP8X4), scales=wg_s[a][:], in_=wg_bf[a][:])
@@ -133,8 +134,8 @@ def tile_list_cubic_recall_weights_kernel(
                                   v2_gs[g][:].rearrange("p (m t) -> p t m", t=PACK))
 
         def deal_v2_words(g):
-            nc.vector.tensor_copy(v2_w[g][:].rearrange("p (t m) -> p m t", t=PACK),
-                                  v2_gw[g][:].rearrange("p (m t) -> p m t", t=PACK))
+            nc.vector.tensor_copy(v2_w[g][:].rearrange("p (u e m) -> p u m e", u=2, e=2),
+                                  v2_gw[g][:].rearrange("p (m u e) -> p u m e", u=2, e=2))
 
         def p_pass(bank, a, x, u):
             sj = slice(x * HALF + u * JT, x * HALF + (u + 1) * JT)
@@ -185,7 +186,7 @@ def tile_list_cubic_recall_weights_kernel(
                 bank = new_bank(banks[t])
                 m = bank[:].rearrange("p t j -> p (t j)")
                 nc.tensor.matmul_mx(
-                    out=m, lhsT=v2_w[g][:, P * t:P * (t + 1)].bitcast(FP8X4), lhsT_scale=v2_s[g][:, P * t:P * (t + 1)],
+                    out=m, lhsT=v2_w[g][:, P * t:P * (t + 1)].bitcast(FP8X4), lhsT_scale=v2_s[g][8:P, P * t:P * (t + 1)],
                     rhs=h_w[x][:].bitcast(FP8X4), rhs_scale=h_s[x][:], start=True, stop=True)
                 if t == PACK - 1 and (g, x) in ((0, 0), (0, 1)):
                     sq = held("sq_hold%d" % x, [P, HALF], F32)
@@ -204,9 +205,9 @@ def tile_list_cubic_recall_weights_kernel(
                 y_bf = held(tag, [P, HALF * PACK], BF16)
             else:
                 y_bf = ring.tile([P, HALF * PACK], BF16, name="y_bf", align_bytes=64)
-            dst = y_bf[:].rearrange("p (c i t) -> p c t i", i=4, t=PACK)
-            src = y[:].rearrange("p t (c i) -> p c t i", i=4)
-            split = HALF // 4 - on_vector // 4
+            dst = y_bf[:].rearrange("p (c i t) -> p c t i", i=2, t=PACK)
+            src = y[:].rearrange("p t (c i) -> p c t i", i=2)
+            split = HALF // 2 - on_vector // 2
             if split > 0:
                 nc.scalar.copy(dst[:, :split], src[:, :split])
             if on_vector > 0:
@@ -253,8 +254,6 @@ def tile_list_cubic_recall_weights_kernel(
         for u in range(TILES):
             a_pass(a_banks[u], 1, 0, u)
             gate(p_banks[u], a_banks[u], 0, u)
-        gather_v2_scales(2, "sig_hold")
-        deal_v2_scales(2)
         gather_v2_words(0, "sig_hold")
         quantize_h(0)
         deal_v2_words(0)
@@ -266,6 +265,8 @@ def tile_list_cubic_recall_weights_kernel(
         h_tile(1, 2, 1)
         gather_v2_words(1, "sq_hold0")
         deal_v2_words(1)
+        gather_v2_scales(2, "sq_hold0")
+        deal_v2_scales(2)
         h_tile(1, 3, 2)
         quantize_h(1)
         b00 = round_y(y00, 0)

@@ -92,9 +92,9 @@ def tile_list_cubic_recall_weights_kernel(
                               wp_scales.rearrange("a (q r) c -> r q a c", r=4)[r].bitcast(I32))
         load_words(tab_w[1], tab_words[1])
         for r in range(4):
-            nc.gpsimd.dma_start(tab2_s[8 + r:P:32, :].bitcast(I32),
+            nc.sync.dma_start(tab2_s[8 + r:P:32, :].bitcast(I32),
                                 tab2_scales[0].rearrange("(q r) c -> r q c", r=4)[r].bitcast(I32))
-        nc.gpsimd.dma_start(strength_t[:], strength.rearrange("(g p t) -> p g t", p=P, t=PACK))
+        nc.sync.dma_start(strength_t[:], strength.rearrange("(g p t) -> p g t", p=P, t=PACK))
         load_wg(0)
         load_wg(1)
 
@@ -156,13 +156,14 @@ def tile_list_cubic_recall_weights_kernel(
                     start=(a == 0 and t == 0), stop=(a == PASSES - 1 and t == PACK - 1))
 
         def gate(p_bank, a_bank, x, u):
-            if (x, u) == (0, 2):
-                sig = held("sig_hold", [P, JT, PACK], F32)
+            if x == 0 and u == 2:
+                sig = held("sig_hold%d" % u, [P, PACK, JT], F32)
             else:
-                sig = ring.tile([P, JT, PACK], F32, name="sig")
-            nc.scalar.activation(sig[:], a_bank[:].rearrange("p t j -> p j t"), ACT.Sigmoid)
-            h_out = h_bf[x][:, u * JT * PACK:(u + 1) * JT * PACK].rearrange("p (j t) -> p j t", t=PACK)
-            nc.vector.tensor_tensor(h_out, p_bank[:].rearrange("p t j -> p j t"), sig[:], MULT)
+                sig = ring.tile([P, PACK, JT], F32, name="sig")
+            nc.scalar.activation(sig[:], a_bank[:], ACT.Sigmoid)
+            h_out = h_bf[x][:, u * JT * PACK:(u + 1) * JT * PACK].rearrange("p (c i t) -> p c t i", i=2, t=PACK)
+            nc.vector.tensor_tensor(h_out, p_bank[:].rearrange("p t (c i) -> p c t i", i=2),
+                                    sig[:].rearrange("p t (c i) -> p c t i", i=2), MULT)
 
         def quantize_h(x):
             nc.vector.quantize_mx(out=h_w[x][:].bitcast(FP8X4), scales=h_s[x][:], in_=h_bf[x][:])
@@ -181,23 +182,20 @@ def tile_list_cubic_recall_weights_kernel(
         y_rows = out_0.rearrange("(g p t) j -> g p t j", p=P, t=PACK)
 
         def cube(g, x, banks, last):
-            y = ring.tile([P, PACK, HALF], F32, name="y", bufs=4)
+            y = ring.tile([P, PACK, HALF], F32, name="y", bufs=6)
             for t in range(PACK):
                 bank = new_bank(banks[t])
                 m = bank[:].rearrange("p t j -> p (t j)")
                 nc.tensor.matmul_mx(
                     out=m, lhsT=v2_w[g][:, P * t:P * (t + 1)].bitcast(FP8X4), lhsT_scale=v2_s[g][8:P, P * t:P * (t + 1)],
                     rhs=h_w[x][:].bitcast(FP8X4), rhs_scale=h_s[x][:], start=True, stop=True)
-                if t == PACK - 1 and (g, x) in ((0, 0), (0, 1)):
+                if t == PACK - 1 and (g, x) == (0, 0):
                     sq = held("sq_hold%d" % x, [P, HALF], F32)
                 else:
                     sq = ring.tile([P, HALF], F32, name="sq", bufs=8)
                 nc.scalar.activation(sq[:], m, ACT.Square)
                 nc.vector.scalar_tensor_tensor(y[:, t, :], m, strength_t[:, g, t:t + 1], sq[:], MULT, MULT)
-                if last:
-                    nc.sync.dma_start(y_rows[g, :, t, x * HALF:(x + 1) * HALF], y[:, t, :])
-            if not last:
-                nc.sync.dma_start(y_rows[g, :, :, x * HALF:(x + 1) * HALF], y[:])
+                nc.sync.dma_start(y_rows[g, :, t, x * HALF:(x + 1) * HALF], y[:, t, :])
             return y
 
         def round_y(y, on_vector, tag=""):
@@ -235,6 +233,8 @@ def tile_list_cubic_recall_weights_kernel(
         gather_v(0)
         deal_wp()
         gather_v(1)
+        gather_v2_scales(0, "tab_w1")
+        deal_v2_scales(0)
         p_banks = [new_bank(TILES + u) for u in range(TILES)]
         a_banks = [new_bank(u) for u in range(TILES)]
         for u in range(TILES):
@@ -243,42 +243,40 @@ def tile_list_cubic_recall_weights_kernel(
         quantize_wg(0)
         for u in range(TILES):
             a_pass(a_banks[u], 0, 0, u)
-        gather_v2_scales(0, "wg_bf0")
-        deal_v2_scales(0)
+        gather_v2_scales(1, "wg_bf0")
+        deal_v2_scales(1)
         for u in range(TILES):
             p_pass(p_banks[u], 1, 0, u)
         round_wg(1)
         quantize_wg(1)
-        gather_v2_scales(1, "wg_bf1")
-        deal_v2_scales(1)
+        gather_v2_scales(2, "wg_bf1")
+        deal_v2_scales(2)
         for u in range(TILES):
             a_pass(a_banks[u], 1, 0, u)
             gate(p_banks[u], a_banks[u], 0, u)
-        gather_v2_words(0, "sig_hold")
+        gather_v2_words(0, "sig_hold2")
         quantize_h(0)
         deal_v2_words(0)
 
-        inner, outer = (1, 5, 2, 6), (0, 4, 3, 7)
+        inner, outer = (3, 7, 2, 6), (1, 5, 0, 4)
         h_tile(1, 0, 0)
-        h_tile(1, 1, 3)
-        y00 = cube(0, 0, inner, False)
-        h_tile(1, 2, 1)
+        h_tile(1, 1, 1)
+        y00 = cube(0, 0, (2, 6, 3, 7), False)
+        h_tile(1, 2, 0)
         gather_v2_words(1, "sq_hold0")
         deal_v2_words(1)
-        gather_v2_scales(2, "sq_hold0")
-        deal_v2_scales(2)
+        gather_v2_words(2, "sq_hold0")
+        deal_v2_words(2)
         h_tile(1, 3, 2)
         quantize_h(1)
         b00 = round_y(y00, 0)
         quantize_y(b00, 0, 0)
         y10 = cube(1, 0, outer, False)
         y01 = cube(0, 1, inner, False)
-        b10 = round_y(y10, 0)
-        gather_v2_words(2, "sq_hold1")
-        deal_v2_words(2)
+        b10 = round_y(y10, 256)
         quantize_y(b10, 1, 0)
         y11 = cube(1, 1, outer, False)
-        b01 = round_y(y01, 0)
+        b01 = round_y(y01, 256)
         quantize_y(b01, 0, 1)
         store_first_scales()
         y20 = cube(2, 0, inner, False)

@@ -15,6 +15,7 @@ FP8X4 = mybir.dt.float8_e4m3fn_x4
 FP4X4 = mybir.dt.float4_e2m1fn_x4
 ACT = mybir.ActivationFunctionType
 MULT = mybir.AluOpType.mult
+ADD = mybir.AluOpType.add
 
 P = 128
 PACK = 4
@@ -51,19 +52,19 @@ def tile_list_cubic_recall_weights_kernel(
         wp_raw_s = held("wp_raw_s", [P, PASSES, H], U8)
         wp_w = held("wp_w", [P, PASSES, 2 * H], U8)
         wp_s = held("wp_s", [P, PASSES, H], U8)
-        wg_raw = [held("wg_raw%d" % a, [P, PACK, H], F32) for a in range(PASSES)]
+        wg_raw = [[] for a in range(PASSES)]
         wg_bf = [held("wg_bf%d" % a, [P, H * PACK], BF16) for a in range(PASSES)]
         wg_w = [held("wg_w%d" % a, [P, H], U32) for a in range(PASSES)]
         wg_s = [held("wg_s%d" % a, [P, H], U8) for a in range(PASSES)]
         strength_t = held("strength_t", [P, GROUPS, PACK], F32)
-        v_w = [held("v_w%d" % a, [P, S], U32) for a in range(PASSES)]
+        v_w = {}
         v_s0 = held("v_s0", [P, S], U8)
         v_s1 = held("v_s1", [P, S], U8)
         v_s = [v_s0, v_s1]
         v2_gw = {}
-        v2_gs = {}
-        v2_w = [held("v2_w%d" % g, [P, KP], U32) for g in range(GROUPS)]
-        v2_s = [held("v2_s%d" % g, [P, KP], U8) for g in range(GROUPS)]
+        v2_ms = held("v2_ms", [P, S2], U8)
+        v2_w = [None] * GROUPS
+        v2_s = [None] * GROUPS
         h_bf = [held("h_bf%d" % x, [P, HALF * PACK], BF16) for x in range(HALVES)]
         h_w = [held("h_w%d" % x, [P, HALF], U32) for x in range(HALVES)]
         h_s = [held("h_s%d" % x, [P, HALF], U8) for x in range(HALVES)]
@@ -71,69 +72,82 @@ def tile_list_cubic_recall_weights_kernel(
         y_s12 = held("y_s12", [P, S], U8)
         y_s = [y_s0[:], y_s12[:], y_s12[4:P, :]]
 
-        for tile in (tab_s, wp_raw_s, tab2_s, v_s1):
+        for tile in (tab_s, wp_raw_s, tab2_s, v_s1, v2_ms):
             flat = tile[:] if len(tile.shape) == 2 else tile[:].rearrange("p a c -> p (a c)")
-            (nc.gpsimd if tile is tab2_s else nc.vector).memset(flat.bitcast(I32), 0)
+            nc.vector.memset(flat.bitcast(I32), 0)
 
         def load_words(tile, words):
             nc.sync.dma_start(tile[:].bitcast(I32), words.rearrange("p t i -> p (t i)").bitcast(I32))
 
-        def load_wg(a):
-            nc.sync.dma_start(wg_raw[a][:], wg[a * KP:(a + 1) * KP, :].rearrange("(p j) c -> p j c", j=PACK))
+        def load_wg(a, c0, c1):
+            tile = held("wg_raw%d_%d" % (a, c0), [P, PACK, c1 - c0], F32)
+            wg_raw[a].append((tile, c0, c1))
+            nc.sync.dma_start(tile[:], wg[a * KP:(a + 1) * KP, c0:c1].rearrange("(p j) c -> p j c", j=PACK))
 
         nc.sync.dma_start(offs_t[:], offs)
+        nc.sync.dma_start(offs2_t[:], offs2)
+        nc.sync.dma_start(wp_raw[:].bitcast(I32), wp_words.rearrange("a p c -> p a c").bitcast(I32))
+        nc.sync.dma_start(strength_t[:], strength.rearrange("(g p t) -> p g t", p=P, t=PACK))
         for q in (0, 2, 1, 3):
             nc.sync.dma_start(tab_s[32 * q:32 * q + 8, :].bitcast(I32), tab_scales[:, 4 * q:4 * q + 4, :].bitcast(I32))
-        nc.sync.dma_start(wp_raw[:].bitcast(I32), wp_words.rearrange("a p c -> p a c").bitcast(I32))
-        nc.sync.dma_start(offs2_t[:], offs2)
         load_words(tab_w[0], tab_words[0])
         for r in range(4):
             nc.sync.dma_start(wp_raw_s[r:P:32, :, :].bitcast(I32),
                               wp_scales.rearrange("a (q r) c -> r q a c", r=4)[r].bitcast(I32))
+        load_wg(0, 0, H)
+        nc.sync.dma_start(tab2_s[0:16, :].bitcast(I32), tab2_scales[0].bitcast(I32))
+        load_wg(1, 0, H // 2)
         load_words(tab_w[1], tab_words[1])
-        for r in range(4):
-            nc.sync.dma_start(tab2_s[8 + r:P:32, :].bitcast(I32),
-                                tab2_scales[0].rearrange("(q r) c -> r q c", r=4)[r].bitcast(I32))
-        nc.sync.dma_start(strength_t[:], strength.rearrange("(g p t) -> p g t", p=P, t=PACK))
-        load_wg(0)
-        load_wg(1)
+        load_wg(1, H // 2, H)
 
-        def deal_wp():
+        def deal_wp_words():
             nc.vector.tensor_copy(wp_w[:].bitcast(U16).rearrange("p a (t m) -> p a t m", t=PACK),
                                   wp_raw[:].bitcast(U16).rearrange("p a (m t) -> p a t m", t=PACK))
+
+        def deal_wp_scales():
             nc.vector.tensor_copy(wp_s[:].rearrange("p a (t m) -> p a t m", t=PACK),
                                   wp_raw_s[:].rearrange("p a (m t) -> p a t m", t=PACK))
 
         def gather_v_scales():
             nc.vector.tensor_copy(v_s0[:], tab_s[:].indirect(offs_t[:]))
-            for r in range(4):
-                nc.sync.dma_start(v_s1[r:P:32, :].bitcast(I32), v_s0[4 + r:P:32, :].bitcast(I32))
+            nc.sync.dma_start(v_s1[0:100, :].bitcast(I32), v_s0[4:104, :].bitcast(I32))
 
-        def gather_v(a):
-            nc.vector.tensor_copy(v_w[a][:], tab_w[a][:].indirect(offs_t[:]))
+        def gather_v(a, halves, tag=""):
+            cols = HALF // PER_COL
+            tile = held("v_w%d%d" % (a, halves[0]), [P, HALF * len(halves)], U32, tag)
+            nc.vector.tensor_copy(tile[:], tab_w[a][:].indirect(offs_t[:, halves[0] * cols:(halves[-1] + 1) * cols]))
+            for x in halves:
+                v_w[a, x] = tile[:, (x - halves[0]) * HALF:(x - halves[0] + 1) * HALF]
 
         def round_wg(a):
-            nc.scalar.copy(wg_bf[a][:].rearrange("p (u e m j) -> p u m j e", u=2, e=2, j=PACK),
-                           wg_raw[a][:].rearrange("p j (m u e) -> p u m j e", u=2, e=2))
+            dst = wg_bf[a][:].rearrange("p (u e m j) -> p u m j e", u=2, e=2, j=PACK)
+            for tile, c0, c1 in wg_raw[a]:
+                nc.scalar.copy(dst[:, :, c0 // PACK:c1 // PACK],
+                               tile[:].rearrange("p j (m u e) -> p u m j e", u=2, e=2))
 
         def quantize_wg(a):
             nc.vector.quantize_mx(out=wg_w[a][:].bitcast(FP8X4), scales=wg_s[a][:], in_=wg_bf[a][:])
 
-        def gather_v2_scales(g, tag=""):
+        def gather_v2_scales(g0, g1, tag):
             cols = KP // PER_COL
-            v2_gs[g] = held("v2_gs%d" % g, [P, KP], U8, tag)
-            nc.vector.tensor_copy(v2_gs[g][:], tab2_s[:].indirect(offs2_t[:, g * cols:(g + 1) * cols]))
+            tile = held("v2_gs%d" % g0, [P, (g1 - g0) * KP], U8, tag)
+            nc.vector.tensor_copy(tile[:], tab2_s[:].indirect(offs2_t[:, g0 * cols:g1 * cols]))
+            for q in range(QUADS):
+                nc.sync.dma_start(v2_ms[32 * q + 8:32 * q + 12, g0 * KP:g1 * KP].bitcast(I32),
+                                  tile[4 * q:4 * q + 4, :].bitcast(I32))
 
         def gather_v2_words(g, tag=""):
             cols = KP // PER_COL
             v2_gw[g] = held("v2_gw%d" % g, [P, KP], U32, tag)
             nc.vector.tensor_copy(v2_gw[g][:], tab2_w[:].indirect(offs2_t[:, g * cols:(g + 1) * cols]))
 
-        def deal_v2_scales(g):
+        def deal_v2_scales(g, tag=""):
+            v2_s[g] = held("v2_s%d" % g, [P, KP], U8, tag)
             nc.vector.tensor_copy(v2_s[g][:].rearrange("p (t m) -> p t m", t=PACK),
-                                  v2_gs[g][:].rearrange("p (m t) -> p t m", t=PACK))
+                                  v2_ms[:, g * KP:(g + 1) * KP].rearrange("p (m t) -> p t m", t=PACK))
 
-        def deal_v2_words(g):
+        def deal_v2_words(g, tag=""):
+            v2_w[g] = held("v2_w%d" % g, [P, KP], U32, tag)
             nc.vector.tensor_copy(v2_w[g][:].rearrange("p (u e m) -> p u m e", u=2, e=2),
                                   v2_gw[g][:].rearrange("p (m u e) -> p u m e", u=2, e=2))
 
@@ -143,7 +157,7 @@ def tile_list_cubic_recall_weights_kernel(
                 nc.tensor.matmul_mx(
                     out=bank[:, t, :],
                     lhsT=wp_w[:, a, 2 * P * t:2 * P * (t + 1)].bitcast(FP4X4), lhsT_scale=wp_s[:, a, P * t:P * (t + 1)],
-                    rhs=v_w[a][:, sj].bitcast(FP8X4), rhs_scale=v_s[a][:, sj],
+                    rhs=v_w[a, x][:, u * JT:(u + 1) * JT].bitcast(FP8X4), rhs_scale=v_s[a][:, sj],
                     start=(a == 0 and t == 0), stop=(a == PASSES - 1 and t == PACK - 1))
 
         def a_pass(bank, a, x, u):
@@ -152,18 +166,20 @@ def tile_list_cubic_recall_weights_kernel(
                 nc.tensor.matmul_mx(
                     out=bank[:, t, :],
                     lhsT=wg_w[a][:, P * t:P * (t + 1)].bitcast(FP8X4), lhsT_scale=wg_s[a][:, P * t:P * (t + 1)],
-                    rhs=v_w[a][:, sj].bitcast(FP8X4), rhs_scale=v_s0[4 * a:P, sj],
+                    rhs=v_w[a, x][:, u * JT:(u + 1) * JT].bitcast(FP8X4), rhs_scale=v_s0[4 * a:P, sj],
                     start=(a == 0 and t == 0), stop=(a == PASSES - 1 and t == PACK - 1))
 
         def gate(p_bank, a_bank, x, u):
-            if x == 0 and u == 2:
-                sig = held("sig_hold%d" % u, [P, PACK, JT], F32)
-            else:
-                sig = ring.tile([P, PACK, JT], F32, name="sig")
+            sig = ring.tile([P, PACK, JT], F32, name="sig")
             nc.scalar.activation(sig[:], a_bank[:], ACT.Sigmoid)
             h_out = h_bf[x][:, u * JT * PACK:(u + 1) * JT * PACK].rearrange("p (c i t) -> p c t i", i=2, t=PACK)
             nc.vector.tensor_tensor(h_out, p_bank[:].rearrange("p t (c i) -> p c t i", i=2),
                                     sig[:].rearrange("p t (c i) -> p c t i", i=2), MULT)
+
+        def woven(name, bank, func):
+            tile = held(name, [P, JT * PACK], F32)
+            nc.scalar.activation(tile[:].rearrange("p (j t) -> p j t", t=PACK), bank[:].rearrange("p t j -> p j t"), func)
+            return tile
 
         def quantize_h(x):
             nc.vector.quantize_mx(out=h_w[x][:].bitcast(FP8X4), scales=h_s[x][:], in_=h_bf[x][:])
@@ -171,43 +187,42 @@ def tile_list_cubic_recall_weights_kernel(
         def new_bank(b):
             return psum.tile([P, PACK, JT], F32, name="bank%d" % b)
 
-        def h_tile(x, u, pair):
-            a_bank, p_bank = new_bank(pair), new_bank(pair + TILES)
-            for a in range(PASSES):
-                a_pass(a_bank, a, x, u)
-            for a in range(PASSES):
-                p_pass(p_bank, a, x, u)
-            gate(p_bank, a_bank, x, u)
+        def h_pass(banks, a, x, u):
+            a_pass(banks[0], a, x, u)
+            p_pass(banks[1], a, x, u)
 
         y_rows = out_0.rearrange("(g p t) j -> g p t j", p=P, t=PACK)
 
-        def cube(g, x, banks, last):
-            y = ring.tile([P, PACK, HALF], F32, name="y", bufs=6)
-            for t in range(PACK):
+        y = {}
+
+        def cube(g, x, banks, slices=range(PACK)):
+            if (g, x) not in y:
+                y.setdefault((g, x), ring.tile([P, PACK, HALF], F32, name="y", bufs=6))
+            for t in slices:
                 bank = new_bank(banks[t])
                 m = bank[:].rearrange("p t j -> p (t j)")
                 nc.tensor.matmul_mx(
                     out=m, lhsT=v2_w[g][:, P * t:P * (t + 1)].bitcast(FP8X4), lhsT_scale=v2_s[g][8:P, P * t:P * (t + 1)],
                     rhs=h_w[x][:].bitcast(FP8X4), rhs_scale=h_s[x][:], start=True, stop=True)
-                if t == PACK - 1 and (g, x) == (0, 0):
-                    sq = held("sq_hold%d" % x, [P, HALF], F32)
+                if x == 0 and g < 2 and t in (1, 2):
+                    sq = held("sq_hold%d%d%d" % (g, x, t), [P, HALF], F32)
                 else:
                     sq = ring.tile([P, HALF], F32, name="sq", bufs=8)
                 nc.scalar.activation(sq[:], m, ACT.Square)
-                nc.vector.scalar_tensor_tensor(y[:, t, :], m, strength_t[:, g, t:t + 1], sq[:], MULT, MULT)
-                nc.sync.dma_start(y_rows[g, :, t, x * HALF:(x + 1) * HALF], y[:, t, :])
-            return y
+                nc.vector.scalar_tensor_tensor(y[g, x][:, t, :], m, strength_t[:, g, t:t + 1], sq[:], MULT, MULT)
+                if t % 2:
+                    nc.sync.dma_start(y_rows[g, :, t - 1:t + 1, x * HALF:(x + 1) * HALF], y[g, x][:, t - 1:t + 1, :])
 
-        def round_y(y, on_vector, tag=""):
-            if tag:
-                y_bf = held(tag, [P, HALF * PACK], BF16)
-            else:
-                y_bf = ring.tile([P, HALF * PACK], BF16, name="y_bf", align_bytes=64)
+        def round_y(g, x, on_gpsimd, on_vector=0, tag="y_bf"):
+            y_bf = held(tag + "_%d%d" % (g, x), [P, HALF * PACK], BF16, tag)
+            if on_gpsimd > 0:
+                nc.gpsimd.tensor_scalar(y_bf[:, :on_gpsimd * PACK].rearrange("p (j t) -> p j t", t=PACK),
+                                        y[g, x][:, :, :on_gpsimd].rearrange("p t j -> p j t"), 1.0, -0.0, MULT, ADD)
             dst = y_bf[:].rearrange("p (c i t) -> p c t i", i=2, t=PACK)
-            src = y[:].rearrange("p t (c i) -> p c t i", i=2)
-            split = HALF // 2 - on_vector // 2
-            if split > 0:
-                nc.scalar.copy(dst[:, :split], src[:, :split])
+            src = y[g, x][:].rearrange("p t (c i) -> p c t i", i=2)
+            first, split = on_gpsimd // 2, HALF // 2 - on_vector // 2
+            if split > first:
+                nc.scalar.copy(dst[:, first:split], src[:, first:split])
             if on_vector > 0:
                 nc.vector.tensor_copy(dst[:, split:], src[:, split:])
             return y_bf
@@ -227,64 +242,71 @@ def tile_list_cubic_recall_weights_kernel(
                 (nc.scalar if q % 2 else nc.sync).dma_start(
                     out_2[1:GROUPS, 4 * q:4 * q + 4, :].bitcast(I32), y_s12[32 * q:32 * q + 8, :].bitcast(I32))
 
+        deal_wp_words()
         gather_v_scales()
         tab2_w = held("tab2_w", [P, T2], U32, "tab_s")
         load_words(tab2_w, tab2_words[0])
-        gather_v(0)
-        deal_wp()
-        gather_v(1)
-        gather_v2_scales(0, "tab_w1")
-        deal_v2_scales(0)
+        gather_v(0, (0, 1))
+        deal_wp_scales()
         p_banks = [new_bank(TILES + u) for u in range(TILES)]
         a_banks = [new_bank(u) for u in range(TILES)]
         for u in range(TILES):
             p_pass(p_banks[u], 0, 0, u)
+        gather_v2_scales(0, 2, "tab_w0")
         round_wg(0)
         quantize_wg(0)
         for u in range(TILES):
             a_pass(a_banks[u], 0, 0, u)
-        gather_v2_scales(1, "wg_bf0")
-        deal_v2_scales(1)
-        for u in range(TILES):
-            p_pass(p_banks[u], 1, 0, u)
+        gather_v(1, (0,))
         round_wg(1)
         quantize_wg(1)
-        gather_v2_scales(2, "wg_bf1")
-        deal_v2_scales(2)
+        gather_v(1, (1,), "wg_bf1")
+        gather_v2_scales(2, 3, "tab_w1")
         for u in range(TILES):
+            p_pass(p_banks[u], 1, 0, u)
+            p_sb = woven("p_sb%d" % u, p_banks[u], ACT.Copy)
             a_pass(a_banks[u], 1, 0, u)
-            gate(p_banks[u], a_banks[u], 0, u)
-        gather_v2_words(0, "sig_hold2")
+            sig = woven("sig%d" % u, a_banks[u], ACT.Sigmoid)
+            nc.gpsimd.tensor_tensor(h_bf[0][:, u * JT * PACK:(u + 1) * JT * PACK], p_sb[:], sig[:], MULT)
+        gather_v2_words(0)
+        pairs = []
+        for u in range(TILES):
+            pairs.append((new_bank(u), new_bank(TILES + u)))
+            for a in range(PASSES):
+                h_pass(pairs[u], a, 1, u)
+        gate(pairs[0][1], pairs[0][0], 1, 0)
+        gate(pairs[1][1], pairs[1][0], 1, 1)
+        gather_v2_words(1)
+        deal_v2_words(0, "p_sb3")
+        deal_v2_scales(0, "sig3")
         quantize_h(0)
-        deal_v2_words(0)
+        gate(pairs[2][1], pairs[2][0], 1, 2)
+        gate(pairs[3][1], pairs[3][0], 1, 3)
 
-        inner, outer = (3, 7, 2, 6), (1, 5, 0, 4)
-        h_tile(1, 0, 0)
-        h_tile(1, 1, 1)
-        y00 = cube(0, 0, (2, 6, 3, 7), False)
-        h_tile(1, 2, 0)
-        gather_v2_words(1, "sq_hold0")
-        deal_v2_words(1)
-        gather_v2_words(2, "sq_hold0")
-        deal_v2_words(2)
-        h_tile(1, 3, 2)
+        outer, inner = (0, 4, 1, 5), (2, 6, 3, 7)
+        cube(0, 0, outer)
         quantize_h(1)
-        b00 = round_y(y00, 0)
+        deal_v2_words(1, "sq_hold002")
+        deal_v2_scales(1, "sq_hold001")
+        b00 = round_y(0, 0, 384)
+        cube(0, 1, inner)
         quantize_y(b00, 0, 0)
-        y10 = cube(1, 0, outer, False)
-        y01 = cube(0, 1, inner, False)
-        b10 = round_y(y10, 256)
-        quantize_y(b10, 1, 0)
-        y11 = cube(1, 1, outer, False)
-        b01 = round_y(y01, 256)
+        b01 = round_y(0, 1, 512)
+        cube(1, 0, outer)
+        gather_v2_words(2, "sq_hold102")
+        deal_v2_scales(2, "sq_hold101")
+        deal_v2_words(2)
         quantize_y(b01, 0, 1)
         store_first_scales()
-        y20 = cube(2, 0, inner, False)
-        y21 = cube(2, 1, outer, True)
-        b11 = round_y(y11, 0)
-        b20 = round_y(y20, 512)
-        quantize_y(b20, 2, 0)
+        b10 = round_y(1, 0, 384)
+        cube(1, 1, inner)
+        quantize_y(b10, 1, 0)
+        b11 = round_y(1, 1, 384)
+        cube(2, 0, outer)
         quantize_y(b11, 1, 1)
-        b21 = round_y(y21, 256)
+        b20 = round_y(2, 0, 384)
+        cube(2, 1, inner)
+        quantize_y(b20, 2, 0)
+        b21 = round_y(2, 1, 0, 256, "y_last")
         quantize_y(b21, 2, 1)
         store_last_scales()

@@ -49,9 +49,9 @@ def tile_list_cubic_recall_weights_kernel(
         tab_s = held("tab_s", [P, T], U8)
         tab2_s = held("tab2_s", [P, T2], U8)
         wp_raw = held("wp_raw", [P, PASSES, 2 * H], U8)
-        wp_raw_s = held("wp_raw_s", [P, PASSES, H], U8)
+        wp_raw_s = held("wp_raw_s", [P, H], U8)
         wp_w = held("wp_w", [P, PASSES, 2 * H], U8)
-        wp_s = held("wp_s", [P, PASSES, H], U8)
+        wp_s = [held("wp_s%d" % a, [P, H], U8) for a in range(PASSES)]
         wg_raw = [[] for a in range(PASSES)]
         wg_bf = [held("wg_bf%d" % a, [P, H * PACK], BF16) for a in range(PASSES)]
         wg_w = [held("wg_w%d" % a, [P, H], U32) for a in range(PASSES)]
@@ -66,15 +66,14 @@ def tile_list_cubic_recall_weights_kernel(
         v2_w = [None] * GROUPS
         v2_s = [None] * GROUPS
         h_bf = [held("h_bf%d" % x, [P, HALF * PACK], BF16) for x in range(HALVES)]
-        h_w = [held("h_w%d" % x, [P, HALF], U32) for x in range(HALVES)]
+        h_w = [None] * HALVES
         h_s = [held("h_s%d" % x, [P, HALF], U8) for x in range(HALVES)]
         y_s0 = held("y_s0", [P, S], U8)
         y_s12 = held("y_s12", [P, S], U8)
         y_s = [y_s0[:], y_s12[:], y_s12[4:P, :]]
 
-        for tile in (tab_s, wp_raw_s, tab2_s, v_s1, v2_ms):
-            flat = tile[:] if len(tile.shape) == 2 else tile[:].rearrange("p a c -> p (a c)")
-            nc.vector.memset(flat.bitcast(I32), 0)
+        for tile in (tab_s, wp_raw_s, tab2_s, v_s1, v2_ms, wp_s[1]):
+            nc.vector.memset(tile[:].bitcast(I32), 0)
 
         def load_words(tile, words):
             nc.sync.dma_start(tile[:].bitcast(I32), words.rearrange("p t i -> p (t i)").bitcast(I32))
@@ -91,9 +90,8 @@ def tile_list_cubic_recall_weights_kernel(
         for q in (0, 2, 1, 3):
             nc.sync.dma_start(tab_s[32 * q:32 * q + 8, :].bitcast(I32), tab_scales[:, 4 * q:4 * q + 4, :].bitcast(I32))
         load_words(tab_w[0], tab_words[0])
-        for r in range(4):
-            nc.sync.dma_start(wp_raw_s[r:P:32, :, :].bitcast(I32),
-                              wp_scales.rearrange("a (q r) c -> r q a c", r=4)[r].bitcast(I32))
+        for q in (0, 2, 1, 3):
+            nc.sync.dma_start(wp_raw_s[32 * q:32 * q + 8, :].bitcast(I32), wp_scales[:, 4 * q:4 * q + 4, :].bitcast(I32))
         load_wg(0, 0, H)
         nc.sync.dma_start(tab2_s[0:16, :].bitcast(I32), tab2_scales[0].bitcast(I32))
         load_wg(1, 0, H // 2)
@@ -105,8 +103,9 @@ def tile_list_cubic_recall_weights_kernel(
                                   wp_raw[:].bitcast(U16).rearrange("p a (m t) -> p a t m", t=PACK))
 
         def deal_wp_scales():
-            nc.vector.tensor_copy(wp_s[:].rearrange("p a (t m) -> p a t m", t=PACK),
-                                  wp_raw_s[:].rearrange("p a (m t) -> p a t m", t=PACK))
+            nc.vector.tensor_copy(wp_s[0][:].rearrange("p (t m) -> p t m", t=PACK),
+                                  wp_raw_s[:].rearrange("p (m t) -> p t m", t=PACK))
+            nc.sync.dma_start(wp_s[1][0:100, :].bitcast(I32), wp_s[0][4:104, :].bitcast(I32))
 
         def gather_v_scales():
             nc.vector.tensor_copy(v_s0[:], tab_s[:].indirect(offs_t[:]))
@@ -136,27 +135,31 @@ def tile_list_cubic_recall_weights_kernel(
                 nc.sync.dma_start(v2_ms[32 * q + 8:32 * q + 12, g0 * KP:g1 * KP].bitcast(I32),
                                   tile[4 * q:4 * q + 4, :].bitcast(I32))
 
-        def gather_v2_words(g, tag=""):
+        def gather_v2_words(g0, g1, tag=""):
             cols = KP // PER_COL
-            v2_gw[g] = held("v2_gw%d" % g, [P, KP], U32, tag)
-            nc.vector.tensor_copy(v2_gw[g][:], tab2_w[:].indirect(offs2_t[:, g * cols:(g + 1) * cols]))
+            v2_gw[g0] = held("v2_gw%d" % g0, [P, (g1 - g0) * KP], U32, tag)
+            nc.vector.tensor_copy(v2_gw[g0][:], tab2_w[:].indirect(offs2_t[:, g0 * cols:g1 * cols]))
 
-        def deal_v2_scales(g, tag=""):
-            v2_s[g] = held("v2_s%d" % g, [P, KP], U8, tag)
-            nc.vector.tensor_copy(v2_s[g][:].rearrange("p (t m) -> p t m", t=PACK),
-                                  v2_ms[:, g * KP:(g + 1) * KP].rearrange("p (m t) -> p t m", t=PACK))
+        def deal_v2_scales(g0, g1, tag):
+            tile = held("v2_s%d" % g0, [P, (g1 - g0) * KP], U8, tag)
+            nc.vector.tensor_copy(tile[:].rearrange("p (g t m) -> p g t m", t=PACK, m=P),
+                                  v2_ms[:, g0 * KP:g1 * KP].rearrange("p (g m t) -> p g t m", t=PACK, m=P))
+            for g in range(g0, g1):
+                v2_s[g] = tile[:, (g - g0) * KP:(g - g0 + 1) * KP]
 
-        def deal_v2_words(g, tag=""):
-            v2_w[g] = held("v2_w%d" % g, [P, KP], U32, tag)
-            nc.vector.tensor_copy(v2_w[g][:].rearrange("p (u e m) -> p u m e", u=2, e=2),
-                                  v2_gw[g][:].rearrange("p (m u e) -> p u m e", u=2, e=2))
+        def deal_v2_words(g0, g1, tag):
+            tile = held("v2_w%d" % g0, [P, (g1 - g0) * KP], U32, tag)
+            nc.vector.tensor_copy(tile[:].rearrange("p (g u e m) -> p g u m e", u=2, e=2, m=P),
+                                  v2_gw[g0][:].rearrange("p (g m u e) -> p g u m e", u=2, e=2, m=P))
+            for g in range(g0, g1):
+                v2_w[g] = tile[:, (g - g0) * KP:(g - g0 + 1) * KP]
 
         def p_pass(bank, a, x, u):
             sj = slice(x * HALF + u * JT, x * HALF + (u + 1) * JT)
             for t in range(PACK):
                 nc.tensor.matmul_mx(
                     out=bank[:, t, :],
-                    lhsT=wp_w[:, a, 2 * P * t:2 * P * (t + 1)].bitcast(FP4X4), lhsT_scale=wp_s[:, a, P * t:P * (t + 1)],
+                    lhsT=wp_w[:, a, 2 * P * t:2 * P * (t + 1)].bitcast(FP4X4), lhsT_scale=wp_s[a][:, P * t:P * (t + 1)],
                     rhs=v_w[a, x][:, u * JT:(u + 1) * JT].bitcast(FP8X4), rhs_scale=v_s[a][:, sj],
                     start=(a == 0 and t == 0), stop=(a == PASSES - 1 and t == PACK - 1))
 
@@ -181,7 +184,8 @@ def tile_list_cubic_recall_weights_kernel(
             nc.scalar.activation(tile[:].rearrange("p (j t) -> p j t", t=PACK), bank[:].rearrange("p t j -> p j t"), func)
             return tile
 
-        def quantize_h(x):
+        def quantize_h(x, tag=""):
+            h_w[x] = held("h_w%d" % x, [P, HALF], U32, tag)
             nc.vector.quantize_mx(out=h_w[x][:].bitcast(FP8X4), scales=h_s[x][:], in_=h_bf[x][:])
 
         def new_bank(b):
@@ -204,7 +208,7 @@ def tile_list_cubic_recall_weights_kernel(
                 nc.tensor.matmul_mx(
                     out=m, lhsT=v2_w[g][:, P * t:P * (t + 1)].bitcast(FP8X4), lhsT_scale=v2_s[g][8:P, P * t:P * (t + 1)],
                     rhs=h_w[x][:].bitcast(FP8X4), rhs_scale=h_s[x][:], start=True, stop=True)
-                if x == 0 and g < 2 and t in (1, 2):
+                if (g, x) == (0, 0) and t in (1, 2):
                     sq = held("sq_hold%d%d%d" % (g, x, t), [P, HALF], F32)
                 else:
                     sq = ring.tile([P, HALF], F32, name="sq", bufs=8)
@@ -244,10 +248,10 @@ def tile_list_cubic_recall_weights_kernel(
 
         deal_wp_words()
         gather_v_scales()
-        tab2_w = held("tab2_w", [P, T2], U32, "tab_s")
-        load_words(tab2_w, tab2_words[0])
         gather_v(0, (0, 1))
         deal_wp_scales()
+        tab2_w = held("tab2_w", [P, T2], U32, "tab_s")
+        load_words(tab2_w, tab2_words[0])
         p_banks = [new_bank(TILES + u) for u in range(TILES)]
         a_banks = [new_bank(u) for u in range(TILES)]
         for u in range(TILES):
@@ -268,7 +272,7 @@ def tile_list_cubic_recall_weights_kernel(
             a_pass(a_banks[u], 1, 0, u)
             sig = woven("sig%d" % u, a_banks[u], ACT.Sigmoid)
             nc.gpsimd.tensor_tensor(h_bf[0][:, u * JT * PACK:(u + 1) * JT * PACK], p_sb[:], sig[:], MULT)
-        gather_v2_words(0)
+        gather_v2_words(0, 1)
         pairs = []
         for u in range(TILES):
             pairs.append((new_bank(u), new_bank(TILES + u)))
@@ -276,9 +280,9 @@ def tile_list_cubic_recall_weights_kernel(
                 h_pass(pairs[u], a, 1, u)
         gate(pairs[0][1], pairs[0][0], 1, 0)
         gate(pairs[1][1], pairs[1][0], 1, 1)
-        gather_v2_words(1)
-        deal_v2_words(0, "p_sb3")
-        deal_v2_scales(0, "sig3")
+        gather_v2_words(1, 3, "y_bf")
+        deal_v2_words(0, 1, "p_sb3")
+        deal_v2_scales(0, 1, "sig3")
         quantize_h(0)
         gate(pairs[2][1], pairs[2][0], 1, 2)
         gate(pairs[3][1], pairs[3][0], 1, 3)
@@ -286,16 +290,13 @@ def tile_list_cubic_recall_weights_kernel(
         outer, inner = (0, 4, 1, 5), (2, 6, 3, 7)
         cube(0, 0, outer)
         quantize_h(1)
-        deal_v2_words(1, "sq_hold002")
-        deal_v2_scales(1, "sq_hold001")
+        deal_v2_scales(1, 3, "sq_hold001")
+        deal_v2_words(1, 3, "sq_hold002")
         b00 = round_y(0, 0, 384)
         cube(0, 1, inner)
         quantize_y(b00, 0, 0)
-        b01 = round_y(0, 1, 512)
+        b01 = round_y(0, 1, 384)
         cube(1, 0, outer)
-        gather_v2_words(2, "sq_hold102")
-        deal_v2_scales(2, "sq_hold101")
-        deal_v2_words(2)
         quantize_y(b01, 0, 1)
         store_first_scales()
         b10 = round_y(1, 0, 384)

@@ -56,12 +56,10 @@ def tile_list_cubic_recall_weights_kernel(
         wg_bf = [held("wg_bf%d" % a, [P, H * PACK], BF16) for a in range(PASSES)]
         wg_w = [held("wg_w%d" % a, [P, H], U32) for a in range(PASSES)]
         wg_s = [held("wg_s%d" % a, [P, H], U8) for a in range(PASSES)]
-        strength_t = held("strength_t", [P, GROUPS, PACK], F32)
         v_w = {}
         v_s0 = held("v_s0", [P, S], U8)
         v_s1 = held("v_s1", [P, S], U8)
         v_s = [v_s0, v_s1]
-        v2_gw = {}
         v2_ms = held("v2_ms", [P, S2], U8)
         v2_w = [None] * GROUPS
         v2_s = [None] * GROUPS
@@ -85,8 +83,8 @@ def tile_list_cubic_recall_weights_kernel(
 
         nc.sync.dma_start(offs_t[:], offs)
         nc.sync.dma_start(offs2_t[:], offs2)
-        nc.sync.dma_start(wp_raw[:].bitcast(I32), wp_words.rearrange("a p c -> p a c").bitcast(I32))
-        nc.sync.dma_start(strength_t[:], strength.rearrange("(g p t) -> p g t", p=P, t=PACK))
+        for a in range(PASSES):
+            nc.sync.dma_start(wp_raw[:, a, :].bitcast(I32), wp_words[a].bitcast(I32))
         for q in (0, 2, 1, 3):
             nc.sync.dma_start(tab_s[32 * q:32 * q + 8, :].bitcast(I32), tab_scales[:, 4 * q:4 * q + 4, :].bitcast(I32))
         load_words(tab_w[0], tab_words[0])
@@ -135,10 +133,13 @@ def tile_list_cubic_recall_weights_kernel(
                 nc.sync.dma_start(v2_ms[32 * q + 8:32 * q + 12, g0 * KP:g1 * KP].bitcast(I32),
                                   tile[4 * q:4 * q + 4, :].bitcast(I32))
 
-        def gather_v2_words(g0, g1, tag=""):
+        def gather_v2_words(g0, g1):
             cols = KP // PER_COL
-            v2_gw[g0] = held("v2_gw%d" % g0, [P, (g1 - g0) * KP], U32, tag)
-            nc.vector.tensor_copy(v2_gw[g0][:], tab2_w[:].indirect(offs2_t[:, g0 * cols:g1 * cols]))
+            tile = held("v2_w%d" % g0, [P, (g1 - g0) * KP], U32)
+            nc.vector.tensor_copy(tile[:].rearrange("p (g t m) -> p g m t", t=PACK, m=P),
+                                  tab2_w[:].indirect(offs2_t[:, g0 * cols:g1 * cols]))
+            for g in range(g0, g1):
+                v2_w[g] = tile[:, (g - g0) * KP:(g - g0 + 1) * KP]
 
         def deal_v2_scales(g0, g1, tag):
             tile = held("v2_s%d" % g0, [P, (g1 - g0) * KP], U8, tag)
@@ -146,13 +147,6 @@ def tile_list_cubic_recall_weights_kernel(
                                   v2_ms[:, g0 * KP:g1 * KP].rearrange("p (g m t) -> p g t m", t=PACK, m=P))
             for g in range(g0, g1):
                 v2_s[g] = tile[:, (g - g0) * KP:(g - g0 + 1) * KP]
-
-        def deal_v2_words(g0, g1, tag):
-            tile = held("v2_w%d" % g0, [P, (g1 - g0) * KP], U32, tag)
-            nc.vector.tensor_copy(tile[:].rearrange("p (g u e m) -> p g u m e", u=2, e=2, m=P),
-                                  v2_gw[g0][:].rearrange("p (g m u e) -> p g u m e", u=2, e=2, m=P))
-            for g in range(g0, g1):
-                v2_w[g] = tile[:, (g - g0) * KP:(g - g0 + 1) * KP]
 
         def p_pass(bank, a, x, u):
             sj = slice(x * HALF + u * JT, x * HALF + (u + 1) * JT)
@@ -208,8 +202,8 @@ def tile_list_cubic_recall_weights_kernel(
                 nc.tensor.matmul_mx(
                     out=m, lhsT=v2_w[g][:, P * t:P * (t + 1)].bitcast(FP8X4), lhsT_scale=v2_s[g][8:P, P * t:P * (t + 1)],
                     rhs=h_w[x][:].bitcast(FP8X4), rhs_scale=h_s[x][:], start=True, stop=True)
-                if (g, x) == (0, 0) and t in (1, 2):
-                    sq = held("sq_hold%d%d%d" % (g, x, t), [P, HALF], F32)
+                if t == PACK - 2:
+                    sq = held("sq_hold%d%d" % (g, x), [P, HALF], F32)
                 else:
                     sq = ring.tile([P, HALF], F32, name="sq", bufs=8)
                 nc.scalar.activation(sq[:], m, ACT.Square)
@@ -217,8 +211,8 @@ def tile_list_cubic_recall_weights_kernel(
                 if t % 2:
                     nc.sync.dma_start(y_rows[g, :, t - 1:t + 1, x * HALF:(x + 1) * HALF], y[g, x][:, t - 1:t + 1, :])
 
-        def round_y(g, x, on_gpsimd, on_vector=0, tag="y_bf"):
-            y_bf = held(tag + "_%d%d" % (g, x), [P, HALF * PACK], BF16, tag)
+        def round_y(g, x, on_gpsimd, on_vector=0):
+            y_bf = held("y_bf%d%d" % (g, x), [P, HALF * PACK], BF16)
             if on_gpsimd > 0:
                 nc.gpsimd.tensor_scalar(y_bf[:, :on_gpsimd * PACK].rearrange("p (j t) -> p j t", t=PACK),
                                         y[g, x][:, :, :on_gpsimd].rearrange("p t j -> p j t"), 1.0, -0.0, MULT, ADD)
@@ -231,8 +225,8 @@ def tile_list_cubic_recall_weights_kernel(
                 nc.vector.tensor_copy(dst[:, split:], src[:, split:])
             return y_bf
 
-        def quantize_y(y_bf, g, x):
-            y_w = ring.tile([P, HALF], U32, name="y_w", align_bytes=64)
+        def quantize_y(y_bf, g, x, tag=""):
+            y_w = held("y_w%d%d" % (g, x), [P, HALF], U32, tag)
             nc.vector.quantize_mx(out=y_w[:].bitcast(FP8X4), scales=y_s[g][:, x * HALF:(x + 1) * HALF], in_=y_bf[:])
             words = out_1[g].rearrange("p m t -> p (m t)").bitcast(I32)
             nc.sync.dma_start(words[:, x * HALF:(x + 1) * HALF], y_w[:].bitcast(I32))
@@ -252,6 +246,8 @@ def tile_list_cubic_recall_weights_kernel(
         deal_wp_scales()
         tab2_w = held("tab2_w", [P, T2], U32, "tab_s")
         load_words(tab2_w, tab2_words[0])
+        strength_t = held("strength_t", [P, GROUPS, PACK], F32, "wp_raw_s")
+        nc.sync.dma_start(strength_t[:], strength.rearrange("(g p t) -> p g t", p=P, t=PACK))
         p_banks = [new_bank(TILES + u) for u in range(TILES)]
         a_banks = [new_bank(u) for u in range(TILES)]
         for u in range(TILES):
@@ -280,34 +276,26 @@ def tile_list_cubic_recall_weights_kernel(
                 h_pass(pairs[u], a, 1, u)
         gate(pairs[0][1], pairs[0][0], 1, 0)
         gate(pairs[1][1], pairs[1][0], 1, 1)
-        gather_v2_words(1, 3, "y_bf")
-        deal_v2_words(0, 1, "p_sb3")
+        gather_v2_words(1, 3)
         deal_v2_scales(0, 1, "sig3")
         quantize_h(0)
         gate(pairs[2][1], pairs[2][0], 1, 2)
         gate(pairs[3][1], pairs[3][0], 1, 3)
 
         outer, inner = (0, 4, 1, 5), (2, 6, 3, 7)
-        cube(0, 0, outer)
+        units = [(g, x) for g in range(GROUPS) for x in range(HALVES)]
         quantize_h(1)
-        deal_v2_scales(1, 3, "sq_hold001")
-        deal_v2_words(1, 3, "sq_hold002")
-        b00 = round_y(0, 0, 384)
-        cube(0, 1, inner)
-        quantize_y(b00, 0, 0)
-        b01 = round_y(0, 1, 384)
-        cube(1, 0, outer)
-        quantize_y(b01, 0, 1)
-        store_first_scales()
-        b10 = round_y(1, 0, 384)
-        cube(1, 1, inner)
-        quantize_y(b10, 1, 0)
-        b11 = round_y(1, 1, 384)
-        cube(2, 0, outer)
-        quantize_y(b11, 1, 1)
-        b20 = round_y(2, 0, 384)
-        cube(2, 1, inner)
-        quantize_y(b20, 2, 0)
-        b21 = round_y(2, 1, 0, 256, "y_last")
-        quantize_y(b21, 2, 1)
+        y_bf = []
+        for n, (g, x) in enumerate(units):
+            cube(g, x, inner if n % 2 else outer)
+            if n == 0:
+                deal_v2_scales(1, GROUPS, "sq_hold00")
+            if n >= 2:
+                quantize_y(y_bf[n - 2], *units[n - 2], "sq_hold%d%d" % (g, x))
+            if n == 3:
+                store_first_scales()
+            if n < len(units) - 1:
+                y_bf.append(round_y(g, x, 384))
+        quantize_y(y_bf[-1], *units[-2])
+        quantize_y(round_y(*units[-1], 0, 160), *units[-1])
         store_last_scales()

@@ -119,8 +119,14 @@ def tile_list_cubic_recall_weights_kernel(
         def round_wg(a):
             dst = wg_bf[a][:].rearrange("p (u e m j) -> p u m j e", u=2, e=2, j=PACK)
             for tile, c0, c1 in wg_raw[a]:
-                nc.scalar.copy(dst[:, :, c0 // PACK:c1 // PACK],
-                               tile[:].rearrange("p j (m u e) -> p u m j e", u=2, e=2))
+                src = tile[:].rearrange("p j (m u e) -> p u m j e", u=2, e=2)
+                m0, m1 = c0 // PACK, c1 // PACK
+                if c0 > 0:
+                    mid = (m1 - m0) // 2
+                    nc.scalar.copy(dst[:, :, m0:m0 + mid], src[:, :, :mid])
+                    nc.vector.tensor_copy(dst[:, :, m0 + mid:m1], src[:, :, mid:])
+                else:
+                    nc.scalar.copy(dst[:, :, m0:m1], src)
 
         def quantize_wg(a):
             nc.vector.quantize_mx(out=wg_w[a][:].bitcast(FP8X4), scales=wg_s[a][:], in_=wg_bf[a][:])
@@ -133,9 +139,9 @@ def tile_list_cubic_recall_weights_kernel(
                 nc.sync.dma_start(v2_ms[32 * q + 8:32 * q + 12, g0 * KP:g1 * KP].bitcast(I32),
                                   tile[4 * q:4 * q + 4, :].bitcast(I32))
 
-        def gather_v2_words(g0, g1):
+        def gather_v2_words(g0, g1, tag=""):
             cols = KP // PER_COL
-            tile = held("v2_w%d" % g0, [P, (g1 - g0) * KP], U32)
+            tile = held("v2_w%d" % g0, [P, (g1 - g0) * KP], U32, tag)
             nc.vector.tensor_copy(tile[:].rearrange("p (g t m) -> p g m t", t=PACK, m=P),
                                   tab2_w[:].indirect(offs2_t[:, g0 * cols:g1 * cols]))
             for g in range(g0, g1):
@@ -208,7 +214,9 @@ def tile_list_cubic_recall_weights_kernel(
                     sq = ring.tile([P, HALF], F32, name="sq", bufs=8)
                 nc.scalar.activation(sq[:], m, ACT.Square)
                 nc.vector.scalar_tensor_tensor(y[g, x][:, t, :], m, strength_t[:, g, t:t + 1], sq[:], MULT, MULT)
-                if t % 2:
+                if (g, x) == (0, 0):
+                    nc.sync.dma_start(y_rows[g, :, t, x * HALF:(x + 1) * HALF], y[g, x][:, t, :])
+                elif t % 2:
                     nc.sync.dma_start(y_rows[g, :, t - 1:t + 1, x * HALF:(x + 1) * HALF], y[g, x][:, t - 1:t + 1, :])
 
         def round_y(g, x, on_gpsimd, on_vector=0):
@@ -225,11 +233,12 @@ def tile_list_cubic_recall_weights_kernel(
                 nc.vector.tensor_copy(dst[:, split:], src[:, split:])
             return y_bf
 
-        def quantize_y(y_bf, g, x, tag=""):
-            y_w = held("y_w%d%d" % (g, x), [P, HALF], U32, tag)
-            nc.vector.quantize_mx(out=y_w[:].bitcast(FP8X4), scales=y_s[g][:, x * HALF:(x + 1) * HALF], in_=y_bf[:])
+        def quantize_y(y_bf, g, x, y_w):
+            nc.vector.quantize_mx(out=y_w.bitcast(FP8X4), scales=y_s[g][:, x * HALF:(x + 1) * HALF], in_=y_bf[:])
+
+        def store_words(g, first, y_w):
             words = out_1[g].rearrange("p m t -> p (m t)").bitcast(I32)
-            nc.sync.dma_start(words[:, x * HALF:(x + 1) * HALF], y_w[:].bitcast(I32))
+            nc.sync.dma_start(words[:, first:first + y_w.shape[1]], y_w[:].bitcast(I32))
 
         def store_first_scales():
             for q in range(QUADS):
@@ -291,11 +300,15 @@ def tile_list_cubic_recall_weights_kernel(
             if n == 0:
                 deal_v2_scales(1, GROUPS, "sq_hold00")
             if n >= 2:
-                quantize_y(y_bf[n - 2], *units[n - 2], "sq_hold%d%d" % (g, x))
+                y_w = held("y_w%d" % n, [P, HALF], U32, "sq_hold%d%d" % (g, x))
+                quantize_y(y_bf[n - 2], *units[n - 2], y_w[:])
+                store_words(units[n - 2][0], units[n - 2][1] * HALF, y_w)
             if n == 3:
                 store_first_scales()
             if n < len(units) - 1:
-                y_bf.append(round_y(g, x, 384))
-        quantize_y(y_bf[-1], *units[-2])
-        quantize_y(round_y(*units[-1], 0, 160), *units[-1])
+                y_bf.append(round_y(g, x, 400))
+        y_w = held("y_w_last", [P, S], U32)
+        quantize_y(y_bf[-1], *units[-2], y_w[:, :HALF])
+        quantize_y(round_y(*units[-1], 0, 160), *units[-1], y_w[:, HALF:])
+        store_words(GROUPS - 1, 0, y_w)
         store_last_scales()

@@ -28,6 +28,7 @@ TILES = HALF // JT
 GROUPS = S2 // KP
 QUADS = 4
 PER_COL = 16
+ON_GPSIMD = 432
 
 
 def tile_list_cubic_recall_weights_kernel(
@@ -197,44 +198,45 @@ def tile_list_cubic_recall_weights_kernel(
 
         y_rows = out_0.rearrange("(g p t) j -> g p t j", p=P, t=PACK)
 
-        y = {}
+        units = [(g, x) for g in range(GROUPS) for x in range(HALVES)]
+        y = {unit: held("y%d%d" % unit, [P, PACK, HALF], F32) for unit in units[:-1]}
+        y_bf = {unit: held("y_bf%d%d" % unit, [P, HALF * PACK], BF16) for unit in units}
 
-        def cube(g, x, banks, slices=range(PACK)):
-            if (g, x) not in y:
-                y.setdefault((g, x), ring.tile([P, PACK, HALF], F32, name="y", bufs=6))
-            for t in slices:
-                bank = new_bank(banks[t])
-                m = bank[:].rearrange("p t j -> p (t j)")
-                nc.tensor.matmul_mx(
-                    out=m, lhsT=v2_w[g][:, P * t:P * (t + 1)].bitcast(FP8X4), lhsT_scale=v2_s[g][8:P, P * t:P * (t + 1)],
-                    rhs=h_w[x][:].bitcast(FP8X4), rhs_scale=h_s[x][:], start=True, stop=True)
-                if t == PACK - 2:
-                    sq = held("sq_hold%d%d" % (g, x), [P, HALF], F32)
-                else:
-                    sq = ring.tile([P, HALF], F32, name="sq", bufs=8)
-                nc.scalar.activation(sq[:], m, ACT.Square)
-                nc.vector.scalar_tensor_tensor(y[g, x][:, t, :], m, strength_t[:, g, t:t + 1], sq[:], MULT, MULT)
-                if (g, x) == (0, 0):
-                    nc.sync.dma_start(y_rows[g, :, t, x * HALF:(x + 1) * HALF], y[g, x][:, t, :])
-                elif t % 2:
-                    nc.sync.dma_start(y_rows[g, :, t - 1:t + 1, x * HALF:(x + 1) * HALF], y[g, x][:, t - 1:t + 1, :])
+        def square(g, x, t, bank):
+            m = new_bank(bank)[:].rearrange("p t j -> p (t j)")
+            nc.tensor.matmul_mx(
+                out=m, lhsT=v2_w[g][:, P * t:P * (t + 1)].bitcast(FP8X4), lhsT_scale=v2_s[g][8:P, P * t:P * (t + 1)],
+                rhs=h_w[x][:].bitcast(FP8X4), rhs_scale=h_s[x][:], start=True, stop=True)
+            if t == PACK - 2:
+                sq = held("sq_hold%d%d" % (g, x), [P, HALF], F32)
+            else:
+                sq = ring.tile([P, HALF], F32, name="sq", bufs=8)
+            nc.scalar.activation(sq[:], m, ACT.Square)
+            return m, sq
 
-        def round_y(g, x, on_gpsimd, on_vector=0):
-            y_bf = held("y_bf%d%d" % (g, x), [P, HALF * PACK], BF16)
-            if on_gpsimd > 0:
-                nc.gpsimd.tensor_scalar(y_bf[:, :on_gpsimd * PACK].rearrange("p (j t) -> p j t", t=PACK),
-                                        y[g, x][:, :, :on_gpsimd].rearrange("p t j -> p j t"), 1.0, -0.0, MULT, ADD)
-            dst = y_bf[:].rearrange("p (c i t) -> p c t i", i=2, t=PACK)
-            src = y[g, x][:].rearrange("p t (c i) -> p c t i", i=2)
-            first, split = on_gpsimd // 2, HALF // 2 - on_vector // 2
-            if split > first:
-                nc.scalar.copy(dst[:, first:split], src[:, first:split])
-            if on_vector > 0:
-                nc.vector.tensor_copy(dst[:, split:], src[:, split:])
-            return y_bf
+        def product(out, g, t, m, sq):
+            nc.vector.scalar_tensor_tensor(out, m, strength_t[:, g, t:t + 1], sq, MULT, MULT)
 
-        def quantize_y(y_bf, g, x, y_w):
-            nc.vector.quantize_mx(out=y_w.bitcast(FP8X4), scales=y_s[g][:, x * HALF:(x + 1) * HALF], in_=y_bf[:])
+        def store_y(g, x, t0, t1):
+            nc.sync.dma_start(y_rows[g, :, t0:t1, x * HALF:(x + 1) * HALF], y[g, x][:, t0:t1, :])
+
+        def cube(g, x, banks, per_store):
+            for t in range(PACK):
+                m, sq = square(g, x, t, banks[t])
+                product(y[g, x][:, t, :], g, t, m, sq[:])
+                if (t + 1) % per_store == 0:
+                    store_y(g, x, t + 1 - per_store, t + 1)
+
+        def round_on_gpsimd(g, x, c0, c1):
+            nc.gpsimd.tensor_scalar(y_bf[g, x][:, c0 * PACK:c1 * PACK].rearrange("p (j t) -> p j t", t=PACK),
+                                    y[g, x][:, :, c0:c1].rearrange("p t j -> p j t"), 1.0, -0.0, MULT, ADD)
+
+        def round_on_scalar(g, x, c0, c1, src):
+            nc.scalar.copy(y_bf[g, x][:, c0 * PACK:c1 * PACK].rearrange("p (c i t) -> p c t i", i=2, t=PACK),
+                           src.rearrange("p t (c i) -> p c t i", i=2))
+
+        def quantize_y(g, x, y_w):
+            nc.vector.quantize_mx(out=y_w.bitcast(FP8X4), scales=y_s[g][:, x * HALF:(x + 1) * HALF], in_=y_bf[g, x][:])
 
         def store_words(g, first, y_w):
             words = out_1[g].rearrange("p m t -> p (m t)").bitcast(I32)
@@ -292,23 +294,36 @@ def tile_list_cubic_recall_weights_kernel(
         gate(pairs[3][1], pairs[3][0], 1, 3)
 
         outer, inner = (0, 4, 1, 5), (2, 6, 3, 7)
-        units = [(g, x) for g in range(GROUPS) for x in range(HALVES)]
         quantize_h(1)
-        y_bf = []
-        for n, (g, x) in enumerate(units):
-            cube(g, x, inner if n % 2 else outer)
+
+        def quantize_behind(n):
+            g, x = units[n - 2]
+            y_w = held("y_w%d" % n, [P, HALF], U32, "sq_hold%d%d" % units[n])
+            quantize_y(g, x, y_w[:])
+            store_words(g, x * HALF, y_w)
+
+        for n, (g, x) in enumerate(units[:-1]):
+            cube(g, x, inner if n % 2 else outer, 2 if n else 1)
             if n == 0:
                 deal_v2_scales(1, GROUPS, "sq_hold00")
             if n >= 2:
-                y_w = held("y_w%d" % n, [P, HALF], U32, "sq_hold%d%d" % (g, x))
-                quantize_y(y_bf[n - 2], *units[n - 2], y_w[:])
-                store_words(units[n - 2][0], units[n - 2][1] * HALF, y_w)
+                quantize_behind(n)
             if n == 3:
                 store_first_scales()
-            if n < len(units) - 1:
-                y_bf.append(round_y(g, x, 400))
+            round_on_gpsimd(g, x, 0, ON_GPSIMD)
+            round_on_scalar(g, x, ON_GPSIMD, HALF, y[g, x][:, :, ON_GPSIMD:])
+        g, x = units[-1]
+        squares = [square(g, x, t, inner[t]) for t in range(PACK)]
+        for c0 in (0, HALF // 2):
+            c1 = c0 + HALF // 2
+            part = held("y_part%d" % c0, [P, PACK, HALF // 2], F32)
+            for t, (m, sq) in enumerate(squares):
+                product(part[:, t, :], g, t, m[:, c0:c1], sq[:, c0:c1])
+            nc.sync.dma_start(y_rows[g, :, :, x * HALF + c0:x * HALF + c1], part[:])
+            round_on_scalar(g, x, c0, c1, part[:])
+        quantize_behind(len(units) - 1)
         y_w = held("y_w_last", [P, S], U32)
-        quantize_y(y_bf[-1], *units[-2], y_w[:, :HALF])
-        quantize_y(round_y(*units[-1], 0, 160), *units[-1], y_w[:, HALF:])
+        quantize_y(*units[-2], y_w[:, :HALF])
+        quantize_y(*units[-1], y_w[:, HALF:])
         store_words(GROUPS - 1, 0, y_w)
         store_last_scales()

@@ -28,7 +28,8 @@ TILES = HALF // JT
 GROUPS = S2 // KP
 QUADS = 4
 PER_COL = 16
-ON_GPSIMD = 432
+Y_ON_GPSIMD = (512, 416, 416, 416, 416)
+V2_BASE = 8
 
 
 def tile_list_cubic_recall_weights_kernel(
@@ -38,7 +39,7 @@ def tile_list_cubic_recall_weights_kernel(
     nc = tc.nc
     with ExitStack() as ctx:
         keep = ctx.enter_context(tc.tile_pool(name="keep", bufs=1))
-        ring = ctx.enter_context(tc.tile_pool(name="ring", bufs=3))
+        ring = ctx.enter_context(tc.tile_pool(name="ring", bufs=6))
         psum = ctx.enter_context(tc.psum_pool(name="psum", bufs=1))
 
         def held(name, shape, dtype, tag=""):
@@ -46,122 +47,93 @@ def tile_list_cubic_recall_weights_kernel(
 
         offs_t = keep.tile([P, S // PER_COL], U16, name="offs_t")
         offs2_t = keep.tile([P, S2 // PER_COL], U16, name="offs2_t")
-        tab_w = [held("tab_w%d" % a, [P, T], U32) for a in range(PASSES)]
         tab_s = held("tab_s", [P, T], U8)
         tab2_s = held("tab2_s", [P, T2], U8)
         wp_raw = held("wp_raw", [P, PASSES, 2 * H], U8)
-        wp_raw_s = held("wp_raw_s", [P, H], U8)
+        wp_raw_s = held("wp_raw_s", [P, PASSES, H], U8)
         wp_w = held("wp_w", [P, PASSES, 2 * H], U8)
-        wp_s = [held("wp_s%d" % a, [P, H], U8) for a in range(PASSES)]
-        wg_raw = [[] for a in range(PASSES)]
         wg_bf = [held("wg_bf%d" % a, [P, H * PACK], BF16) for a in range(PASSES)]
         wg_w = [held("wg_w%d" % a, [P, H], U32) for a in range(PASSES)]
         wg_s = [held("wg_s%d" % a, [P, H], U8) for a in range(PASSES)]
         v_w = {}
-        v_s0 = held("v_s0", [P, S], U8)
-        v_s1 = held("v_s1", [P, S], U8)
-        v_s = [v_s0, v_s1]
-        v2_ms = held("v2_ms", [P, S2], U8)
+        v_gs = held("v_gs", [P, S], U8)
+        v_s = held("v_s", [P, PASSES, S], U8)
+        v2_s = held("v2_s", [P, S2], U8)
         v2_w = [None] * GROUPS
-        v2_s = [None] * GROUPS
         h_bf = [held("h_bf%d" % x, [P, HALF * PACK], BF16) for x in range(HALVES)]
         h_w = [None] * HALVES
         h_s = [held("h_s%d" % x, [P, HALF], U8) for x in range(HALVES)]
         y_s0 = held("y_s0", [P, S], U8)
         y_s12 = held("y_s12", [P, S], U8)
         y_s = [y_s0[:], y_s12[:], y_s12[4:P, :]]
+        tab_w = [held("tab_w0", [P, T], U32), None]
+        wg_raw = [held("wg_raw%d" % a, [P, PACK, H], F32) for a in range(PASSES)]
 
-        for tile in (tab_s, wp_raw_s, tab2_s, v_s1, v2_ms, wp_s[1]):
-            nc.vector.memset(tile[:].bitcast(I32), 0)
+        warm = held("warm", [P, 2], F32)
+        nc.gpsimd.memset(wp_raw_s[:].rearrange("p a c -> p (a c)").bitcast(I32), 0)
+        nc.vector.memset(warm[:, 0:1], 0.0)
+        nc.vector.memset(tab2_s[:].bitcast(I32), 0)
+        nc.vector.memset(tab_s[32:64, :].bitcast(I32), 0)
+        nc.gpsimd.memset(tab_s[64:P, :].bitcast(I32), 0)
+        nc.gpsimd.memset(v_s[:].rearrange("p a c -> p (a c)").bitcast(I32), 0)
+        nc.gpsimd.memset(v2_s[:].bitcast(I32), 0)
 
         def load_words(tile, words):
             nc.sync.dma_start(tile[:].bitcast(I32), words.rearrange("p t i -> p (t i)").bitcast(I32))
 
-        def load_wg(a, c0, c1):
-            tile = held("wg_raw%d_%d" % (a, c0), [P, PACK, c1 - c0], F32)
-            wg_raw[a].append((tile, c0, c1))
-            nc.sync.dma_start(tile[:], wg[a * KP:(a + 1) * KP, c0:c1].rearrange("(p j) c -> p j c", j=PACK))
-
         nc.sync.dma_start(offs_t[:], offs)
-        nc.sync.dma_start(offs2_t[:], offs2)
-        for a in range(PASSES):
-            nc.sync.dma_start(wp_raw[:, a, :].bitcast(I32), wp_words[a].bitcast(I32))
-        for q in (0, 2, 1, 3):
-            nc.sync.dma_start(tab_s[32 * q:32 * q + 8, :].bitcast(I32), tab_scales[:, 4 * q:4 * q + 4, :].bitcast(I32))
+        nc.sync.dma_start(tab_s[0:32, :].bitcast(I32), tab_scales.rearrange("a q c -> q a c").bitcast(I32))
+        nc.sync.dma_start(wp_raw[:].bitcast(I32), wp_words.rearrange("a p c -> p a c").bitcast(I32))
+        for q in range(QUADS):
+            nc.sync.dma_start(wp_raw_s[32 * q:32 * q + 4].bitcast(I32),
+                              wp_scales[:, 4 * q:4 * q + 4, :].rearrange("a r c -> r a c").bitcast(I32))
         load_words(tab_w[0], tab_words[0])
-        for q in (0, 2, 1, 3):
-            nc.sync.dma_start(wp_raw_s[32 * q:32 * q + 8, :].bitcast(I32), wp_scales[:, 4 * q:4 * q + 4, :].bitcast(I32))
-        load_wg(0, 0, H)
+        nc.sync.dma_start(offs2_t[:], offs2)
         nc.sync.dma_start(tab2_s[0:16, :].bitcast(I32), tab2_scales[0].bitcast(I32))
-        load_wg(1, 0, H // 2)
-        load_words(tab_w[1], tab_words[1])
-        load_wg(1, H // 2, H)
+        for a in range(PASSES):
+            nc.sync.dma_start(wg_raw[a][:], wg[a * KP:(a + 1) * KP, :].rearrange("(p j) c -> p j c", j=PACK))
+        nc.scalar.activation(warm[:, 1:2], warm[:, 0:1], ACT.Sigmoid)
 
-        def deal_wp_words():
-            nc.vector.tensor_copy(wp_w[:].bitcast(U16).rearrange("p a (t m) -> p a t m", t=PACK),
-                                  wp_raw[:].bitcast(U16).rearrange("p a (m t) -> p a t m", t=PACK))
-
-        def deal_wp_scales():
-            nc.vector.tensor_copy(wp_s[0][:].rearrange("p (t m) -> p t m", t=PACK),
-                                  wp_raw_s[:].rearrange("p (m t) -> p t m", t=PACK))
-            nc.sync.dma_start(wp_s[1][0:100, :].bitcast(I32), wp_s[0][4:104, :].bitcast(I32))
-
-        def gather_v_scales():
-            nc.vector.tensor_copy(v_s0[:], tab_s[:].indirect(offs_t[:]))
-            nc.sync.dma_start(v_s1[0:100, :].bitcast(I32), v_s0[4:104, :].bitcast(I32))
-
-        def gather_v(a, halves, tag=""):
-            cols = HALF // PER_COL
-            tile = held("v_w%d%d" % (a, halves[0]), [P, HALF * len(halves)], U32, tag)
-            nc.vector.tensor_copy(tile[:], tab_w[a][:].indirect(offs_t[:, halves[0] * cols:(halves[-1] + 1) * cols]))
-            for x in halves:
-                v_w[a, x] = tile[:, (x - halves[0]) * HALF:(x - halves[0] + 1) * HALF]
+        def gather_v(a, u0, u1, tag=""):
+            cols = JT // PER_COL
+            tile = held("v_w%d%d" % (a, u0), [P, JT * (u1 - u0)], U32, tag)
+            nc.vector.tensor_copy(tile[:], tab_w[a][:].indirect(offs_t[:, u0 * cols:u1 * cols]))
+            for u in range(u0, u1):
+                v_w[a, u] = tile[:, (u - u0) * JT:(u - u0 + 1) * JT]
 
         def round_wg(a):
-            dst = wg_bf[a][:].rearrange("p (u e m j) -> p u m j e", u=2, e=2, j=PACK)
-            for tile, c0, c1 in wg_raw[a]:
-                src = tile[:].rearrange("p j (m u e) -> p u m j e", u=2, e=2)
-                m0, m1 = c0 // PACK, c1 // PACK
-                if c0 > 0:
-                    mid = (m1 - m0) // 2
-                    nc.scalar.copy(dst[:, :, m0:m0 + mid], src[:, :, :mid])
-                    nc.vector.tensor_copy(dst[:, :, m0 + mid:m1], src[:, :, mid:])
-                else:
-                    nc.scalar.copy(dst[:, :, m0:m1], src)
+            nc.scalar.copy(wg_bf[a][:].rearrange("p (u e m j) -> p u m j e", u=2, e=2, j=PACK),
+                           wg_raw[a][:].rearrange("p j (m u e) -> p u m j e", u=2, e=2))
 
         def quantize_wg(a):
             nc.vector.quantize_mx(out=wg_w[a][:].bitcast(FP8X4), scales=wg_s[a][:], in_=wg_bf[a][:])
 
-        def gather_v2_scales(g0, g1, tag):
+        def gather_v2_words(g, tag=""):
             cols = KP // PER_COL
-            tile = held("v2_gs%d" % g0, [P, (g1 - g0) * KP], U8, tag)
+            v2_w[g] = held("v2_w%d" % g, [P, KP], U32, tag)
+            nc.vector.tensor_copy(v2_w[g][:].rearrange("p (t m) -> p m t", t=PACK),
+                                  tab2_w[:].indirect(offs2_t[:, g * cols:(g + 1) * cols]))
+
+        def gather_v2_scales(tile, g0, g1):
+            cols = KP // PER_COL
             nc.vector.tensor_copy(tile[:], tab2_s[:].indirect(offs2_t[:, g0 * cols:g1 * cols]))
+            return tile
+
+        def deal_v2_scales(gathered, g0, g1, tag=""):
+            dealt = held("v2_ds%d" % g0, [P, (g1 - g0) * KP], U8, tag)
+            nc.vector.tensor_copy(dealt[:].rearrange("p (g t m) -> p t g m", t=PACK, m=P),
+                                  gathered[:].rearrange("p (g m t) -> p t g m", t=PACK, m=P))
             for q in range(QUADS):
-                nc.sync.dma_start(v2_ms[32 * q + 8:32 * q + 12, g0 * KP:g1 * KP].bitcast(I32),
-                                  tile[4 * q:4 * q + 4, :].bitcast(I32))
-
-        def gather_v2_words(g0, g1, tag=""):
-            cols = KP // PER_COL
-            tile = held("v2_w%d" % g0, [P, (g1 - g0) * KP], U32, tag)
-            nc.vector.tensor_copy(tile[:].rearrange("p (g t m) -> p g m t", t=PACK, m=P),
-                                  tab2_w[:].indirect(offs2_t[:, g0 * cols:g1 * cols]))
-            for g in range(g0, g1):
-                v2_w[g] = tile[:, (g - g0) * KP:(g - g0 + 1) * KP]
-
-        def deal_v2_scales(g0, g1, tag):
-            tile = held("v2_s%d" % g0, [P, (g1 - g0) * KP], U8, tag)
-            nc.vector.tensor_copy(tile[:].rearrange("p (g t m) -> p g t m", t=PACK, m=P),
-                                  v2_ms[:, g0 * KP:g1 * KP].rearrange("p (g m t) -> p g t m", t=PACK, m=P))
-            for g in range(g0, g1):
-                v2_s[g] = tile[:, (g - g0) * KP:(g - g0 + 1) * KP]
+                nc.sync.dma_start(v2_s[32 * q + V2_BASE:32 * q + V2_BASE + 4, g0 * KP:g1 * KP].bitcast(I32),
+                                  dealt[4 * q:4 * q + 4, :].bitcast(I32))
 
         def p_pass(bank, a, x, u):
             sj = slice(x * HALF + u * JT, x * HALF + (u + 1) * JT)
             for t in range(PACK):
                 nc.tensor.matmul_mx(
                     out=bank[:, t, :],
-                    lhsT=wp_w[:, a, 2 * P * t:2 * P * (t + 1)].bitcast(FP4X4), lhsT_scale=wp_s[a][:, P * t:P * (t + 1)],
-                    rhs=v_w[a, x][:, u * JT:(u + 1) * JT].bitcast(FP8X4), rhs_scale=v_s[a][:, sj],
+                    lhsT=wp_w[:, a, 2 * P * t:2 * P * (t + 1)].bitcast(FP4X4), lhsT_scale=wp_s[:, a, P * t:P * (t + 1)],
+                    rhs=v_w[a, x * TILES + u].bitcast(FP8X4), rhs_scale=v_s[:, a, sj],
                     start=(a == 0 and t == 0), stop=(a == PASSES - 1 and t == PACK - 1))
 
         def a_pass(bank, a, x, u):
@@ -170,18 +142,17 @@ def tile_list_cubic_recall_weights_kernel(
                 nc.tensor.matmul_mx(
                     out=bank[:, t, :],
                     lhsT=wg_w[a][:, P * t:P * (t + 1)].bitcast(FP8X4), lhsT_scale=wg_s[a][:, P * t:P * (t + 1)],
-                    rhs=v_w[a, x][:, u * JT:(u + 1) * JT].bitcast(FP8X4), rhs_scale=v_s0[4 * a:P, sj],
+                    rhs=v_w[a, x * TILES + u].bitcast(FP8X4), rhs_scale=v_s[:, a, sj],
                     start=(a == 0 and t == 0), stop=(a == PASSES - 1 and t == PACK - 1))
 
-        def gate(p_bank, a_bank, x, u):
-            sig = ring.tile([P, PACK, JT], F32, name="sig")
+        def gate(p_bank, a_bank, x, u, tag=""):
+            sig = held("sig%d%d" % (x, u), [P, PACK, JT], F32, tag)
             nc.scalar.activation(sig[:], a_bank[:], ACT.Sigmoid)
             h_out = h_bf[x][:, u * JT * PACK:(u + 1) * JT * PACK].rearrange("p (c i t) -> p c t i", i=2, t=PACK)
             nc.vector.tensor_tensor(h_out, p_bank[:].rearrange("p t (c i) -> p c t i", i=2),
                                     sig[:].rearrange("p t (c i) -> p c t i", i=2), MULT)
 
-        def woven(name, bank, func):
-            tile = held(name, [P, JT * PACK], F32)
+        def woven(tile, bank, func):
             nc.scalar.activation(tile[:].rearrange("p (j t) -> p j t", t=PACK), bank[:].rearrange("p t j -> p j t"), func)
             return tile
 
@@ -192,25 +163,22 @@ def tile_list_cubic_recall_weights_kernel(
         def new_bank(b):
             return psum.tile([P, PACK, JT], F32, name="bank%d" % b)
 
-        def h_pass(banks, a, x, u):
-            a_pass(banks[0], a, x, u)
-            p_pass(banks[1], a, x, u)
-
         y_rows = out_0.rearrange("(g p t) j -> g p t j", p=P, t=PACK)
 
-        units = [(g, x) for g in range(GROUPS) for x in range(HALVES)]
+        units = [(0, 0), (1, 0), (0, 1), (1, 1), (2, 0), (2, 1)]
         y = {unit: held("y%d%d" % unit, [P, PACK, HALF], F32) for unit in units[:-1]}
         y_bf = {unit: held("y_bf%d%d" % unit, [P, HALF * PACK], BF16) for unit in units}
 
         def square(g, x, t, bank):
             m = new_bank(bank)[:].rearrange("p t j -> p (t j)")
+            cols = slice(g * KP + P * t, g * KP + P * (t + 1))
             nc.tensor.matmul_mx(
-                out=m, lhsT=v2_w[g][:, P * t:P * (t + 1)].bitcast(FP8X4), lhsT_scale=v2_s[g][8:P, P * t:P * (t + 1)],
+                out=m, lhsT=v2_w[g][:, P * t:P * (t + 1)].bitcast(FP8X4), lhsT_scale=v2_s[V2_BASE:P, cols],
                 rhs=h_w[x][:].bitcast(FP8X4), rhs_scale=h_s[x][:], start=True, stop=True)
-            if t == PACK - 2:
-                sq = held("sq_hold%d%d" % (g, x), [P, HALF], F32)
+            if t == PACK - 2 or (g, x) == units[0]:
+                sq = held("sq_hold%d%d%d" % (g, x, t), [P, HALF], F32)
             else:
-                sq = ring.tile([P, HALF], F32, name="sq", bufs=8)
+                sq = ring.tile([P, HALF], F32, name="sq")
             nc.scalar.activation(sq[:], m, ACT.Square)
             return m, sq
 
@@ -220,10 +188,12 @@ def tile_list_cubic_recall_weights_kernel(
         def store_y(g, x, t0, t1):
             nc.sync.dma_start(y_rows[g, :, t0:t1, x * HALF:(x + 1) * HALF], y[g, x][:, t0:t1, :])
 
-        def cube(g, x, banks, per_store):
+        def cube(g, x, banks, per_store, inside=None):
             for t in range(PACK):
                 m, sq = square(g, x, t, banks[t])
                 product(y[g, x][:, t, :], g, t, m, sq[:])
+                if t == 0 and inside is not None:
+                    inside()
                 if (t + 1) % per_store == 0:
                     store_y(g, x, t + 1 - per_store, t + 1)
 
@@ -251,69 +221,93 @@ def tile_list_cubic_recall_weights_kernel(
                 (nc.scalar if q % 2 else nc.sync).dma_start(
                     out_2[1:GROUPS, 4 * q:4 * q + 4, :].bitcast(I32), y_s12[32 * q:32 * q + 8, :].bitcast(I32))
 
-        deal_wp_words()
-        gather_v_scales()
-        gather_v(0, (0, 1))
-        deal_wp_scales()
-        tab2_w = held("tab2_w", [P, T2], U32, "tab_s")
+        nc.vector.tensor_copy(v_gs[:], tab_s[:].indirect(offs_t[:]))
+        for q in range(QUADS):
+            nc.sync.dma_start(v_s[32 * q:32 * q + 4].rearrange("p a c -> p (a c)").bitcast(I32),
+                              v_gs[8 * q:8 * q + 8, :].bitcast(I32))
+        nc.vector.tensor_copy(wp_w[:].bitcast(U16).rearrange("p a (t m) -> p a t m", t=PACK),
+                              wp_raw[:].bitcast(U16).rearrange("p a (m t) -> p a t m", t=PACK))
+        tab_w[1] = held("tab_w1", [P, T], U32, "wp_raw")
+        load_words(tab_w[1], tab_words[1])
+        wp_s = held("wp_s", [P, PASSES, H], U8)
+        for a in range(PASSES):
+            nc.gpsimd.tensor_copy(wp_s[:, a, :].rearrange("p (t m) -> p t m", t=PACK),
+                                  wp_raw_s[:, a, :].rearrange("p (m t) -> p t m", t=PACK))
+        gather_v(0, 0, 2 * TILES)
+        tab2_w = held("tab2_w", [P, T2], U32, "tab_w0")
         load_words(tab2_w, tab2_words[0])
-        strength_t = held("strength_t", [P, GROUPS, PACK], F32, "wp_raw_s")
-        nc.sync.dma_start(strength_t[:], strength.rearrange("(g p t) -> p g t", p=P, t=PACK))
-        p_banks = [new_bank(TILES + u) for u in range(TILES)]
+        v2_gs01 = gather_v2_scales(held("v2_gs", [P, S2], U8), 0, GROUPS)
+
         a_banks = [new_bank(u) for u in range(TILES)]
+        p_banks = [new_bank(TILES + u) for u in range(TILES)]
         for u in range(TILES):
             p_pass(p_banks[u], 0, 0, u)
-        gather_v2_scales(0, 2, "tab_w0")
         round_wg(0)
         quantize_wg(0)
+        strength_t = held("strength_t", [P, GROUPS, PACK], F32, "wg_raw0")
+        nc.sync.dma_start(strength_t[:], strength.rearrange("(g p t) -> p g t", p=P, t=PACK))
+        deal_v2_scales(v2_gs01, 0, GROUPS, "wg_bf0")
         for u in range(TILES):
             a_pass(a_banks[u], 0, 0, u)
-        gather_v(1, (0,))
         round_wg(1)
         quantize_wg(1)
-        gather_v(1, (1,), "wg_bf1")
-        gather_v2_scales(2, 3, "tab_w1")
-        for u in range(TILES):
-            p_pass(p_banks[u], 1, 0, u)
-            p_sb = woven("p_sb%d" % u, p_banks[u], ACT.Copy)
-            a_pass(a_banks[u], 1, 0, u)
-            sig = woven("sig%d" % u, a_banks[u], ACT.Sigmoid)
-            nc.gpsimd.tensor_tensor(h_bf[0][:, u * JT * PACK:(u + 1) * JT * PACK], p_sb[:], sig[:], MULT)
-        gather_v2_words(0, 1)
-        pairs = []
-        for u in range(TILES):
-            pairs.append((new_bank(u), new_bank(TILES + u)))
-            for a in range(PASSES):
-                h_pass(pairs[u], a, 1, u)
-        gate(pairs[0][1], pairs[0][0], 1, 0)
-        gate(pairs[1][1], pairs[1][0], 1, 1)
-        gather_v2_words(1, 3)
-        deal_v2_scales(0, 1, "sig3")
-        quantize_h(0)
-        gate(pairs[2][1], pairs[2][0], 1, 2)
-        gate(pairs[3][1], pairs[3][0], 1, 3)
+        gather_v(1, 0, 2)
+        gather_v(1, 2, TILES)
+        gather_v(1, TILES, 2 * TILES)
 
-        outer, inner = (0, 4, 1, 5), (2, 6, 3, 7)
-        quantize_h(1)
+        def gate_on_gpsimd(p_sb, a_bank, x, u, tag=""):
+            sig = woven(held("sig%d%d" % (x, u), [P, JT * PACK], F32, tag), a_bank, ACT.Sigmoid)
+            nc.gpsimd.tensor_tensor(h_bf[x][:, u * JT * PACK:(u + 1) * JT * PACK], p_sb[:], sig[:], MULT)
+
+        def both_passes(one_pass, bank, u):
+            for a in range(PASSES):
+                one_pass(bank, a, 1, u)
+            return bank
+
+        def late_tile_on_gpsimd(u, banks, tag="", tag2=""):
+            late_p = both_passes(p_pass, new_bank(banks[0]), u)
+            late_a = both_passes(a_pass, new_bank(banks[1]), u)
+            p_sb = woven(held("p_sb1%d" % u, [P, JT * PACK], F32, tag), late_p, ACT.Copy)
+            gate_on_gpsimd(p_sb, late_a, 1, u, tag2)
+
+        for u in range(TILES):
+            a_pass(a_banks[u], 1, 0, u)
+            p_pass(p_banks[u], 1, 0, u)
+            if u < TILES - 1:
+                gate(p_banks[u], a_banks[u], 0, u)
+            else:
+                gate_on_gpsimd(woven(held("p_sb0", [P, JT * PACK], F32), p_banks[u], ACT.Copy), a_banks[u], 0, u)
+        gather_v2_words(0)
+        quantize_h(0)
+        gather_v2_words(1, "h_bf0")
+        late_tile_on_gpsimd(0, (0, 1))
+        late_tile_on_gpsimd(1, (4, 5))
+
+        first, second = (2, 7, 3, 6), (0, 1, 4, 5)
 
         def quantize_behind(n):
             g, x = units[n - 2]
-            y_w = held("y_w%d" % n, [P, HALF], U32, "sq_hold%d%d" % units[n])
+            y_w = held("y_w%d" % n, [P, HALF], U32, "sq_hold%d%d2" % units[n])
             quantize_y(g, x, y_w[:])
             store_words(g, x * HALF, y_w)
 
         for n, (g, x) in enumerate(units[:-1]):
-            cube(g, x, inner if n % 2 else outer, 2 if n else 1)
+            cube(g, x, first if n in (0, 1, 3) else second, 2 if n else 1, (lambda: quantize_h(1)) if n == 1 else None)
             if n == 0:
-                deal_v2_scales(1, GROUPS, "sq_hold00")
+                gather_v2_words(2, "sq_hold002")
+                late_tile_on_gpsimd(2, (0, 1), "sq_hold000", "sq_hold001")
+                late_a, late_p = both_passes(a_pass, new_bank(4), 3), both_passes(p_pass, new_bank(5), 3)
+                gate(late_p, late_a, 1, 3, "sq_hold003")
             if n >= 2:
                 quantize_behind(n)
-            if n == 3:
+            if n == 4:
                 store_first_scales()
-            round_on_gpsimd(g, x, 0, ON_GPSIMD)
-            round_on_scalar(g, x, ON_GPSIMD, HALF, y[g, x][:, :, ON_GPSIMD:])
+            share = Y_ON_GPSIMD[n]
+            round_on_gpsimd(g, x, 0, share)
+            if share < HALF:
+                round_on_scalar(g, x, share, HALF, y[g, x][:, :, share:])
         g, x = units[-1]
-        squares = [square(g, x, t, inner[t]) for t in range(PACK)]
+        squares = [square(g, x, t, first[t]) for t in range(PACK)]
         for c0 in (0, HALF // 2):
             c1 = c0 + HALF // 2
             part = held("y_part%d" % c0, [P, PACK, HALF // 2], F32)

@@ -145,8 +145,8 @@ def tile_list_cubic_recall_weights_kernel(
                     rhs=v_w[a, x * TILES + u].bitcast(FP8X4), rhs_scale=v_s[:, a, sj],
                     start=(a == 0 and t == 0), stop=(a == PASSES - 1 and t == PACK - 1))
 
-        def gate(p_bank, a_bank, x, u, tag=""):
-            sig = held("sig%d%d" % (x, u), [P, PACK, JT], F32, tag)
+        def gate(p_bank, a_bank, x, u):
+            sig = held("sig%d%d" % (x, u), [P, PACK, JT], F32)
             nc.scalar.activation(sig[:], a_bank[:], ACT.Sigmoid)
             h_out = h_bf[x][:, u * JT * PACK:(u + 1) * JT * PACK].rearrange("p (c i t) -> p c t i", i=2, t=PACK)
             nc.vector.tensor_tensor(h_out, p_bank[:].rearrange("p t (c i) -> p c t i", i=2),
@@ -175,7 +175,7 @@ def tile_list_cubic_recall_weights_kernel(
             nc.tensor.matmul_mx(
                 out=m, lhsT=v2_w[g][:, P * t:P * (t + 1)].bitcast(FP8X4), lhsT_scale=v2_s[V2_BASE:P, cols],
                 rhs=h_w[x][:].bitcast(FP8X4), rhs_scale=h_s[x][:], start=True, stop=True)
-            if t == PACK - 2 or (g, x) == units[0]:
+            if t == PACK - 2 or (g, x, t) == (1, 0, 0):
                 sq = held("sq_hold%d%d%d" % (g, x, t), [P, HALF], F32)
             else:
                 sq = ring.tile([P, HALF], F32, name="sq")
@@ -188,12 +188,12 @@ def tile_list_cubic_recall_weights_kernel(
         def store_y(g, x, t0, t1):
             nc.sync.dma_start(y_rows[g, :, t0:t1, x * HALF:(x + 1) * HALF], y[g, x][:, t0:t1, :])
 
-        def cube(g, x, banks, per_store, inside=None):
+        def cube(g, x, banks, per_store, between=None):
             for t in range(PACK):
                 m, sq = square(g, x, t, banks[t])
                 product(y[g, x][:, t, :], g, t, m, sq[:])
-                if t == 0 and inside is not None:
-                    inside()
+                if t == 1 and between is not None:
+                    between()
                 if (t + 1) % per_store == 0:
                     store_y(g, x, t + 1 - per_store, t + 1)
 
@@ -218,7 +218,7 @@ def tile_list_cubic_recall_weights_kernel(
 
         def store_last_scales():
             for q in range(QUADS):
-                (nc.scalar if q % 2 else nc.sync).dma_start(
+                nc.sync.dma_start(
                     out_2[1:GROUPS, 4 * q:4 * q + 4, :].bitcast(I32), y_s12[32 * q:32 * q + 8, :].bitcast(I32))
 
         nc.vector.tensor_copy(v_gs[:], tab_s[:].indirect(offs_t[:]))
@@ -255,8 +255,8 @@ def tile_list_cubic_recall_weights_kernel(
         gather_v(1, 2, TILES)
         gather_v(1, TILES, 2 * TILES)
 
-        def gate_on_gpsimd(p_sb, a_bank, x, u, tag=""):
-            sig = woven(held("sig%d%d" % (x, u), [P, JT * PACK], F32, tag), a_bank, ACT.Sigmoid)
+        def gate_on_gpsimd(p_sb, a_bank, x, u):
+            sig = woven(held("sig%d%d" % (x, u), [P, JT * PACK], F32), a_bank, ACT.Sigmoid)
             nc.gpsimd.tensor_tensor(h_bf[x][:, u * JT * PACK:(u + 1) * JT * PACK], p_sb[:], sig[:], MULT)
 
         def both_passes(one_pass, bank, u):
@@ -264,26 +264,24 @@ def tile_list_cubic_recall_weights_kernel(
                 one_pass(bank, a, 1, u)
             return bank
 
-        def late_tile_on_gpsimd(u, banks, tag="", tag2=""):
+        def late_tile_on_gpsimd(u, banks):
             late_p = both_passes(p_pass, new_bank(banks[0]), u)
             late_a = both_passes(a_pass, new_bank(banks[1]), u)
-            p_sb = woven(held("p_sb1%d" % u, [P, JT * PACK], F32, tag), late_p, ACT.Copy)
-            gate_on_gpsimd(p_sb, late_a, 1, u, tag2)
+            p_sb = woven(held("p_sb1%d" % u, [P, JT * PACK], F32), late_p, ACT.Copy)
+            gate_on_gpsimd(p_sb, late_a, 1, u)
 
         for u in range(TILES):
             a_pass(a_banks[u], 1, 0, u)
             p_pass(p_banks[u], 1, 0, u)
-            if u < TILES - 1:
-                gate(p_banks[u], a_banks[u], 0, u)
-            else:
-                gate_on_gpsimd(woven(held("p_sb0", [P, JT * PACK], F32), p_banks[u], ACT.Copy), a_banks[u], 0, u)
-        gather_v2_words(0)
+            gate(p_banks[u], a_banks[u], 0, u)
         quantize_h(0)
-        gather_v2_words(1, "h_bf0")
+        gather_v2_words(0)
+        gather_v2_words(1)
         late_tile_on_gpsimd(0, (0, 1))
         late_tile_on_gpsimd(1, (4, 5))
+        late_tile_on_gpsimd(2, (2, 3))
 
-        first, second = (2, 7, 3, 6), (0, 1, 4, 5)
+        banks = [(6, 7, 0, 1), (4, 5, 2, 3), (0, 1, 4, 5), (2, 3, 6, 7), (0, 1, 4, 5), (2, 3, 6, 7)]
 
         def quantize_behind(n):
             g, x = units[n - 2]
@@ -292,12 +290,11 @@ def tile_list_cubic_recall_weights_kernel(
             store_words(g, x * HALF, y_w)
 
         for n, (g, x) in enumerate(units[:-1]):
-            cube(g, x, first if n in (0, 1, 3) else second, 2 if n else 1, (lambda: quantize_h(1)) if n == 1 else None)
+            cube(g, x, banks[n], 2 if n else 1, (lambda: quantize_h(1, "sq_hold100")) if n == 1 else None)
             if n == 0:
                 gather_v2_words(2, "sq_hold002")
-                late_tile_on_gpsimd(2, (0, 1), "sq_hold000", "sq_hold001")
-                late_a, late_p = both_passes(a_pass, new_bank(4), 3), both_passes(p_pass, new_bank(5), 3)
-                gate(late_p, late_a, 1, 3, "sq_hold003")
+                late_a, late_p = both_passes(a_pass, new_bank(6), 3), both_passes(p_pass, new_bank(7), 3)
+                gate(late_p, late_a, 1, 3)
             if n >= 2:
                 quantize_behind(n)
             if n == 4:
@@ -307,7 +304,7 @@ def tile_list_cubic_recall_weights_kernel(
             if share < HALF:
                 round_on_scalar(g, x, share, HALF, y[g, x][:, :, share:])
         g, x = units[-1]
-        squares = [square(g, x, t, first[t]) for t in range(PACK)]
+        squares = [square(g, x, t, banks[-1][t]) for t in range(PACK)]
         for c0 in (0, HALF // 2):
             c1 = c0 + HALF // 2
             part = held("y_part%d" % c0, [P, PACK, HALF // 2], F32)

@@ -28,7 +28,7 @@ TILES = HALF // JT
 GROUPS = S2 // KP
 QUADS = 4
 PER_COL = 16
-Y_ON_GPSIMD = (512, 416, 416, 416, 416)
+Y_ON_GPSIMD = (512, 400, 400, 400, 448)
 V2_BASE = 8
 
 
@@ -39,11 +39,15 @@ def tile_list_cubic_recall_weights_kernel(
     nc = tc.nc
     with ExitStack() as ctx:
         keep = ctx.enter_context(tc.tile_pool(name="keep", bufs=1))
+        shared = ctx.enter_context(tc.tile_pool(name="shared", bufs=1))
         ring = ctx.enter_context(tc.tile_pool(name="ring", bufs=6))
         psum = ctx.enter_context(tc.psum_pool(name="psum", bufs=1))
 
         def held(name, shape, dtype, tag=""):
             return keep.tile(shape, dtype, name=name, tag=tag or name, align_bytes=64)
+
+        def placed(name, shape, dtype, at):
+            return shared.tile(shape, dtype, name=name, tag=name, align_bytes=64, offset=at)
 
         offs_t = keep.tile([P, S // PER_COL], U16, name="offs_t")
         offs2_t = keep.tile([P, S2 // PER_COL], U16, name="offs2_t")
@@ -52,7 +56,7 @@ def tile_list_cubic_recall_weights_kernel(
         wp_raw = held("wp_raw", [P, PASSES, 2 * H], U8)
         wp_raw_s = held("wp_raw_s", [P, PASSES, H], U8)
         wp_w = held("wp_w", [P, PASSES, 2 * H], U8)
-        wg_bf = [held("wg_bf%d" % a, [P, H * PACK], BF16) for a in range(PASSES)]
+        wg_bf = [held("wg_bf0", [P, H * PACK], BF16), placed("wg_bf1", [P, H * PACK], BF16, 8192)]
         wg_w = [held("wg_w%d" % a, [P, H], U32) for a in range(PASSES)]
         wg_s = [held("wg_s%d" % a, [P, H], U8) for a in range(PASSES)]
         v_w = {}
@@ -60,26 +64,31 @@ def tile_list_cubic_recall_weights_kernel(
         v_s = held("v_s", [P, PASSES, S], U8)
         v2_s = held("v2_s", [P, S2], U8)
         v2_w = [None] * GROUPS
-        h_bf = [held("h_bf%d" % x, [P, HALF * PACK], BF16) for x in range(HALVES)]
+        h_bf = [held("h_bf0", [P, HALF * PACK], BF16), None]
         h_w = [None] * HALVES
         h_s = [held("h_s%d" % x, [P, HALF], U8) for x in range(HALVES)]
         y_s0 = held("y_s0", [P, S], U8)
         y_s12 = held("y_s12", [P, S], U8)
         y_s = [y_s0[:], y_s12[:], y_s12[4:P, :]]
-        tab_w = [held("tab_w0", [P, T], U32), None]
-        wg_raw = [held("wg_raw%d" % a, [P, PACK, H], F32) for a in range(PASSES)]
+        tab_w = [placed("tab_w0", [P, T], U32, 0), None]
+        wg0_raw = held("wg0_raw", [P, PACK, H], F32)
 
-        warm = held("warm", [P, 2], F32)
         nc.gpsimd.memset(wp_raw_s[:].rearrange("p a c -> p (a c)").bitcast(I32), 0)
-        nc.vector.memset(warm[:, 0:1], 0.0)
         nc.vector.memset(tab2_s[:].bitcast(I32), 0)
         nc.vector.memset(tab_s[32:64, :].bitcast(I32), 0)
         nc.gpsimd.memset(tab_s[64:P, :].bitcast(I32), 0)
         nc.gpsimd.memset(v_s[:].rearrange("p a c -> p (a c)").bitcast(I32), 0)
         nc.gpsimd.memset(v2_s[:].bitcast(I32), 0)
 
+        warm = held("warm", [P, 2], F32)
+        nc.gpsimd.memset(warm[:, 0:1], 0.0)
+        nc.scalar.activation(warm[:, 1:2], warm[:, 0:1], ACT.Sigmoid)
+
         def load_words(tile, words):
             nc.sync.dma_start(tile[:].bitcast(I32), words.rearrange("p t i -> p (t i)").bitcast(I32))
+
+        def load_wg(tile, a, c0, c1):
+            nc.sync.dma_start(tile[:], wg[a * KP:(a + 1) * KP, c0:c1].rearrange("(p j) c -> p j c", j=PACK))
 
         nc.sync.dma_start(offs_t[:], offs)
         nc.sync.dma_start(tab_s[0:32, :].bitcast(I32), tab_scales.rearrange("a q c -> q a c").bitcast(I32))
@@ -90,9 +99,7 @@ def tile_list_cubic_recall_weights_kernel(
         load_words(tab_w[0], tab_words[0])
         nc.sync.dma_start(offs2_t[:], offs2)
         nc.sync.dma_start(tab2_s[0:16, :].bitcast(I32), tab2_scales[0].bitcast(I32))
-        for a in range(PASSES):
-            nc.sync.dma_start(wg_raw[a][:], wg[a * KP:(a + 1) * KP, :].rearrange("(p j) c -> p j c", j=PACK))
-        nc.scalar.activation(warm[:, 1:2], warm[:, 0:1], ACT.Sigmoid)
+        load_wg(wg0_raw, 0, 0, H)
 
         def gather_v(a, u0, u1, tag=""):
             cols = JT // PER_COL
@@ -101,9 +108,10 @@ def tile_list_cubic_recall_weights_kernel(
             for u in range(u0, u1):
                 v_w[a, u] = tile[:, (u - u0) * JT:(u - u0 + 1) * JT]
 
-        def round_wg(a):
-            nc.scalar.copy(wg_bf[a][:].rearrange("p (u e m j) -> p u m j e", u=2, e=2, j=PACK),
-                           wg_raw[a][:].rearrange("p j (m u e) -> p u m j e", u=2, e=2))
+        def wg_views(a, raw, m0):
+            dst = wg_bf[a][:].rearrange("p (u e m j) -> p u m j e", u=2, e=2, j=PACK)
+            src = raw[:].rearrange("p j (m u e) -> p u m j e", u=2, e=2)
+            return dst[:, :, m0:m0 + src.shape[2]], src
 
         def quantize_wg(a):
             nc.vector.quantize_mx(out=wg_w[a][:].bitcast(FP8X4), scales=wg_s[a][:], in_=wg_bf[a][:])
@@ -119,8 +127,7 @@ def tile_list_cubic_recall_weights_kernel(
             nc.vector.tensor_copy(tile[:], tab2_s[:].indirect(offs2_t[:, g0 * cols:g1 * cols]))
             return tile
 
-        def deal_v2_scales(gathered, g0, g1, tag=""):
-            dealt = held("v2_ds%d" % g0, [P, (g1 - g0) * KP], U8, tag)
+        def deal_v2_scales(dealt, gathered, g0, g1):
             nc.vector.tensor_copy(dealt[:].rearrange("p (g t m) -> p t g m", t=PACK, m=P),
                                   gathered[:].rearrange("p (g m t) -> p t g m", t=PACK, m=P))
             for q in range(QUADS):
@@ -225,35 +232,43 @@ def tile_list_cubic_recall_weights_kernel(
         for q in range(QUADS):
             nc.sync.dma_start(v_s[32 * q:32 * q + 4].rearrange("p a c -> p (a c)").bitcast(I32),
                               v_gs[8 * q:8 * q + 8, :].bitcast(I32))
-        nc.vector.tensor_copy(wp_w[:].bitcast(U16).rearrange("p a (t m) -> p a t m", t=PACK),
-                              wp_raw[:].bitcast(U16).rearrange("p a (m t) -> p a t m", t=PACK))
-        tab_w[1] = held("tab_w1", [P, T], U32, "wp_raw")
+        tab_w[1] = held("tab_w1", [P, T], U32, "tab_s")
         load_words(tab_w[1], tab_words[1])
         wp_s = held("wp_s", [P, PASSES, H], U8)
         for a in range(PASSES):
             nc.gpsimd.tensor_copy(wp_s[:, a, :].rearrange("p (t m) -> p t m", t=PACK),
                                   wp_raw_s[:, a, :].rearrange("p (m t) -> p t m", t=PACK))
+            nc.gpsimd.tensor_copy(wp_w[:, a, :].rearrange("p (t m b) -> p t m b", t=PACK, b=2),
+                                  wp_raw[:, a, :].rearrange("p (m t b) -> p t m b", t=PACK, b=2))
         gather_v(0, 0, 2 * TILES)
-        tab2_w = held("tab2_w", [P, T2], U32, "tab_w0")
+        wg1_raw = [placed("wg1_raw%d" % c, [P, PACK, H // 2], F32, 4096 * c) for c in range(2)]
+        for c in range(2):
+            load_wg(wg1_raw[c], 1, c * H // 2, (c + 1) * H // 2)
+        tab2_w = held("tab2_w", [P, T2], U32, "v_gs")
         load_words(tab2_w, tab2_words[0])
-        v2_gs01 = gather_v2_scales(held("v2_gs", [P, S2], U8), 0, GROUPS)
+        v2_gs01 = gather_v2_scales(held("v2_gs01", [P, 2 * KP], U8), 0, 2)
 
         a_banks = [new_bank(u) for u in range(TILES)]
         p_banks = [new_bank(TILES + u) for u in range(TILES)]
         for u in range(TILES):
             p_pass(p_banks[u], 0, 0, u)
-        round_wg(0)
+        nc.scalar.copy(*wg_views(0, wg0_raw, 0))
         quantize_wg(0)
-        strength_t = held("strength_t", [P, GROUPS, PACK], F32, "wg_raw0")
+        strength_t = held("strength_t", [P, GROUPS, PACK], F32, "wg0_raw")
         nc.sync.dma_start(strength_t[:], strength.rearrange("(g p t) -> p g t", p=P, t=PACK))
-        deal_v2_scales(v2_gs01, 0, GROUPS, "wg_bf0")
         for u in range(TILES):
             a_pass(a_banks[u], 0, 0, u)
-        round_wg(1)
-        quantize_wg(1)
-        gather_v(1, 0, 2)
-        gather_v(1, 2, TILES)
+        gather_v(1, 0, TILES)
         gather_v(1, TILES, 2 * TILES)
+        for u in range(TILES):
+            p_pass(p_banks[u], 1, 0, u)
+        nc.scalar.copy(*wg_views(1, wg1_raw[0], 0))
+        dst, src = wg_views(1, wg1_raw[1], P // 2)
+        nc.scalar.copy(dst[:, 0], src[:, 0])
+        nc.vector.tensor_copy(dst[:, 1], src[:, 1])
+        quantize_wg(1)
+        deal_v2_scales(placed("v2_ds01", [P, 2 * KP], U8, 8192), v2_gs01, 0, 2)
+        v2_gs2 = gather_v2_scales(placed("v2_gs2", [P, KP], U8, 8192 + 2048), 2, 3)
 
         def gate_on_gpsimd(p_sb, a_bank, x, u):
             sig = woven(held("sig%d%d" % (x, u), [P, JT * PACK], F32), a_bank, ACT.Sigmoid)
@@ -270,18 +285,23 @@ def tile_list_cubic_recall_weights_kernel(
             p_sb = woven(held("p_sb1%d" % u, [P, JT * PACK], F32), late_p, ACT.Copy)
             gate_on_gpsimd(p_sb, late_a, 1, u)
 
+        p_sb = [woven(placed("p_sb0%d" % u, [P, JT * PACK], F32, 4096 + 2048 * u), p_banks[u], ACT.Copy) for u in range(2)]
         for u in range(TILES):
             a_pass(a_banks[u], 1, 0, u)
-            p_pass(p_banks[u], 1, 0, u)
-            gate(p_banks[u], a_banks[u], 0, u)
+            if u < 2:
+                gate_on_gpsimd(p_sb[u], a_banks[u], 0, u)
+            else:
+                gate(p_banks[u], a_banks[u], 0, u)
         quantize_h(0)
+        h_bf[1] = held("h_bf1", [P, HALF * PACK], BF16, "h_bf0")
         gather_v2_words(0)
         gather_v2_words(1)
-        late_tile_on_gpsimd(0, (0, 1))
-        late_tile_on_gpsimd(1, (4, 5))
+        gather_v2_words(2)
+        late_tile_on_gpsimd(0, (4, 0))
+        late_tile_on_gpsimd(1, (1, 5))
         late_tile_on_gpsimd(2, (2, 3))
 
-        banks = [(6, 7, 0, 1), (4, 5, 2, 3), (0, 1, 4, 5), (2, 3, 6, 7), (0, 1, 4, 5), (2, 3, 6, 7)]
+        banks = [(6, 7, 4, 0), (5, 1, 2, 3), (4, 0, 5, 1), (2, 3, 6, 7), (4, 0, 5, 1), (2, 3, 6, 7)]
 
         def quantize_behind(n):
             g, x = units[n - 2]
@@ -292,7 +312,7 @@ def tile_list_cubic_recall_weights_kernel(
         for n, (g, x) in enumerate(units[:-1]):
             cube(g, x, banks[n], 2 if n else 1, (lambda: quantize_h(1, "sq_hold100")) if n == 1 else None)
             if n == 0:
-                gather_v2_words(2, "sq_hold002")
+                deal_v2_scales(held("v2_ds2", [P, KP], U8, "sq_hold002"), v2_gs2, 2, 3)
                 late_a, late_p = both_passes(a_pass, new_bank(6), 3), both_passes(p_pass, new_bank(7), 3)
                 gate(late_p, late_a, 1, 3)
             if n >= 2:
@@ -313,8 +333,8 @@ def tile_list_cubic_recall_weights_kernel(
             nc.sync.dma_start(y_rows[g, :, :, x * HALF + c0:x * HALF + c1], part[:])
             round_on_scalar(g, x, c0, c1, part[:])
         quantize_behind(len(units) - 1)
-        y_w = held("y_w_last", [P, S], U32)
-        quantize_y(*units[-2], y_w[:, :HALF])
-        quantize_y(*units[-1], y_w[:, HALF:])
-        store_words(GROUPS - 1, 0, y_w)
+        for g, x in units[-2:]:
+            y_w = held("y_w_last%d" % x, [P, HALF], U32)
+            quantize_y(g, x, y_w[:])
+            store_words(g, x * HALF, y_w)
         store_last_scales()

@@ -234,12 +234,12 @@ def tile_list_cubic_recall_weights_kernel(
                               v_gs[8 * q:8 * q + 8, :].bitcast(I32))
         tab_w[1] = held("tab_w1", [P, T], U32, "tab_s")
         load_words(tab_w[1], tab_words[1])
-        wp_s = held("wp_s", [P, PASSES, H], U8)
+        nc.vector.tensor_copy(wp_w[:].bitcast(U16).rearrange("p a (t m) -> p a t m", t=PACK),
+                              wp_raw[:].bitcast(U16).rearrange("p a (m t) -> p a t m", t=PACK))
+        wp_s = held("wp_s", [P, PASSES, H], U8, "wp_raw")
         for a in range(PASSES):
             nc.gpsimd.tensor_copy(wp_s[:, a, :].rearrange("p (t m) -> p t m", t=PACK),
                                   wp_raw_s[:, a, :].rearrange("p (m t) -> p t m", t=PACK))
-            nc.gpsimd.tensor_copy(wp_w[:, a, :].rearrange("p (t m b) -> p t m b", t=PACK, b=2),
-                                  wp_raw[:, a, :].rearrange("p (m t b) -> p t m b", t=PACK, b=2))
         gather_v(0, 0, 2 * TILES)
         wg1_raw = [placed("wg1_raw%d" % c, [P, PACK, H // 2], F32, 4096 * c) for c in range(2)]
         for c in range(2):

@@ -236,10 +236,9 @@ def tile_list_cubic_recall_weights_kernel(
         load_words(tab_w[1], tab_words[1])
         nc.vector.tensor_copy(wp_w[:].bitcast(U16).rearrange("p a (t m) -> p a t m", t=PACK),
                               wp_raw[:].bitcast(U16).rearrange("p a (m t) -> p a t m", t=PACK))
-        wp_s = held("wp_s", [P, PASSES, H], U8, "wp_raw")
-        for a in range(PASSES):
-            nc.gpsimd.tensor_copy(wp_s[:, a, :].rearrange("p (t m) -> p t m", t=PACK),
-                                  wp_raw_s[:, a, :].rearrange("p (m t) -> p t m", t=PACK))
+        wp_s = held("wp_s", [P, PASSES, H], U8)
+        nc.vector.tensor_copy(wp_s[:].rearrange("p a (t m) -> p a t m", t=PACK),
+                              wp_raw_s[:].rearrange("p a (m t) -> p a t m", t=PACK))
         gather_v(0, 0, 2 * TILES)
         wg1_raw = [placed("wg1_raw%d" % c, [P, PACK, H // 2], F32, 4096 * c) for c in range(2)]
         for c in range(2):

@@ -28,7 +28,7 @@ TILES = HALF // JT
 GROUPS = S2 // KP
 QUADS = 4
 PER_COL = 16
-Y_ON_GPSIMD = (512, 400, 400, 400, 448)
+Y_ON_GPSIMD = (368, 416, 416, 448)
 V2_BASE = 8
 
 
@@ -54,9 +54,9 @@ def tile_list_cubic_recall_weights_kernel(
         tab_s = held("tab_s", [P, T], U8)
         tab2_s = held("tab2_s", [P, T2], U8)
         wp_raw = held("wp_raw", [P, PASSES, 2 * H], U8)
-        wp_raw_s = held("wp_raw_s", [P, PASSES, H], U8)
+        wp_raw_s = placed("wp_raw_s", [P, PASSES, H], U8, 0)
         wp_w = held("wp_w", [P, PASSES, 2 * H], U8)
-        wg_bf = [held("wg_bf0", [P, H * PACK], BF16), placed("wg_bf1", [P, H * PACK], BF16, 8192)]
+        wg_bf = [held("wg_bf0", [P, H * PACK], BF16), placed("wg_bf1", [P, H * PACK], BF16, 4096)]
         wg_w = [held("wg_w%d" % a, [P, H], U32) for a in range(PASSES)]
         wg_s = [held("wg_s%d" % a, [P, H], U8) for a in range(PASSES)]
         v_w = {}
@@ -70,7 +70,7 @@ def tile_list_cubic_recall_weights_kernel(
         y_s0 = held("y_s0", [P, S], U8)
         y_s12 = held("y_s12", [P, S], U8)
         y_s = [y_s0[:], y_s12[:], y_s12[4:P, :]]
-        tab_w = [placed("tab_w0", [P, T], U32, 0), None]
+        tab_w = [held("tab_w0", [P, T], U32), None]
         wg0_raw = held("wg0_raw", [P, PACK, H], F32)
 
         nc.gpsimd.memset(wp_raw_s[:].rearrange("p a c -> p (a c)").bitcast(I32), 0)
@@ -100,10 +100,13 @@ def tile_list_cubic_recall_weights_kernel(
         nc.sync.dma_start(offs2_t[:], offs2)
         nc.sync.dma_start(tab2_s[0:16, :].bitcast(I32), tab2_scales[0].bitcast(I32))
         load_wg(wg0_raw, 0, 0, H)
+        wg1_raw = [held("wg1_raw0", [P, PACK, H // 2], F32), None]
+        load_wg(wg1_raw[0], 1, 0, H // 2)
 
-        def gather_v(a, u0, u1, tag=""):
+        def gather_v(a, u0, u1, at=None):
             cols = JT // PER_COL
-            tile = held("v_w%d%d" % (a, u0), [P, JT * (u1 - u0)], U32, tag)
+            name, shape = "v_w%d%d" % (a, u0), [P, JT * (u1 - u0)]
+            tile = held(name, shape, U32) if at is None else placed(name, shape, U32, at)
             nc.vector.tensor_copy(tile[:], tab_w[a][:].indirect(offs_t[:, u0 * cols:u1 * cols]))
             for u in range(u0, u1):
                 v_w[a, u] = tile[:, (u - u0) * JT:(u - u0 + 1) * JT]
@@ -174,7 +177,8 @@ def tile_list_cubic_recall_weights_kernel(
 
         units = [(0, 0), (1, 0), (0, 1), (1, 1), (2, 0), (2, 1)]
         y = {unit: held("y%d%d" % unit, [P, PACK, HALF], F32) for unit in units[:-1]}
-        y_bf = {unit: held("y_bf%d%d" % unit, [P, HALF * PACK], BF16) for unit in units}
+        y_bf = {unit: held("y_bf%d%d" % unit, [P, HALF * PACK], BF16) for unit in units[1:]}
+        y_bf_first = held("y_bf_first", [P, HALF * PACK // 2], BF16)
 
         def square(g, x, t, bank):
             m = new_bank(bank)[:].rearrange("p t j -> p (t j)")
@@ -204,20 +208,20 @@ def tile_list_cubic_recall_weights_kernel(
                 if (t + 1) % per_store == 0:
                     store_y(g, x, t + 1 - per_store, t + 1)
 
-        def round_on_gpsimd(g, x, c0, c1):
-            nc.gpsimd.tensor_scalar(y_bf[g, x][:, c0 * PACK:c1 * PACK].rearrange("p (j t) -> p j t", t=PACK),
+        def round_on_gpsimd(g, x, c0, c1, dst):
+            nc.gpsimd.tensor_scalar(dst.rearrange("p (j t) -> p j t", t=PACK),
                                     y[g, x][:, :, c0:c1].rearrange("p t j -> p j t"), 1.0, -0.0, MULT, ADD)
 
         def round_on_scalar(g, x, c0, c1, src):
             nc.scalar.copy(y_bf[g, x][:, c0 * PACK:c1 * PACK].rearrange("p (c i t) -> p c t i", i=2, t=PACK),
                            src.rearrange("p t (c i) -> p c t i", i=2))
 
-        def quantize_y(g, x, y_w):
-            nc.vector.quantize_mx(out=y_w.bitcast(FP8X4), scales=y_s[g][:, x * HALF:(x + 1) * HALF], in_=y_bf[g, x][:])
-
-        def store_words(g, first, y_w):
+        def quantize_y(g, first, rounded, tag=""):
+            width = rounded.shape[1] // PACK
+            y_w = held("y_w%d_%d" % (g, first), [P, width], U32, tag)
+            nc.vector.quantize_mx(out=y_w[:].bitcast(FP8X4), scales=y_s[g][:, first:first + width], in_=rounded[:])
             words = out_1[g].rearrange("p m t -> p (m t)").bitcast(I32)
-            nc.sync.dma_start(words[:, first:first + y_w.shape[1]], y_w[:].bitcast(I32))
+            nc.sync.dma_start(words[:, first:first + width], y_w[:].bitcast(I32))
 
         def store_first_scales():
             for q in range(QUADS):
@@ -239,11 +243,10 @@ def tile_list_cubic_recall_weights_kernel(
         wp_s = held("wp_s", [P, PASSES, H], U8)
         nc.vector.tensor_copy(wp_s[:].rearrange("p a (t m) -> p a t m", t=PACK),
                               wp_raw_s[:].rearrange("p a (m t) -> p a t m", t=PACK))
+        wg1_raw[1] = placed("wg1_raw1", [P, PACK, H // 2], F32, 0)
+        load_wg(wg1_raw[1], 1, H // 2, H)
         gather_v(0, 0, 2 * TILES)
-        wg1_raw = [placed("wg1_raw%d" % c, [P, PACK, H // 2], F32, 4096 * c) for c in range(2)]
-        for c in range(2):
-            load_wg(wg1_raw[c], 1, c * H // 2, (c + 1) * H // 2)
-        tab2_w = held("tab2_w", [P, T2], U32, "v_gs")
+        tab2_w = held("tab2_w", [P, T2], U32, "tab_w0")
         load_words(tab2_w, tab2_words[0])
         v2_gs01 = gather_v2_scales(held("v2_gs01", [P, 2 * KP], U8), 0, 2)
 
@@ -258,7 +261,6 @@ def tile_list_cubic_recall_weights_kernel(
         for u in range(TILES):
             a_pass(a_banks[u], 0, 0, u)
         gather_v(1, 0, TILES)
-        gather_v(1, TILES, 2 * TILES)
         for u in range(TILES):
             p_pass(p_banks[u], 1, 0, u)
         nc.scalar.copy(*wg_views(1, wg1_raw[0], 0))
@@ -266,8 +268,9 @@ def tile_list_cubic_recall_weights_kernel(
         nc.scalar.copy(dst[:, 0], src[:, 0])
         nc.vector.tensor_copy(dst[:, 1], src[:, 1])
         quantize_wg(1)
-        deal_v2_scales(placed("v2_ds01", [P, 2 * KP], U8, 8192), v2_gs01, 0, 2)
-        v2_gs2 = gather_v2_scales(placed("v2_gs2", [P, KP], U8, 8192 + 2048), 2, 3)
+        deal_v2_scales(placed("v2_ds01", [P, 2 * KP], U8, 4096), v2_gs01, 0, 2)
+        gather_v(1, TILES, 2 * TILES, 4096 + 1024)
+        v2_gs2 = gather_v2_scales(placed("v2_gs2", [P, KP], U8, 4096 + 3072), 2, 3)
 
         def gate_on_gpsimd(p_sb, a_bank, x, u):
             sig = woven(held("sig%d%d" % (x, u), [P, JT * PACK], F32), a_bank, ACT.Sigmoid)
@@ -284,7 +287,7 @@ def tile_list_cubic_recall_weights_kernel(
             p_sb = woven(held("p_sb1%d" % u, [P, JT * PACK], F32), late_p, ACT.Copy)
             gate_on_gpsimd(p_sb, late_a, 1, u)
 
-        p_sb = [woven(placed("p_sb0%d" % u, [P, JT * PACK], F32, 4096 + 2048 * u), p_banks[u], ACT.Copy) for u in range(2)]
+        p_sb = [woven(placed("p_sb0%d" % u, [P, JT * PACK], F32, 2048 * u), p_banks[u], ACT.Copy) for u in range(2)]
         for u in range(TILES):
             a_pass(a_banks[u], 1, 0, u)
             if u < 2:
@@ -304,12 +307,15 @@ def tile_list_cubic_recall_weights_kernel(
 
         def quantize_behind(n):
             g, x = units[n - 2]
-            y_w = held("y_w%d" % n, [P, HALF], U32, "sq_hold%d%d2" % units[n])
-            quantize_y(g, x, y_w[:])
-            store_words(g, x * HALF, y_w)
+            rounded = y_bf[g, x]
+            quantize_y(g, (x + 1) * HALF - rounded.shape[1] // PACK, rounded, "sq_hold%d%d2" % units[n])
+
+        def inside_second_cube():
+            quantize_h(1, "sq_hold100")
+            quantize_y(0, 0, y_bf_first)
 
         for n, (g, x) in enumerate(units[:-1]):
-            cube(g, x, banks[n], 2 if n else 1, (lambda: quantize_h(1, "sq_hold100")) if n == 1 else None)
+            cube(g, x, banks[n], 2 if n else 1, inside_second_cube if n == 1 else None)
             if n == 0:
                 deal_v2_scales(held("v2_ds2", [P, KP], U8, "sq_hold002"), v2_gs2, 2, 3)
                 late_a, late_p = both_passes(a_pass, new_bank(6), 3), both_passes(p_pass, new_bank(7), 3)
@@ -318,10 +324,15 @@ def tile_list_cubic_recall_weights_kernel(
                 quantize_behind(n)
             if n == 4:
                 store_first_scales()
-            share = Y_ON_GPSIMD[n]
-            round_on_gpsimd(g, x, 0, share)
-            if share < HALF:
-                round_on_scalar(g, x, share, HALF, y[g, x][:, :, share:])
+            if n == 0:
+                round_on_gpsimd(g, x, 0, HALF // 2, y_bf_first[:])
+                continue
+            if n == 1:
+                y_bf[units[0]] = held("y_bf00", [P, HALF * PACK // 2], BF16, "h_bf0")
+                round_on_gpsimd(*units[0], HALF // 2, HALF, y_bf[units[0]][:])
+            share = Y_ON_GPSIMD[n - 1]
+            round_on_gpsimd(g, x, 0, share, y_bf[g, x][:, :share * PACK])
+            round_on_scalar(g, x, share, HALF, y[g, x][:, :, share:])
         g, x = units[-1]
         squares = [square(g, x, t, banks[-1][t]) for t in range(PACK)]
         for c0 in (0, HALF // 2):
@@ -333,7 +344,5 @@ def tile_list_cubic_recall_weights_kernel(
             round_on_scalar(g, x, c0, c1, part[:])
         quantize_behind(len(units) - 1)
         for g, x in units[-2:]:
-            y_w = held("y_w_last%d" % x, [P, HALF], U32)
-            quantize_y(g, x, y_w[:])
-            store_words(g, x * HALF, y_w)
+            quantize_y(g, x * HALF, y_bf[g, x])
         store_last_scales()

@@ -26,10 +26,11 @@ HALVES = S // HALF
 JT = 128
 TILES = HALF // JT
 GROUPS = S2 // KP
-QUADS = 4
+QUADS = (0, 2, 1, 3)
 PER_COL = 16
 Y_ON_GPSIMD = (368, 416, 416, 448)
 V2_BASE = 8
+V2_RAW = 16
 
 
 def tile_list_cubic_recall_weights_kernel(
@@ -93,12 +94,12 @@ def tile_list_cubic_recall_weights_kernel(
         nc.sync.dma_start(offs_t[:], offs)
         nc.sync.dma_start(tab_s[0:32, :].bitcast(I32), tab_scales.rearrange("a q c -> q a c").bitcast(I32))
         nc.sync.dma_start(wp_raw[:].bitcast(I32), wp_words.rearrange("a p c -> p a c").bitcast(I32))
-        for q in range(QUADS):
-            nc.sync.dma_start(wp_raw_s[32 * q:32 * q + 4].bitcast(I32),
-                              wp_scales[:, 4 * q:4 * q + 4, :].rearrange("a r c -> r a c").bitcast(I32))
+        for r in range(4):
+            nc.sync.dma_start(wp_raw_s[r:P:32].bitcast(I32),
+                              wp_scales[:, r:16:4, :].rearrange("a q c -> q a c").bitcast(I32))
         load_words(tab_w[0], tab_words[0])
         nc.sync.dma_start(offs2_t[:], offs2)
-        nc.sync.dma_start(tab2_s[0:16, :].bitcast(I32), tab2_scales[0].bitcast(I32))
+        nc.sync.dma_start(tab2_s[V2_RAW:V2_RAW + 16, :].bitcast(I32), tab2_scales[0].bitcast(I32))
         load_wg(wg0_raw, 0, 0, H)
         wg1_raw = [held("wg1_raw0", [P, PACK, H // 2], F32), None]
         load_wg(wg1_raw[0], 1, 0, H // 2)
@@ -133,9 +134,9 @@ def tile_list_cubic_recall_weights_kernel(
         def deal_v2_scales(dealt, gathered, g0, g1):
             nc.vector.tensor_copy(dealt[:].rearrange("p (g t m) -> p t g m", t=PACK, m=P),
                                   gathered[:].rearrange("p (g m t) -> p t g m", t=PACK, m=P))
-            for q in range(QUADS):
-                nc.sync.dma_start(v2_s[32 * q + V2_BASE:32 * q + V2_BASE + 4, g0 * KP:g1 * KP].bitcast(I32),
-                                  dealt[4 * q:4 * q + 4, :].bitcast(I32))
+            for r in range(4):
+                nc.sync.dma_start(v2_s[V2_BASE + r:P:32, g0 * KP:g1 * KP].bitcast(I32),
+                                  dealt[V2_RAW + r:V2_RAW + 16:4, :].bitcast(I32))
 
         def p_pass(bank, a, x, u):
             sj = slice(x * HALF + u * JT, x * HALF + (u + 1) * JT)
@@ -224,16 +225,16 @@ def tile_list_cubic_recall_weights_kernel(
             nc.sync.dma_start(words[:, first:first + width], y_w[:].bitcast(I32))
 
         def store_first_scales():
-            for q in range(QUADS):
-                nc.sync.dma_start(out_2[0, 4 * q:4 * q + 4, :].bitcast(I32), y_s0[32 * q:32 * q + 4, :].bitcast(I32))
+            for r in range(4):
+                nc.sync.dma_start(out_2[0, r:16:4, :].bitcast(I32), y_s0[r:P:32, :].bitcast(I32))
 
         def store_last_scales():
-            for q in range(QUADS):
+            for q in QUADS:
                 nc.sync.dma_start(
                     out_2[1:GROUPS, 4 * q:4 * q + 4, :].bitcast(I32), y_s12[32 * q:32 * q + 8, :].bitcast(I32))
 
         nc.vector.tensor_copy(v_gs[:], tab_s[:].indirect(offs_t[:]))
-        for q in range(QUADS):
+        for q in QUADS:
             nc.sync.dma_start(v_s[32 * q:32 * q + 4].rearrange("p a c -> p (a c)").bitcast(I32),
                               v_gs[8 * q:8 * q + 8, :].bitcast(I32))
         tab_w[1] = held("tab_w1", [P, T], U32, "tab_s")

@@ -28,9 +28,10 @@ TILES = HALF // JT
 GROUPS = S2 // KP
 QUADS = (0, 2, 1, 3)
 PER_COL = 16
-Y_ON_GPSIMD = (368, 416, 416, 448)
+Y_ON_GPSIMD = (320, 416, 416, 448)
 V2_BASE = 8
 V2_RAW = 16
+AT_SIG3 = 9216
 
 
 def tile_list_cubic_recall_weights_kernel(
@@ -55,7 +56,7 @@ def tile_list_cubic_recall_weights_kernel(
         tab_s = held("tab_s", [P, T], U8)
         tab2_s = held("tab2_s", [P, T2], U8)
         wp_raw = held("wp_raw", [P, PASSES, 2 * H], U8)
-        wp_raw_s = placed("wp_raw_s", [P, PASSES, H], U8, 0)
+        wp_raw_s = placed("wp_raw_s", [P, PASSES, H], U8, 1024)
         wp_w = held("wp_w", [P, PASSES, 2 * H], U8)
         wg_bf = [held("wg_bf0", [P, H * PACK], BF16), placed("wg_bf1", [P, H * PACK], BF16, 4096)]
         wg_w = [held("wg_w%d" % a, [P, H], U32) for a in range(PASSES)]
@@ -101,7 +102,7 @@ def tile_list_cubic_recall_weights_kernel(
         nc.sync.dma_start(offs2_t[:], offs2)
         nc.sync.dma_start(tab2_s[V2_RAW:V2_RAW + 16, :].bitcast(I32), tab2_scales[0].bitcast(I32))
         load_wg(wg0_raw, 0, 0, H)
-        wg1_raw = [held("wg1_raw0", [P, PACK, H // 2], F32), None]
+        wg1_raw = [held("wg1_raw0", [P, PACK, H // 2], F32), None, None]
         load_wg(wg1_raw[0], 1, 0, H // 2)
 
         def gather_v(a, u0, u1, at=None):
@@ -120,11 +121,13 @@ def tile_list_cubic_recall_weights_kernel(
         def quantize_wg(a):
             nc.vector.quantize_mx(out=wg_w[a][:].bitcast(FP8X4), scales=wg_s[a][:], in_=wg_bf[a][:])
 
-        def gather_v2_words(g, tag=""):
+        def gather_v2_words(g0, g1, at):
             cols = KP // PER_COL
-            v2_w[g] = held("v2_w%d" % g, [P, KP], U32, tag)
-            nc.vector.tensor_copy(v2_w[g][:].rearrange("p (t m) -> p m t", t=PACK),
-                                  tab2_w[:].indirect(offs2_t[:, g * cols:(g + 1) * cols]))
+            tile = placed("v2_w%d" % g0, [P, (g1 - g0) * KP], U32, at)
+            nc.vector.tensor_copy(tile[:].rearrange("p (g t m) -> p g m t", t=PACK, m=P),
+                                  tab2_w[:].indirect(offs2_t[:, g0 * cols:g1 * cols]))
+            for g in range(g0, g1):
+                v2_w[g] = tile[:, (g - g0) * KP:(g - g0 + 1) * KP]
 
         def gather_v2_scales(tile, g0, g1):
             cols = KP // PER_COL
@@ -157,7 +160,8 @@ def tile_list_cubic_recall_weights_kernel(
                     start=(a == 0 and t == 0), stop=(a == PASSES - 1 and t == PACK - 1))
 
         def gate(p_bank, a_bank, x, u):
-            sig = held("sig%d%d" % (x, u), [P, PACK, JT], F32)
+            name, shape = "sig%d%d" % (x, u), [P, PACK, JT]
+            sig = placed(name, shape, F32, AT_SIG3) if u == TILES - 1 else held(name, shape, F32)
             nc.scalar.activation(sig[:], a_bank[:], ACT.Sigmoid)
             h_out = h_bf[x][:, u * JT * PACK:(u + 1) * JT * PACK].rearrange("p (c i t) -> p c t i", i=2, t=PACK)
             nc.vector.tensor_tensor(h_out, p_bank[:].rearrange("p t (c i) -> p c t i", i=2),
@@ -179,7 +183,6 @@ def tile_list_cubic_recall_weights_kernel(
         units = [(0, 0), (1, 0), (0, 1), (1, 1), (2, 0), (2, 1)]
         y = {unit: held("y%d%d" % unit, [P, PACK, HALF], F32) for unit in units[:-1]}
         y_bf = {unit: held("y_bf%d%d" % unit, [P, HALF * PACK], BF16) for unit in units[1:]}
-        y_bf_first = held("y_bf_first", [P, HALF * PACK // 2], BF16)
 
         def square(g, x, t, bank):
             m = new_bank(bank)[:].rearrange("p t j -> p (t j)")
@@ -187,7 +190,7 @@ def tile_list_cubic_recall_weights_kernel(
             nc.tensor.matmul_mx(
                 out=m, lhsT=v2_w[g][:, P * t:P * (t + 1)].bitcast(FP8X4), lhsT_scale=v2_s[V2_BASE:P, cols],
                 rhs=h_w[x][:].bitcast(FP8X4), rhs_scale=h_s[x][:], start=True, stop=True)
-            if t == PACK - 2 or (g, x, t) == (1, 0, 0):
+            if t == PACK - 2:
                 sq = held("sq_hold%d%d%d" % (g, x, t), [P, HALF], F32)
             else:
                 sq = ring.tile([P, HALF], F32, name="sq")
@@ -200,12 +203,10 @@ def tile_list_cubic_recall_weights_kernel(
         def store_y(g, x, t0, t1):
             nc.sync.dma_start(y_rows[g, :, t0:t1, x * HALF:(x + 1) * HALF], y[g, x][:, t0:t1, :])
 
-        def cube(g, x, banks, per_store, between=None):
+        def cube(g, x, banks, per_store):
             for t in range(PACK):
                 m, sq = square(g, x, t, banks[t])
                 product(y[g, x][:, t, :], g, t, m, sq[:])
-                if t == 1 and between is not None:
-                    between()
                 if (t + 1) % per_store == 0:
                     store_y(g, x, t + 1 - per_store, t + 1)
 
@@ -244,8 +245,10 @@ def tile_list_cubic_recall_weights_kernel(
         wp_s = held("wp_s", [P, PASSES, H], U8)
         nc.vector.tensor_copy(wp_s[:].rearrange("p a (t m) -> p a t m", t=PACK),
                               wp_raw_s[:].rearrange("p a (m t) -> p a t m", t=PACK))
-        wg1_raw[1] = placed("wg1_raw1", [P, PACK, H // 2], F32, 0)
-        load_wg(wg1_raw[1], 1, H // 2, H)
+        wg1_raw[1] = held("wg1_raw1", [P, PACK, H // 4], F32, "wp_raw")
+        wg1_raw[2] = placed("wg1_raw2", [P, PACK, H // 4], F32, 1024)
+        for piece in (1, 2):
+            load_wg(wg1_raw[piece], 1, (piece + 1) * H // 4, (piece + 2) * H // 4)
         gather_v(0, 0, 2 * TILES)
         tab2_w = held("tab2_w", [P, T2], U32, "tab_w0")
         load_words(tab2_w, tab2_words[0])
@@ -262,14 +265,12 @@ def tile_list_cubic_recall_weights_kernel(
         for u in range(TILES):
             a_pass(a_banks[u], 0, 0, u)
         gather_v(1, 0, TILES)
-        for u in range(TILES):
-            p_pass(p_banks[u], 1, 0, u)
+        p_pass(p_banks[0], 1, 0, 0)
         nc.scalar.copy(*wg_views(1, wg1_raw[0], 0))
-        dst, src = wg_views(1, wg1_raw[1], P // 2)
-        nc.scalar.copy(dst[:, 0], src[:, 0])
-        nc.vector.tensor_copy(dst[:, 1], src[:, 1])
+        for piece in (1, 2):
+            nc.scalar.copy(*wg_views(1, wg1_raw[piece], (piece + 1) * P // 4))
         quantize_wg(1)
-        deal_v2_scales(placed("v2_ds01", [P, 2 * KP], U8, 4096), v2_gs01, 0, 2)
+        deal_v2_scales(held("v2_ds01", [P, 2 * KP], U8, "wp_raw"), v2_gs01, 0, 2)
         gather_v(1, TILES, 2 * TILES, 4096 + 1024)
         v2_gs2 = gather_v2_scales(placed("v2_gs2", [P, KP], U8, 4096 + 3072), 2, 3)
 
@@ -283,59 +284,59 @@ def tile_list_cubic_recall_weights_kernel(
             return bank
 
         def late_tile_on_gpsimd(u, banks):
-            late_p = both_passes(p_pass, new_bank(banks[0]), u)
-            late_a = both_passes(a_pass, new_bank(banks[1]), u)
+            late_a = both_passes(a_pass, new_bank(banks[0]), u)
+            late_p = both_passes(p_pass, new_bank(banks[1]), u)
+            sig = woven(held("sig1%d" % u, [P, JT * PACK], F32), late_a, ACT.Sigmoid)
             p_sb = woven(held("p_sb1%d" % u, [P, JT * PACK], F32), late_p, ACT.Copy)
-            gate_on_gpsimd(p_sb, late_a, 1, u)
+            nc.gpsimd.tensor_tensor(h_bf[1][:, u * JT * PACK:(u + 1) * JT * PACK], p_sb[:], sig[:], MULT)
 
-        p_sb = [woven(placed("p_sb0%d" % u, [P, JT * PACK], F32, 2048 * u), p_banks[u], ACT.Copy) for u in range(2)]
+        p_sb = woven(placed("p_sb00", [P, JT * PACK], F32, 0), p_banks[0], ACT.Copy)
         for u in range(TILES):
             a_pass(a_banks[u], 1, 0, u)
-            if u < 2:
-                gate_on_gpsimd(p_sb[u], a_banks[u], 0, u)
+            if u == 0:
+                gate_on_gpsimd(p_sb, a_banks[u], 0, u)
+                deal_v2_scales(placed("v2_ds2", [P, KP], U8, 0), v2_gs2, 2, 3)
             else:
+                p_pass(p_banks[u], 1, 0, u)
                 gate(p_banks[u], a_banks[u], 0, u)
         quantize_h(0)
         h_bf[1] = held("h_bf1", [P, HALF * PACK], BF16, "h_bf0")
-        gather_v2_words(0)
-        gather_v2_words(1)
-        gather_v2_words(2)
+        gather_v2_words(0, 1, AT_SIG3 - 1024)
+        gather_v2_words(1, 3, AT_SIG3 + 1024)
         late_tile_on_gpsimd(0, (4, 0))
-        late_tile_on_gpsimd(1, (1, 5))
-        late_tile_on_gpsimd(2, (2, 3))
+        late_tile_on_gpsimd(1, (1, 2))
+        late_tile_on_gpsimd(2, (5, 3))
+        late_tile_on_gpsimd(3, (6, 7))
 
-        banks = [(6, 7, 4, 0), (5, 1, 2, 3), (4, 0, 5, 1), (2, 3, 6, 7), (4, 0, 5, 1), (2, 3, 6, 7)]
+        banks = [(4, 0, 1, 2), (5, 3, 6, 7)] * GROUPS
 
         def quantize_behind(n):
             g, x = units[n - 2]
             rounded = y_bf[g, x]
             quantize_y(g, (x + 1) * HALF - rounded.shape[1] // PACK, rounded, "sq_hold%d%d2" % units[n])
 
-        def inside_second_cube():
-            quantize_h(1, "sq_hold100")
-            quantize_y(0, 0, y_bf_first)
+        def round_rest(n):
+            share = Y_ON_GPSIMD[n - 1]
+            round_on_scalar(*units[n], share, HALF, y[units[n]][:, :, share:])
 
         for n, (g, x) in enumerate(units[:-1]):
-            cube(g, x, banks[n], 2 if n else 1, inside_second_cube if n == 1 else None)
+            cube(g, x, banks[n], 2 if n else 1)
             if n == 0:
-                deal_v2_scales(held("v2_ds2", [P, KP], U8, "sq_hold002"), v2_gs2, 2, 3)
-                late_a, late_p = both_passes(a_pass, new_bank(6), 3), both_passes(p_pass, new_bank(7), 3)
-                gate(late_p, late_a, 1, 3)
+                quantize_h(1, "sq_hold002")
+                y_bf[g, x] = held("y_bf00", [P, HALF * PACK], BF16, "h_bf0")
+                round_on_gpsimd(g, x, 0, HALF, y_bf[g, x][:])
+                continue
             if n >= 2:
                 quantize_behind(n)
             if n == 4:
                 store_first_scales()
-            if n == 0:
-                round_on_gpsimd(g, x, 0, HALF // 2, y_bf_first[:])
-                continue
-            if n == 1:
-                y_bf[units[0]] = held("y_bf00", [P, HALF * PACK // 2], BF16, "h_bf0")
-                round_on_gpsimd(*units[0], HALF // 2, HALF, y_bf[units[0]][:])
             share = Y_ON_GPSIMD[n - 1]
             round_on_gpsimd(g, x, 0, share, y_bf[g, x][:, :share * PACK])
-            round_on_scalar(g, x, share, HALF, y[g, x][:, :, share:])
+            if n >= 2:
+                round_rest(n - 1)
         g, x = units[-1]
         squares = [square(g, x, t, banks[-1][t]) for t in range(PACK)]
+        round_rest(len(units) - 2)
         for c0 in (0, HALF // 2):
             c1 = c0 + HALF // 2
             part = held("y_part%d" % c0, [P, PACK, HALF // 2], F32)

@@ -30,7 +30,7 @@ QUADS = (0, 2, 1, 3)
 PER_COL = 16
 Y_ON_GPSIMD = (320, 416, 416, 448)
 V2_BASE = 8
-V2_RAW = 16
+V2_RAW = 4
 AT_SIG3 = 9216
 
 
@@ -100,7 +100,7 @@ def tile_list_cubic_recall_weights_kernel(
                               wp_scales[:, r:16:4, :].rearrange("a q c -> q a c").bitcast(I32))
         load_words(tab_w[0], tab_words[0])
         nc.sync.dma_start(offs2_t[:], offs2)
-        nc.sync.dma_start(tab2_s[V2_RAW:V2_RAW + 16, :].bitcast(I32), tab2_scales[0].bitcast(I32))
+        nc.sync.dma_start(tab2_s[V2_RAW:P:8, :].bitcast(I32), tab2_scales[0].bitcast(I32))
         load_wg(wg0_raw, 0, 0, H)
         wg1_raw = [held("wg1_raw0", [P, PACK, H // 2], F32), None, None]
         load_wg(wg1_raw[0], 1, 0, H // 2)
@@ -139,7 +139,7 @@ def tile_list_cubic_recall_weights_kernel(
                                   gathered[:].rearrange("p (g m t) -> p t g m", t=PACK, m=P))
             for r in range(4):
                 nc.sync.dma_start(v2_s[V2_BASE + r:P:32, g0 * KP:g1 * KP].bitcast(I32),
-                                  dealt[V2_RAW + r:V2_RAW + 16:4, :].bitcast(I32))
+                                  dealt[V2_RAW + 8 * r:P:32, :].bitcast(I32))
 
         def p_pass(bank, a, x, u):
             sj = slice(x * HALF + u * JT, x * HALF + (u + 1) * JT)
@@ -252,7 +252,7 @@ def tile_list_cubic_recall_weights_kernel(
         gather_v(0, 0, 2 * TILES)
         tab2_w = held("tab2_w", [P, T2], U32, "tab_w0")
         load_words(tab2_w, tab2_words[0])
-        v2_gs01 = gather_v2_scales(held("v2_gs01", [P, 2 * KP], U8), 0, 2)
+        v2_gs = gather_v2_scales(held("v2_gs", [P, S2], U8), 0, GROUPS)
 
         a_banks = [new_bank(u) for u in range(TILES)]
         p_banks = [new_bank(TILES + u) for u in range(TILES)]
@@ -270,9 +270,8 @@ def tile_list_cubic_recall_weights_kernel(
         for piece in (1, 2):
             nc.scalar.copy(*wg_views(1, wg1_raw[piece], (piece + 1) * P // 4))
         quantize_wg(1)
-        deal_v2_scales(held("v2_ds01", [P, 2 * KP], U8, "wp_raw"), v2_gs01, 0, 2)
-        gather_v(1, TILES, 2 * TILES, 4096 + 1024)
-        v2_gs2 = gather_v2_scales(placed("v2_gs2", [P, KP], U8, 4096 + 3072), 2, 3)
+        deal_v2_scales(placed("v2_ds", [P, S2], U8, 4096), v2_gs, 0, GROUPS)
+        gather_v(1, TILES, 2 * TILES, 4096 + S2)
 
         def gate_on_gpsimd(p_sb, a_bank, x, u):
             sig = woven(held("sig%d%d" % (x, u), [P, JT * PACK], F32), a_bank, ACT.Sigmoid)
@@ -295,7 +294,6 @@ def tile_list_cubic_recall_weights_kernel(
             a_pass(a_banks[u], 1, 0, u)
             if u == 0:
                 gate_on_gpsimd(p_sb, a_banks[u], 0, u)
-                deal_v2_scales(placed("v2_ds2", [P, KP], U8, 0), v2_gs2, 2, 3)
             else:
                 p_pass(p_banks[u], 1, 0, u)
                 gate(p_banks[u], a_banks[u], 0, u)
@@ -344,7 +342,14 @@ def tile_list_cubic_recall_weights_kernel(
                 product(part[:, t, :], g, t, m[:, c0:c1], sq[:, c0:c1])
             nc.sync.dma_start(y_rows[g, :, :, x * HALF + c0:x * HALF + c1], part[:])
             round_on_scalar(g, x, c0, c1, part[:])
-        quantize_behind(len(units) - 1)
-        for g, x in units[-2:]:
-            quantize_y(g, x * HALF, y_bf[g, x])
+        pair_w = held("pair_w", [P, 2, HALF], U32, "sq_hold%d%d2" % units[-1])
+        for n, (g, x) in enumerate(units[-3:-1]):
+            nc.vector.quantize_mx(out=pair_w[:, n, :].bitcast(FP8X4), scales=y_s[g][:, x * HALF:(x + 1) * HALF],
+                                  in_=y_bf[g, x][:])
+        rows = out_1.rearrange("g p m t -> (g p m t)").bitcast(I32).rearrange("(c w) -> c w", w=HALF)
+        first, apart = 2 * P + 1, 2 * P - 1
+        both = rows[first:first + 2 * apart, :].rearrange("(n c) w -> c n w", n=2)
+        nc.sync.dma_start(both[0:apart:2], pair_w[:].bitcast(I32))
+        g, x = units[-1]
+        quantize_y(g, x * HALF, y_bf[g, x])
         store_last_scales()

@@ -28,7 +28,7 @@ TILES = HALF // JT
 GROUPS = S2 // KP
 QUADS = (0, 2, 1, 3)
 PER_COL = 16
-Y_ON_GPSIMD = (320, 416, 416, 448)
+Y_ON_GPSIMD = (416, 416, 416, 416, 448)
 V2_BASE = 8
 V2_RAW = 4
 AT_SIG3 = 9216
@@ -64,14 +64,14 @@ def tile_list_cubic_recall_weights_kernel(
         v_w = {}
         v_gs = held("v_gs", [P, S], U8)
         v_s = held("v_s", [P, PASSES, S], U8)
-        v2_s = held("v2_s", [P, S2], U8)
+        v2_s01 = held("v2_s01", [P, 2 * KP], U8)
+        v2_s2 = held("v2_s2", [P, KP], U8)
+        v2_s = [v2_s01[:, :KP], v2_s01[:, KP:], v2_s2[:]]
         v2_w = [None] * GROUPS
         h_bf = [held("h_bf0", [P, HALF * PACK], BF16), None]
         h_w = [None] * HALVES
         h_s = [held("h_s%d" % x, [P, HALF], U8) for x in range(HALVES)]
-        y_s0 = held("y_s0", [P, S], U8)
-        y_s12 = held("y_s12", [P, S], U8)
-        y_s = [y_s0[:], y_s12[:], y_s12[4:P, :]]
+        y_s = [held("y_s%d" % x, [P, GROUPS, HALF], U8) for x in range(HALVES)]
         tab_w = [held("tab_w0", [P, T], U32), None]
         wg0_raw = held("wg0_raw", [P, PACK, H], F32)
 
@@ -80,7 +80,8 @@ def tile_list_cubic_recall_weights_kernel(
         nc.vector.memset(tab_s[32:64, :].bitcast(I32), 0)
         nc.gpsimd.memset(tab_s[64:P, :].bitcast(I32), 0)
         nc.gpsimd.memset(v_s[:].rearrange("p a c -> p (a c)").bitcast(I32), 0)
-        nc.gpsimd.memset(v2_s[:].bitcast(I32), 0)
+        nc.gpsimd.memset(v2_s01[:].bitcast(I32), 0)
+        nc.gpsimd.memset(v2_s2[:].bitcast(I32), 0)
 
         warm = held("warm", [P, 2], F32)
         nc.gpsimd.memset(warm[:, 0:1], 0.0)
@@ -134,11 +135,11 @@ def tile_list_cubic_recall_weights_kernel(
             nc.vector.tensor_copy(tile[:], tab2_s[:].indirect(offs2_t[:, g0 * cols:g1 * cols]))
             return tile
 
-        def deal_v2_scales(dealt, gathered, g0, g1):
+        def deal_v2_scales(plane, dealt, gathered):
             nc.vector.tensor_copy(dealt[:].rearrange("p (g t m) -> p t g m", t=PACK, m=P),
                                   gathered[:].rearrange("p (g m t) -> p t g m", t=PACK, m=P))
             for r in range(4):
-                nc.sync.dma_start(v2_s[V2_BASE + r:P:32, g0 * KP:g1 * KP].bitcast(I32),
+                nc.sync.dma_start(plane[V2_BASE + r:P:32, :].bitcast(I32),
                                   dealt[V2_RAW + 8 * r:P:32, :].bitcast(I32))
 
         def p_pass(bank, a, x, u):
@@ -180,15 +181,14 @@ def tile_list_cubic_recall_weights_kernel(
 
         y_rows = out_0.rearrange("(g p t) j -> g p t j", p=P, t=PACK)
 
-        units = [(0, 0), (1, 0), (0, 1), (1, 1), (2, 0), (2, 1)]
+        units = [(g, x) for x in range(HALVES) for g in range(GROUPS)]
         y = {unit: held("y%d%d" % unit, [P, PACK, HALF], F32) for unit in units[:-1]}
-        y_bf = {unit: held("y_bf%d%d" % unit, [P, HALF * PACK], BF16) for unit in units[1:]}
+        y_bf = {unit: held("y_bf%d%d" % unit, [P, HALF * PACK], BF16) for unit in units}
 
         def square(g, x, t, bank):
             m = new_bank(bank)[:].rearrange("p t j -> p (t j)")
-            cols = slice(g * KP + P * t, g * KP + P * (t + 1))
             nc.tensor.matmul_mx(
-                out=m, lhsT=v2_w[g][:, P * t:P * (t + 1)].bitcast(FP8X4), lhsT_scale=v2_s[V2_BASE:P, cols],
+                out=m, lhsT=v2_w[g][:, P * t:P * (t + 1)].bitcast(FP8X4), lhsT_scale=v2_s[g][V2_BASE:P, P * t:P * (t + 1)],
                 rhs=h_w[x][:].bitcast(FP8X4), rhs_scale=h_s[x][:], start=True, stop=True)
             if t == PACK - 2:
                 sq = held("sq_hold%d%d%d" % (g, x, t), [P, HALF], F32)
@@ -218,21 +218,18 @@ def tile_list_cubic_recall_weights_kernel(
             nc.scalar.copy(y_bf[g, x][:, c0 * PACK:c1 * PACK].rearrange("p (c i t) -> p c t i", i=2, t=PACK),
                            src.rearrange("p t (c i) -> p c t i", i=2))
 
-        def quantize_y(g, first, rounded, tag=""):
-            width = rounded.shape[1] // PACK
-            y_w = held("y_w%d_%d" % (g, first), [P, width], U32, tag)
-            nc.vector.quantize_mx(out=y_w[:].bitcast(FP8X4), scales=y_s[g][:, first:first + width], in_=rounded[:])
-            words = out_1[g].rearrange("p m t -> p (m t)").bitcast(I32)
-            nc.sync.dma_start(words[:, first:first + width], y_w[:].bitcast(I32))
+        word_rows = out_1.rearrange("g p m t -> p g (m t)").bitcast(I32)
 
-        def store_first_scales():
+        def quantize_y(x, g0, g1, tag=""):
+            y_w = held("y_w%d%d" % (g0, x), [P, g1 - g0, HALF], U32, tag)
+            for g in range(g0, g1):
+                nc.vector.quantize_mx(out=y_w[:, g - g0, :].bitcast(FP8X4), scales=y_s[x][:, g, :], in_=y_bf[g, x][:])
+            nc.sync.dma_start(word_rows[:, g0:g1, x * HALF:(x + 1) * HALF], y_w[:].bitcast(I32))
+
+        def store_scales(x):
             for r in range(4):
-                nc.sync.dma_start(out_2[0, r:16:4, :].bitcast(I32), y_s0[r:P:32, :].bitcast(I32))
-
-        def store_last_scales():
-            for q in QUADS:
-                nc.sync.dma_start(
-                    out_2[1:GROUPS, 4 * q:4 * q + 4, :].bitcast(I32), y_s12[32 * q:32 * q + 8, :].bitcast(I32))
+                nc.sync.dma_start(out_2[:, r:16:4, x * HALF:(x + 1) * HALF].rearrange("g q c -> q g c").bitcast(I32),
+                                  y_s[x][r:P:32].bitcast(I32))
 
         nc.vector.tensor_copy(v_gs[:], tab_s[:].indirect(offs_t[:]))
         for q in QUADS:
@@ -252,7 +249,7 @@ def tile_list_cubic_recall_weights_kernel(
         gather_v(0, 0, 2 * TILES)
         tab2_w = held("tab2_w", [P, T2], U32, "tab_w0")
         load_words(tab2_w, tab2_words[0])
-        v2_gs = gather_v2_scales(held("v2_gs", [P, S2], U8), 0, GROUPS)
+        v2_gs01 = gather_v2_scales(held("v2_gs01", [P, 2 * KP], U8), 0, 2)
 
         a_banks = [new_bank(u) for u in range(TILES)]
         p_banks = [new_bank(TILES + u) for u in range(TILES)]
@@ -265,13 +262,14 @@ def tile_list_cubic_recall_weights_kernel(
         for u in range(TILES):
             a_pass(a_banks[u], 0, 0, u)
         gather_v(1, 0, TILES)
+        gather_v(1, TILES, 2 * TILES)
         p_pass(p_banks[0], 1, 0, 0)
         nc.scalar.copy(*wg_views(1, wg1_raw[0], 0))
         for piece in (1, 2):
             nc.scalar.copy(*wg_views(1, wg1_raw[piece], (piece + 1) * P // 4))
         quantize_wg(1)
-        deal_v2_scales(placed("v2_ds", [P, S2], U8, 4096), v2_gs, 0, GROUPS)
-        gather_v(1, TILES, 2 * TILES, 4096 + S2)
+        deal_v2_scales(v2_s01, placed("v2_ds01", [P, 2 * KP], U8, 4096), v2_gs01)
+        v2_gs2 = gather_v2_scales(placed("v2_gs2", [P, KP], U8, 4096 + 2 * KP), 2, 3)
 
         def gate_on_gpsimd(p_sb, a_bank, x, u):
             sig = woven(held("sig%d%d" % (x, u), [P, JT * PACK], F32), a_bank, ACT.Sigmoid)
@@ -297,9 +295,10 @@ def tile_list_cubic_recall_weights_kernel(
             else:
                 p_pass(p_banks[u], 1, 0, u)
                 gate(p_banks[u], a_banks[u], 0, u)
+        deal_v2_scales(v2_s2, placed("v2_ds2", [P, KP], U8, AT_SIG3 + 512), v2_gs2)
         quantize_h(0)
         h_bf[1] = held("h_bf1", [P, HALF * PACK], BF16, "h_bf0")
-        gather_v2_words(0, 1, AT_SIG3 - 1024)
+        gather_v2_words(0, 1, AT_SIG3 - 1536)
         gather_v2_words(1, 3, AT_SIG3 + 1024)
         late_tile_on_gpsimd(0, (4, 0))
         late_tile_on_gpsimd(1, (1, 2))
@@ -310,27 +309,23 @@ def tile_list_cubic_recall_weights_kernel(
 
         def quantize_behind(n):
             g, x = units[n - 2]
-            rounded = y_bf[g, x]
-            quantize_y(g, (x + 1) * HALF - rounded.shape[1] // PACK, rounded, "sq_hold%d%d2" % units[n])
+            quantize_y(x, g, g + 1, "sq_hold%d%d2" % units[n])
 
         def round_rest(n):
-            share = Y_ON_GPSIMD[n - 1]
+            share = Y_ON_GPSIMD[n]
             round_on_scalar(*units[n], share, HALF, y[units[n]][:, :, share:])
 
         for n, (g, x) in enumerate(units[:-1]):
             cube(g, x, banks[n], 2 if n else 1)
-            if n == 0:
-                quantize_h(1, "sq_hold002")
-                y_bf[g, x] = held("y_bf00", [P, HALF * PACK], BF16, "h_bf0")
-                round_on_gpsimd(g, x, 0, HALF, y_bf[g, x][:])
-                continue
+            if n == 1:
+                quantize_h(1, "sq_hold%d%d2" % units[n])
             if n >= 2:
                 quantize_behind(n)
             if n == 4:
-                store_first_scales()
-            share = Y_ON_GPSIMD[n - 1]
+                store_scales(0)
+            share = Y_ON_GPSIMD[n]
             round_on_gpsimd(g, x, 0, share, y_bf[g, x][:, :share * PACK])
-            if n >= 2:
+            if n >= 1:
                 round_rest(n - 1)
         g, x = units[-1]
         squares = [square(g, x, t, banks[-1][t]) for t in range(PACK)]
@@ -342,14 +337,6 @@ def tile_list_cubic_recall_weights_kernel(
                 product(part[:, t, :], g, t, m[:, c0:c1], sq[:, c0:c1])
             nc.sync.dma_start(y_rows[g, :, :, x * HALF + c0:x * HALF + c1], part[:])
             round_on_scalar(g, x, c0, c1, part[:])
-        pair_w = held("pair_w", [P, 2, HALF], U32, "sq_hold%d%d2" % units[-1])
-        for n, (g, x) in enumerate(units[-3:-1]):
-            nc.vector.quantize_mx(out=pair_w[:, n, :].bitcast(FP8X4), scales=y_s[g][:, x * HALF:(x + 1) * HALF],
-                                  in_=y_bf[g, x][:])
-        rows = out_1.rearrange("g p m t -> (g p m t)").bitcast(I32).rearrange("(c w) -> c w", w=HALF)
-        first, apart = 2 * P + 1, 2 * P - 1
-        both = rows[first:first + 2 * apart, :].rearrange("(n c) w -> c n w", n=2)
-        nc.sync.dma_start(both[0:apart:2], pair_w[:].bitcast(I32))
-        g, x = units[-1]
-        quantize_y(g, x * HALF, y_bf[g, x])
-        store_last_scales()
+        quantize_y(x, 0, g, "sq_hold%d%d2" % units[-1])
+        quantize_y(x, g, GROUPS)
+        store_scales(x)

@@ -29,7 +29,6 @@ GROUPS = S2 // KP
 QUADS = (0, 2, 1, 3)
 PER_COL = 16
 Y_ON_GPSIMD = (416, 416, 416, 416, 448)
-V2_BASE = 8
 V2_RAW = 4
 AT_SIG3 = 9216
 
@@ -139,7 +138,7 @@ def tile_list_cubic_recall_weights_kernel(
             nc.vector.tensor_copy(dealt[:].rearrange("p (g t m) -> p t g m", t=PACK, m=P),
                                   gathered[:].rearrange("p (g m t) -> p t g m", t=PACK, m=P))
             for r in range(4):
-                nc.sync.dma_start(plane[V2_BASE + r:P:32, :].bitcast(I32),
+                nc.sync.dma_start(plane[r:P:32, :].bitcast(I32),
                                   dealt[V2_RAW + 8 * r:P:32, :].bitcast(I32))
 
         def p_pass(bank, a, x, u):
@@ -188,7 +187,7 @@ def tile_list_cubic_recall_weights_kernel(
         def square(g, x, t, bank):
             m = new_bank(bank)[:].rearrange("p t j -> p (t j)")
             nc.tensor.matmul_mx(
-                out=m, lhsT=v2_w[g][:, P * t:P * (t + 1)].bitcast(FP8X4), lhsT_scale=v2_s[g][V2_BASE:P, P * t:P * (t + 1)],
+                out=m, lhsT=v2_w[g][:, P * t:P * (t + 1)].bitcast(FP8X4), lhsT_scale=v2_s[g][:, P * t:P * (t + 1)],
                 rhs=h_w[x][:].bitcast(FP8X4), rhs_scale=h_s[x][:], start=True, stop=True)
             if t == PACK - 2:
                 sq = held("sq_hold%d%d%d" % (g, x, t), [P, HALF], F32)

@@ -31,6 +31,8 @@ PER_COL = 16
 Y_ON_GPSIMD = (416, 416, 416, 416, 448)
 V2_RAW = 4
 AT_SIG3 = 9216
+AT_TAB1 = 20480
+WG1_CUTS = (0, 128, 320, 512)
 
 
 def tile_list_cubic_recall_weights_kernel(
@@ -52,7 +54,7 @@ def tile_list_cubic_recall_weights_kernel(
 
         offs_t = keep.tile([P, S // PER_COL], U16, name="offs_t")
         offs2_t = keep.tile([P, S2 // PER_COL], U16, name="offs2_t")
-        tab_s = held("tab_s", [P, T], U8)
+        tab_s = placed("tab_s", [P, T], U8, AT_TAB1 - 1024)
         tab2_s = held("tab2_s", [P, T2], U8)
         wp_raw = held("wp_raw", [P, PASSES, 2 * H], U8)
         wp_raw_s = placed("wp_raw_s", [P, PASSES, H], U8, 1024)
@@ -102,8 +104,6 @@ def tile_list_cubic_recall_weights_kernel(
         nc.sync.dma_start(offs2_t[:], offs2)
         nc.sync.dma_start(tab2_s[V2_RAW:P:8, :].bitcast(I32), tab2_scales[0].bitcast(I32))
         load_wg(wg0_raw, 0, 0, H)
-        wg1_raw = [held("wg1_raw0", [P, PACK, H // 2], F32), None, None]
-        load_wg(wg1_raw[0], 1, 0, H // 2)
 
         def gather_v(a, u0, u1, at=None):
             cols = JT // PER_COL
@@ -234,17 +234,19 @@ def tile_list_cubic_recall_weights_kernel(
         for q in QUADS:
             nc.sync.dma_start(v_s[32 * q:32 * q + 4].rearrange("p a c -> p (a c)").bitcast(I32),
                               v_gs[8 * q:8 * q + 8, :].bitcast(I32))
-        tab_w[1] = held("tab_w1", [P, T], U32, "tab_s")
+        wg1_raw = [placed("wg1_raw0", [P, PACK, WG1_CUTS[1]], F32, AT_TAB1 - 16 * WG1_CUTS[1]), None, None]
+        load_wg(wg1_raw[0], 1, 0, WG1_CUTS[1])
+        tab_w[1] = placed("tab_w1", [P, T], U32, AT_TAB1)
         load_words(tab_w[1], tab_words[1])
-        nc.vector.tensor_copy(wp_w[:].bitcast(U16).rearrange("p a (t m) -> p a t m", t=PACK),
+        nc.scalar.copy(wp_w[:].bitcast(U16).rearrange("p a (t m) -> p a t m", t=PACK),
                               wp_raw[:].bitcast(U16).rearrange("p a (m t) -> p a t m", t=PACK))
         wp_s = held("wp_s", [P, PASSES, H], U8)
         nc.vector.tensor_copy(wp_s[:].rearrange("p a (t m) -> p a t m", t=PACK),
                               wp_raw_s[:].rearrange("p a (m t) -> p a t m", t=PACK))
-        wg1_raw[1] = held("wg1_raw1", [P, PACK, H // 4], F32, "wp_raw")
-        wg1_raw[2] = placed("wg1_raw2", [P, PACK, H // 4], F32, 1024)
+        wg1_raw[1] = held("wg1_raw1", [P, PACK, WG1_CUTS[2] - WG1_CUTS[1]], F32, "wp_raw")
+        wg1_raw[2] = placed("wg1_raw2", [P, PACK, WG1_CUTS[3] - WG1_CUTS[2]], F32, 1024)
         for piece in (1, 2):
-            load_wg(wg1_raw[piece], 1, (piece + 1) * H // 4, (piece + 2) * H // 4)
+            load_wg(wg1_raw[piece], 1, WG1_CUTS[piece], WG1_CUTS[piece + 1])
         gather_v(0, 0, 2 * TILES)
         tab2_w = held("tab2_w", [P, T2], U32, "tab_w0")
         load_words(tab2_w, tab2_words[0])
@@ -264,9 +266,13 @@ def tile_list_cubic_recall_weights_kernel(
         gather_v(1, TILES, 2 * TILES)
         p_pass(p_banks[0], 1, 0, 0)
         nc.scalar.copy(*wg_views(1, wg1_raw[0], 0))
-        for piece in (1, 2):
-            nc.scalar.copy(*wg_views(1, wg1_raw[piece], (piece + 1) * P // 4))
-        quantize_wg(1)
+        nc.scalar.copy(*wg_views(1, wg1_raw[1], WG1_CUTS[1] // PACK))
+        dst, src = wg_views(1, wg1_raw[2], WG1_CUTS[2] // PACK)
+        for u in range(2):
+            nc.scalar.copy(dst[:, u], src[:, u])
+            cols = slice(u * H // 2, (u + 1) * H // 2)
+            nc.vector.quantize_mx(out=wg_w[1][:, cols].bitcast(FP8X4), scales=wg_s[1][:, cols],
+                                  in_=wg_bf[1][:, u * 2 * H:(u + 1) * 2 * H])
         deal_v2_scales(v2_s01, placed("v2_ds01", [P, 2 * KP], U8, 4096), v2_gs01)
         v2_gs2 = gather_v2_scales(placed("v2_gs2", [P, KP], U8, 4096 + 2 * KP), 2, 3)
 

@@ -202,6 +202,18 @@ def tile_list_cubic_recall_weights_kernel(
         def store_y(g, x, t0, t1):
             nc.sync.dma_start(y_rows[g, :, t0:t1, x * HALF:(x + 1) * HALF], y[g, x][:, t0:t1, :])
 
+        def first_cube(banks):
+            g, x = units[0]
+            for t in (0, 3, 1, 2):
+                m, sq = square(g, x, t, banks[t])
+                if t == PACK - 1:
+                    scaled = held("scaled", [P, HALF], F32)
+                    nc.scalar.activation(scaled[:], m, ACT.Copy, scale=strength_t[:, g, t:t + 1])
+                    nc.gpsimd.tensor_tensor(y[g, x][:, t, :], scaled[:], sq[:], MULT)
+                else:
+                    product(y[g, x][:, t, :], g, t, m, sq[:])
+                store_y(g, x, t, t + 1)
+
         def cube(g, x, banks, per_store):
             for t in range(PACK):
                 m, sq = square(g, x, t, banks[t])
@@ -303,9 +315,10 @@ def tile_list_cubic_recall_weights_kernel(
         deal_v2_scales(v2_s2, placed("v2_ds2", [P, KP], U8, AT_SIG3 + 512), v2_gs2)
         quantize_h(0)
         h_bf[1] = held("h_bf1", [P, HALF * PACK], BF16, "h_bf0")
+        late_a = both_passes(a_pass, new_bank(4), 0)
+        gate(both_passes(p_pass, new_bank(0), 0), late_a, 1, 0)
         gather_v2_words(0, 1, AT_SIG3 - 1536)
         gather_v2_words(1, 3, AT_SIG3 + 1024)
-        late_tile_on_gpsimd(0, (4, 0))
         late_tile_on_gpsimd(1, (1, 2))
         late_tile_on_gpsimd(2, (5, 3))
         late_tile_on_gpsimd(3, (6, 7))
@@ -321,7 +334,10 @@ def tile_list_cubic_recall_weights_kernel(
             round_on_scalar(*units[n], share, HALF, y[units[n]][:, :, share:])
 
         for n, (g, x) in enumerate(units[:-1]):
-            cube(g, x, banks[n], 2 if n else 1)
+            if n:
+                cube(g, x, banks[n], 2)
+            else:
+                first_cube(banks[n])
             if n == 1:
                 quantize_h(1, "sq_hold%d%d2" % units[n])
             if n >= 2:

from contextlib import ExitStack

import concourse.mybir as mybir

K, H, T, S, T2, S2 = 1024, 512, 2048, 1024, 4096, 1536
FLOPS = 2 * 2 * K * H * S + 2 * H * S2 * S

F32 = mybir.dt.float32
BF16 = mybir.dt.bfloat16
I32 = mybir.dt.int32
U32 = mybir.dt.uint32
U16 = mybir.dt.uint16
U8 = mybir.dt.uint8
FP8X4 = mybir.dt.float8_e4m3fn_x4
FP4X4 = mybir.dt.float4_e2m1fn_x4
ACT = mybir.ActivationFunctionType
MULT = mybir.AluOpType.mult
ADD = mybir.AluOpType.add

P = 128
PACK = 4
KP = P * PACK
PASSES = K // KP
HALF = 512
HALVES = S // HALF
JT = 128
TILES = HALF // JT
GROUPS = S2 // KP
QUADS = (0, 2, 1, 3)
PER_COL = 16
Y_ON_GPSIMD = (416, 416, 416, 416, 448)
V2_RAW = 4
AT_SIG3 = 9216
AT_TAB1 = 20480
WG1_CUTS = (0, 128, 320, 512)


def tile_list_cubic_recall_weights_kernel(
    tc, tab_words, tab_scales, tab2_words, tab2_scales, wp_words, wp_scales, wg, strength, offs, offs2,
    out_0, out_1, out_2,
):
    nc = tc.nc
    with ExitStack() as ctx:
        keep = ctx.enter_context(tc.tile_pool(name="keep", bufs=1))
        shared = ctx.enter_context(tc.tile_pool(name="shared", bufs=1))
        ring = ctx.enter_context(tc.tile_pool(name="ring", bufs=6))
        psum = ctx.enter_context(tc.psum_pool(name="psum", bufs=1))

        def held(name, shape, dtype, tag=""):
            return keep.tile(shape, dtype, name=name, tag=tag or name, align_bytes=64)

        def placed(name, shape, dtype, at):
            return shared.tile(shape, dtype, name=name, tag=name, align_bytes=64, offset=at)

        offs_t = keep.tile([P, S // PER_COL], U16, name="offs_t")
        offs2_t = keep.tile([P, S2 // PER_COL], U16, name="offs2_t")
        tab_s = placed("tab_s", [P, T], U8, AT_TAB1 - 1024)
        tab2_s = held("tab2_s", [P, T2], U8)
        wp_raw = held("wp_raw", [P, PASSES, 2 * H], U8)
        wp_raw_s = placed("wp_raw_s", [P, PASSES, H], U8, 1024)
        wp_w = held("wp_w", [P, PASSES, 2 * H], U8)
        wg_bf = [held("wg_bf0", [P, H * PACK], BF16), placed("wg_bf1", [P, H * PACK], BF16, 4096)]
        wg_w = [held("wg_w%d" % a, [P, H], U32) for a in range(PASSES)]
        wg_s = [held("wg_s%d" % a, [P, H], U8) for a in range(PASSES)]
        v_w = {}
        v_gs = held("v_gs", [P, S], U8)
        v_s = held("v_s", [P, PASSES, S], U8)
        v2_s01 = held("v2_s01", [P, 2 * KP], U8)
        v2_s2 = held("v2_s2", [P, KP], U8)
        v2_s = [v2_s01[:, :KP], v2_s01[:, KP:], v2_s2[:]]
        v2_w = [None] * GROUPS
        h_bf = [held("h_bf0", [P, HALF * PACK], BF16), None]
        h_w = [None] * HALVES
        h_s = [held("h_s%d" % x, [P, HALF], U8) for x in range(HALVES)]
        y_s = [held("y_s%d" % x, [P, GROUPS, HALF], U8) for x in range(HALVES)]
        tab_w = [held("tab_w0", [P, T], U32), None]
        wg0_raw = held("wg0_raw", [P, PACK, H], F32)

        nc.gpsimd.memset(wp_raw_s[:].rearrange("p a c -> p (a c)").bitcast(I32), 0)
        nc.vector.memset(tab2_s[:].bitcast(I32), 0)
        nc.vector.memset(tab_s[32:64, :].bitcast(I32), 0)
        nc.gpsimd.memset(tab_s[64:P, :].bitcast(I32), 0)
        nc.gpsimd.memset(v_s[:].rearrange("p a c -> p (a c)").bitcast(I32), 0)
        nc.gpsimd.memset(v2_s01[:].bitcast(I32), 0)
        nc.gpsimd.memset(v2_s2[:].bitcast(I32), 0)

        warm = held("warm", [P, 2], F32)
        nc.gpsimd.memset(warm[:, 0:1], 0.0)
        nc.scalar.activation(warm[:, 1:2], warm[:, 0:1], ACT.Sigmoid)

        def load_words(tile, words):
            nc.sync.dma_start(tile[:].bitcast(I32), words.rearrange("p t i -> p (t i)").bitcast(I32))

        def load_wg(tile, a, c0, c1):
            nc.sync.dma_start(tile[:], wg[a * KP:(a + 1) * KP, c0:c1].rearrange("(p j) c -> p j c", j=PACK))

        nc.sync.dma_start(offs_t[:], offs)
        nc.sync.dma_start(tab_s[0:32, :].bitcast(I32), tab_scales.rearrange("a q c -> q a c").bitcast(I32))
        nc.sync.dma_start(wp_raw[:].bitcast(I32), wp_words.rearrange("a p c -> p a c").bitcast(I32))
        for r in range(4):
            nc.sync.dma_start(wp_raw_s[r:P:32].bitcast(I32),
                              wp_scales[:, r:16:4, :].rearrange("a q c -> q a c").bitcast(I32))
        load_words(tab_w[0], tab_words[0])
        nc.sync.dma_start(offs2_t[:], offs2)
        nc.sync.dma_start(tab2_s[V2_RAW:P:8, :].bitcast(I32), tab2_scales[0].bitcast(I32))
        load_wg(wg0_raw, 0, 0, H)

        def gather_v(a, u0, u1, at=None):
            cols = JT // PER_COL
            name, shape = "v_w%d%d" % (a, u0), [P, JT * (u1 - u0)]
            tile = held(name, shape, U32) if at is None else placed(name, shape, U32, at)
            nc.vector.tensor_copy(tile[:], tab_w[a][:].indirect(offs_t[:, u0 * cols:u1 * cols]))
            for u in range(u0, u1):
                v_w[a, u] = tile[:, (u - u0) * JT:(u - u0 + 1) * JT]

        def wg_views(a, raw, m0):
            dst = wg_bf[a][:].rearrange("p (u e m j) -> p u m j e", u=2, e=2, j=PACK)
            src = raw[:].rearrange("p j (m u e) -> p u m j e", u=2, e=2)
            return dst[:, :, m0:m0 + src.shape[2]], src

        def quantize_wg(a):
            nc.vector.quantize_mx(out=wg_w[a][:].bitcast(FP8X4), scales=wg_s[a][:], in_=wg_bf[a][:])

        def gather_v2_words(g0, g1, at):
            cols = KP // PER_COL
            tile = placed("v2_w%d" % g0, [P, (g1 - g0) * KP], U32, at)
            nc.vector.tensor_copy(tile[:].rearrange("p (g t m) -> p g m t", t=PACK, m=P),
                                  tab2_w[:].indirect(offs2_t[:, g0 * cols:g1 * cols]))
            for g in range(g0, g1):
                v2_w[g] = tile[:, (g - g0) * KP:(g - g0 + 1) * KP]

        def gather_v2_scales(tile, g0, g1):
            cols = KP // PER_COL
            nc.vector.tensor_copy(tile[:], tab2_s[:].indirect(offs2_t[:, g0 * cols:g1 * cols]))
            return tile

        def deal_v2_scales(plane, dealt, gathered):
            nc.vector.tensor_copy(dealt[:].rearrange("p (g t m) -> p t g m", t=PACK, m=P),
                                  gathered[:].rearrange("p (g m t) -> p t g m", t=PACK, m=P))
            for r in range(4):
                nc.sync.dma_start(plane[r:P:32, :].bitcast(I32),
                                  dealt[V2_RAW + 8 * r:P:32, :].bitcast(I32))

        def p_pass(bank, a, x, u):
            sj = slice(x * HALF + u * JT, x * HALF + (u + 1) * JT)
            for t in range(PACK):
                nc.tensor.matmul_mx(
                    out=bank[:, t, :],
                    lhsT=wp_w[:, a, 2 * P * t:2 * P * (t + 1)].bitcast(FP4X4), lhsT_scale=wp_s[:, a, P * t:P * (t + 1)],
                    rhs=v_w[a, x * TILES + u].bitcast(FP8X4), rhs_scale=v_s[:, a, sj],
                    start=(a == 0 and t == 0), stop=(a == PASSES - 1 and t == PACK - 1))

        def a_pass(bank, a, x, u):
            sj = slice(x * HALF + u * JT, x * HALF + (u + 1) * JT)
            for t in range(PACK):
                nc.tensor.matmul_mx(
                    out=bank[:, t, :],
                    lhsT=wg_w[a][:, P * t:P * (t + 1)].bitcast(FP8X4), lhsT_scale=wg_s[a][:, P * t:P * (t + 1)],
                    rhs=v_w[a, x * TILES + u].bitcast(FP8X4), rhs_scale=v_s[:, a, sj],
                    start=(a == 0 and t == 0), stop=(a == PASSES - 1 and t == PACK - 1))

        def gate(p_bank, a_bank, x, u):
            name, shape = "sig%d%d" % (x, u), [P, PACK, JT]
            sig = placed(name, shape, F32, AT_SIG3) if u == TILES - 1 else held(name, shape, F32)
            nc.scalar.activation(sig[:], a_bank[:], ACT.Sigmoid)
            h_out = h_bf[x][:, u * JT * PACK:(u + 1) * JT * PACK].rearrange("p (c i t) -> p c t i", i=2, t=PACK)
            nc.vector.tensor_tensor(h_out, p_bank[:].rearrange("p t (c i) -> p c t i", i=2),
                                    sig[:].rearrange("p t (c i) -> p c t i", i=2), MULT)

        def woven(tile, bank, func):
            nc.scalar.activation(tile[:].rearrange("p (j t) -> p j t", t=PACK), bank[:].rearrange("p t j -> p j t"), func)
            return tile

        def quantize_h(x, tag=""):
            h_w[x] = held("h_w%d" % x, [P, HALF], U32, tag)
            nc.vector.quantize_mx(out=h_w[x][:].bitcast(FP8X4), scales=h_s[x][:], in_=h_bf[x][:])

        def new_bank(b):
            return psum.tile([P, PACK, JT], F32, name="bank%d" % b)

        y_rows = out_0.rearrange("(g p t) j -> g p t j", p=P, t=PACK)

        units = [(g, x) for x in range(HALVES) for g in range(GROUPS)]
        y = {unit: held("y%d%d" % unit, [P, PACK, HALF], F32) for unit in units[:-1]}
        y_bf = {unit: held("y_bf%d%d" % unit, [P, HALF * PACK], BF16) for unit in units}

        def square(g, x, t, bank):
            m = new_bank(bank)[:].rearrange("p t j -> p (t j)")
            nc.tensor.matmul_mx(
                out=m, lhsT=v2_w[g][:, P * t:P * (t + 1)].bitcast(FP8X4), lhsT_scale=v2_s[g][:, P * t:P * (t + 1)],
                rhs=h_w[x][:].bitcast(FP8X4), rhs_scale=h_s[x][:], start=True, stop=True)
            if t == PACK - 2:
                sq = held("sq_hold%d%d%d" % (g, x, t), [P, HALF], F32)
            else:
                sq = ring.tile([P, HALF], F32, name="sq")
            nc.scalar.activation(sq[:], m, ACT.Square)
            return m, sq

        def product(out, g, t, m, sq):
            nc.vector.scalar_tensor_tensor(out, m, strength_t[:, g, t:t + 1], sq, MULT, MULT)

        def store_y(g, x, t0, t1):
            nc.sync.dma_start(y_rows[g, :, t0:t1, x * HALF:(x + 1) * HALF], y[g, x][:, t0:t1, :])

        def first_cube(banks):
            g, x = units[0]
            for t in (0, 3, 1, 2):
                m, sq = square(g, x, t, banks[t])
                if t == PACK - 1:
                    scaled = held("scaled", [P, HALF], F32)
                    nc.scalar.activation(scaled[:], m, ACT.Copy, scale=strength_t[:, g, t:t + 1])
                    nc.gpsimd.tensor_tensor(y[g, x][:, t, :], scaled[:], sq[:], MULT)
                else:
                    product(y[g, x][:, t, :], g, t, m, sq[:])
                store_y(g, x, t, t + 1)

        def cube(g, x, banks, per_store):
            for t in range(PACK):
                m, sq = square(g, x, t, banks[t])
                product(y[g, x][:, t, :], g, t, m, sq[:])
                if (t + 1) % per_store == 0:
                    store_y(g, x, t + 1 - per_store, t + 1)

        def round_on_gpsimd(g, x, c0, c1, dst):
            nc.gpsimd.tensor_scalar(dst.rearrange("p (j t) -> p j t", t=PACK),
                                    y[g, x][:, :, c0:c1].rearrange("p t j -> p j t"), 1.0, -0.0, MULT, ADD)

        def round_on_scalar(g, x, c0, c1, src):
            nc.scalar.copy(y_bf[g, x][:, c0 * PACK:c1 * PACK].rearrange("p (c i t) -> p c t i", i=2, t=PACK),
                           src.rearrange("p t (c i) -> p c t i", i=2))

        word_rows = out_1.rearrange("g p m t -> p g (m t)").bitcast(I32)

        def quantize_y(x, g0, g1, tag=""):
            y_w = held("y_w%d%d" % (g0, x), [P, g1 - g0, HALF], U32, tag)
            for g in range(g0, g1):
                nc.vector.quantize_mx(out=y_w[:, g - g0, :].bitcast(FP8X4), scales=y_s[x][:, g, :], in_=y_bf[g, x][:])
            nc.sync.dma_start(word_rows[:, g0:g1, x * HALF:(x + 1) * HALF], y_w[:].bitcast(I32))

        def store_scales(x):
            for r in range(4):
                nc.sync.dma_start(out_2[:, r:16:4, x * HALF:(x + 1) * HALF].rearrange("g q c -> q g c").bitcast(I32),
                                  y_s[x][r:P:32].bitcast(I32))

        nc.vector.tensor_copy(v_gs[:], tab_s[:].indirect(offs_t[:]))
        for q in QUADS:
            nc.sync.dma_start(v_s[32 * q:32 * q + 4].rearrange("p a c -> p (a c)").bitcast(I32),
                              v_gs[8 * q:8 * q + 8, :].bitcast(I32))
        wg1_raw = [placed("wg1_raw0", [P, PACK, WG1_CUTS[1]], F32, AT_TAB1 - 16 * WG1_CUTS[1]), None, None]
        load_wg(wg1_raw[0], 1, 0, WG1_CUTS[1])
        tab_w[1] = placed("tab_w1", [P, T], U32, AT_TAB1)
        load_words(tab_w[1], tab_words[1])
        nc.scalar.copy(wp_w[:].bitcast(U16).rearrange("p a (t m) -> p a t m", t=PACK),
                              wp_raw[:].bitcast(U16).rearrange("p a (m t) -> p a t m", t=PACK))
        wp_s = held("wp_s", [P, PASSES, H], U8)
        nc.vector.tensor_copy(wp_s[:].rearrange("p a (t m) -> p a t m", t=PACK),
                              wp_raw_s[:].rearrange("p a (m t) -> p a t m", t=PACK))
        wg1_raw[1] = held("wg1_raw1", [P, PACK, WG1_CUTS[2] - WG1_CUTS[1]], F32, "wp_raw")
        wg1_raw[2] = placed("wg1_raw2", [P, PACK, WG1_CUTS[3] - WG1_CUTS[2]], F32, 1024)
        for piece in (1, 2):
            load_wg(wg1_raw[piece], 1, WG1_CUTS[piece], WG1_CUTS[piece + 1])
        gather_v(0, 0, 2 * TILES)
        tab2_w = held("tab2_w", [P, T2], U32, "tab_w0")
        load_words(tab2_w, tab2_words[0])
        v2_gs01 = gather_v2_scales(held("v2_gs01", [P, 2 * KP], U8), 0, 2)

        a_banks = [new_bank(u) for u in range(TILES)]
        p_banks = [new_bank(TILES + u) for u in range(TILES)]
        for u in range(TILES):
            p_pass(p_banks[u], 0, 0, u)
        nc.scalar.copy(*wg_views(0, wg0_raw, 0))
        quantize_wg(0)
        strength_t = held("strength_t", [P, GROUPS, PACK], F32, "wg0_raw")
        nc.sync.dma_start(strength_t[:], strength.rearrange("(g p t) -> p g t", p=P, t=PACK))
        for u in range(TILES):
            a_pass(a_banks[u], 0, 0, u)
        gather_v(1, 0, TILES)
        gather_v(1, TILES, 2 * TILES)
        p_pass(p_banks[0], 1, 0, 0)
        nc.scalar.copy(*wg_views(1, wg1_raw[0], 0))
        nc.scalar.copy(*wg_views(1, wg1_raw[1], WG1_CUTS[1] // PACK))
        dst, src = wg_views(1, wg1_raw[2], WG1_CUTS[2] // PACK)
        for u in range(2):
            nc.scalar.copy(dst[:, u], src[:, u])
            cols = slice(u * H // 2, (u + 1) * H // 2)
            nc.vector.quantize_mx(out=wg_w[1][:, cols].bitcast(FP8X4), scales=wg_s[1][:, cols],
                                  in_=wg_bf[1][:, u * 2 * H:(u + 1) * 2 * H])
        deal_v2_scales(v2_s01, placed("v2_ds01", [P, 2 * KP], U8, 4096), v2_gs01)
        v2_gs2 = gather_v2_scales(placed("v2_gs2", [P, KP], U8, 4096 + 2 * KP), 2, 3)

        def gate_on_gpsimd(p_sb, a_bank, x, u):
            sig = woven(held("sig%d%d" % (x, u), [P, JT * PACK], F32), a_bank, ACT.Sigmoid)
            nc.gpsimd.tensor_tensor(h_bf[x][:, u * JT * PACK:(u + 1) * JT * PACK], p_sb[:], sig[:], MULT)

        def both_passes(one_pass, bank, u):
            for a in range(PASSES):
                one_pass(bank, a, 1, u)
            return bank

        def late_tile_on_gpsimd(u, banks):
            late_a = both_passes(a_pass, new_bank(banks[0]), u)
            late_p = both_passes(p_pass, new_bank(banks[1]), u)
            sig = woven(held("sig1%d" % u, [P, JT * PACK], F32), late_a, ACT.Sigmoid)
            p_sb = woven(held("p_sb1%d" % u, [P, JT * PACK], F32), late_p, ACT.Copy)
            nc.gpsimd.tensor_tensor(h_bf[1][:, u * JT * PACK:(u + 1) * JT * PACK], p_sb[:], sig[:], MULT)

        p_sb = woven(placed("p_sb00", [P, JT * PACK], F32, 0), p_banks[0], ACT.Copy)
        for u in range(TILES):
            a_pass(a_banks[u], 1, 0, u)
            if u == 0:
                gate_on_gpsimd(p_sb, a_banks[u], 0, u)
            else:
                p_pass(p_banks[u], 1, 0, u)
                gate(p_banks[u], a_banks[u], 0, u)
        deal_v2_scales(v2_s2, placed("v2_ds2", [P, KP], U8, AT_SIG3 + 512), v2_gs2)
        quantize_h(0)
        h_bf[1] = held("h_bf1", [P, HALF * PACK], BF16, "h_bf0")
        late_a = both_passes(a_pass, new_bank(4), 0)
        gate(both_passes(p_pass, new_bank(0), 0), late_a, 1, 0)
        gather_v2_words(0, 1, AT_SIG3 - 1536)
        gather_v2_words(1, 3, AT_SIG3 + 1024)
        late_tile_on_gpsimd(1, (1, 2))
        late_tile_on_gpsimd(2, (5, 3))
        late_tile_on_gpsimd(3, (6, 7))

        banks = [(4, 0, 1, 2), (5, 3, 6, 7)] * GROUPS

        def quantize_behind(n):
            g, x = units[n - 2]
            quantize_y(x, g, g + 1, "sq_hold%d%d2" % units[n])

        def round_rest(n):
            share = Y_ON_GPSIMD[n]
            round_on_scalar(*units[n], share, HALF, y[units[n]][:, :, share:])

        for n, (g, x) in enumerate(units[:-1]):
            if n:
                cube(g, x, banks[n], 2)
            else:
                first_cube(banks[n])
            if n == 1:
                quantize_h(1, "sq_hold%d%d2" % units[n])
            if n >= 2:
                quantize_behind(n)
            if n == 4:
                store_scales(0)
            share = Y_ON_GPSIMD[n]
            round_on_gpsimd(g, x, 0, share, y_bf[g, x][:, :share * PACK])
            if n >= 1:
                round_rest(n - 1)
        g, x = units[-1]
        squares = [square(g, x, t, banks[-1][t]) for t in range(PACK)]
        round_rest(len(units) - 2)
        for c0 in (0, HALF // 2):
            c1 = c0 + HALF // 2
            part = held("y_part%d" % c0, [P, PACK, HALF // 2], F32)
            for t, (m, sq) in enumerate(squares):
                product(part[:, t, :], g, t, m[:, c0:c1], sq[:, c0:c1])
            nc.sync.dma_start(y_rows[g, :, :, x * HALF + c0:x * HALF + c1], part[:])
            round_on_scalar(g, x, c0, c1, part[:])
        quantize_y(x, 0, g, "sq_hold%d%d2" % units[-1])
        quantize_y(x, g, GROUPS)
        store_scales(x)
